import numpy as np
import ml_dtypes


def mxq(x, axis, fmt="e4m3"):
    dtype, down = {"e4m3": (ml_dtypes.float8_e4m3fn, 7), "e5m2": (ml_dtypes.float8_e5m2, 14)}[fmt]
    v = np.moveaxis(np.asarray(x, np.float32).astype(ml_dtypes.bfloat16).astype(np.float64), axis, -1)
    blocks = v.reshape(v.shape[:-1] + (-1, 32))
    amax = np.abs(blocks).max(-1, keepdims=True)
    byte = np.maximum(np.where(amax > 0, np.frexp(amax)[1] - 1 + 127, 0) - down, 1)
    scale = np.exp2(byte - 127.0)
    codes = (blocks / scale).astype(np.float32).astype(dtype).astype(np.float64)
    return np.moveaxis((codes * scale).reshape(v.shape), -1, axis)


WIDE = False


def mx_kscale(k):
    if not WIDE:
        return np.ones(k)
    levels = np.array([10, -10, 5, -5, 0])
    if k % 512:
        return np.exp2(np.random.permutation(np.resize(levels, k // 32))).repeat(32)
    a = np.empty((k // 512, 16))
    for p in range(k // 512):
        a[p, :8] = np.random.permutation(np.resize(levels, 8))
        for g in range(8):
            far = levels[np.abs(levels - a[p, g]) >= 10]
            a[p, g + 8] = far[np.random.randint(len(far))]
    return np.exp2(a.ravel()).repeat(32)


def f64(x):
    return np.asarray(x).astype(np.float64)


def striped(idx):
    return np.tile(idx.reshape(-1, 16).T, (8, 1)).astype(np.uint16)


def unstriped(offs):
    return offs[:16].T.reshape(-1).astype(np.int64)


E2M1 = np.array([0.0, 0.5, 1.0, 1.5, 2.0, 3.0, 4.0, 6.0, -0.0, -0.5, -1.0, -1.5, -2.0, -3.0, -4.0, -6.0])


def pack_weight(w, fmt):
    k, n = w.shape
    w = f64(np.asarray(w, np.float32).astype(ml_dtypes.bfloat16)).reshape(k // 32, 32, n)
    amax = np.abs(w).max(1)
    if fmt == "e4m3":
        byte = np.frexp(amax)[1] - 1 + 127 - 7
    else:
        mant, ex = np.frexp(amax / 6.0)
        byte = np.where(mant > 0.5, ex, ex - 1) + 127
    byte = np.clip(np.where(amax > 0, byte, 1), 1, 254)
    scaled = (w * np.exp2(127.0 - byte)[:, None, :]).reshape(k, n).astype(np.float32)
    by_word = np.ascontiguousarray(scaled.reshape(k // 512, 128, 4, n).transpose(0, 1, 3, 2))
    if fmt == "e4m3":
        words = by_word.astype(ml_dtypes.float8_e4m3fn).view(np.uint8)
    else:
        c = by_word.astype(ml_dtypes.float4_e2m1fn).view(np.uint8) & 0xF
        words = (c[..., 0::2] | (c[..., 1::2] << 4)).reshape(k // 512, 128, 2 * n)
    return np.ascontiguousarray(words), np.ascontiguousarray(byte.astype(np.uint8).reshape(k // 512, 16, n))


def unpack_weight(words, scales, fmt):
    g, _, n = scales.shape
    words = np.ascontiguousarray(words).reshape(g, 128, n, -1)
    if fmt == "e4m3":
        vals = words.view(ml_dtypes.float8_e4m3fn).astype(np.float64)
    else:
        nib = np.empty((g, 128, n, 4), np.uint8)
        nib[..., 0::2] = words & 0xF
        nib[..., 1::2] = words >> 4
        vals = E2M1[nib]
    vals = vals * np.repeat(np.exp2(scales.astype(np.float64) - 127.0), 8, axis=1)[..., None]
    return vals.transpose(0, 1, 3, 2).reshape(g * 512, n)


def gelu(v):
    return 0.5 * v * (1.0 + np.tanh(np.sqrt(2.0 / np.pi) * (v + 0.044715 * v**3)))


K, T, T2, S, H, N = 1024, 2048, 1024, 512, 1024, 384

def setup_inputs():
    n = np.random.standard_normal
    s = mx_kscale(K)[:, None]
    u = mx_kscale(H)[:, None]
    tab_words, tab_scales = pack_weight(n((K, T)) * s, "e4m3")
    w2_words, w2_scales = pack_weight(n((K, H)) * u.T / (s * np.sqrt(K)), "e2m1")
    w3_words, w3_scales = pack_weight(n((H, N)) / (u * np.sqrt(H)), "e4m3")
    return {
        "tab_words": tab_words, "tab_scales": tab_scales,
        "offs": striped(np.random.permutation(T)[:S]),
        "xT": (np.round(16 * n((K, T2))) / 16 * s).astype(np.float32),
        "offs2": striped(np.random.permutation(T2)[:S]),
        "offs3": striped(np.random.permutation(T2)[:S]),
        "w1": (0.7 * n((K, H)) / (s * np.sqrt(K))).astype(np.float32),
        "w2_words": w2_words, "w2_scales": w2_scales,
        "c1": (n(H) * u[:, 0]).astype(np.float32),
        "c2": (0.5 * n(H) * u[:, 0]).astype(np.float32),
        "w3_words": w3_words, "w3_scales": w3_scales,
        "b": (0.5 * n(N)).astype(np.float32),
    }

def reference(tab_words, tab_scales, offs, xT, offs2, offs3, w1, w2_words, w2_scales, c1, c2, w3_words, w3_scales, b):
    v = unpack_weight(tab_words, tab_scales, "e4m3")[:, unstriped(offs)]
    x = f64(xT)[:, unstriped(offs2)] - f64(xT)[:, unstriped(offs3)]
    d = mxq(f64(w1), 0, "e4m3").T @ mxq(x, 0, "e4m3")
    m = unpack_weight(w2_words, w2_scales, "e2m1").T @ v
    h = (f64(c2)[:, None] * d + f64(c1)[:, None]) * d + m
    y = unpack_weight(w3_words, w3_scales, "e4m3").T @ mxq(h, 0, "e4m3")
    return y + f64(b)[:, None]

@@ -1,0 +1,252 @@
+from contextlib import ExitStack
+
+import concourse.mybir as mybir
+from concourse.masks import make_identity
+
+K, T, T2, S, H, N = 1024, 2048, 1024, 512, 1024, 384
+FLOPS = 2 * S * (K * H + K * H + H * N)
+
+F32 = mybir.dt.float32
+BF16 = mybir.dt.bfloat16
+I32 = mybir.dt.int32
+U32 = mybir.dt.uint32
+U16 = mybir.dt.uint16
+U8 = mybir.dt.uint8
+FP8X4 = mybir.dt.float8_e4m3fn_x4
+FP4X4 = mybir.dt.float4_e2m1fn_x4
+ALU = mybir.AluOpType
+ACT = mybir.ActivationFunctionType
+
+P = 128
+PACK = 4
+KP = P * PACK
+HALF = S // 2
+QUARTER = S // 4
+N_TILES = N // P
+
+
+def tile_list_frost_risk_map_kernel(
+    tc, tab_words, tab_scales, offs, xT, offs2, offs3, w1, w2_words, w2_scales, c1, c2, w3_words, w3_scales, b, out
+):
+    nc = tc.nc
+    with ExitStack() as ctx:
+        lists = ctx.enter_context(tc.tile_pool(name="lists", bufs=1))
+        keep = ctx.enter_context(tc.tile_pool(name="keep", bufs=1))
+        ring = ctx.enter_context(tc.tile_pool(name="ring", bufs=2))
+        psum = ctx.enter_context(tc.psum_pool(name="psum", bufs=1))
+
+        idx = lists.tile([P, S // 16], U16, name="idx")
+        idx2 = lists.tile([P, S // 16], U16, name="idx2")
+        idx3 = lists.tile([P, S // 16], U16, name="idx3")
+
+        planes = [keep.tile([P, T2], F32, name=f"plane{i}") for i in range(2 * PACK)]
+        tab_w = [keep.tile([P, T], I32, name=f"tab_w{a}") for a in range(2)]
+        tab_s = keep.tile([P, T], U8, name="tab_s")
+        v_w = [keep.tile([P, S], U32, name=f"v_w{a}", align_bytes=64) for a in range(2)]
+        v_s = [keep.tile([P, S], U8, name=f"v_s{a}", align_bytes=64) for a in range(2)]
+        w2_w = keep.tile([P, 2, 2 * H], U8, name="w2_w", align_bytes=64)
+        w2_s = keep.tile([P, 2, H], U8, name="w2_s", align_bytes=64)
+        w3_w = keep.tile([P, 2, N], I32, name="w3_w", align_bytes=64)
+        w3_s = keep.tile([P, 2, N], U8, name="w3_s", align_bytes=64)
+        c1_sb = keep.tile([P, 2, PACK], F32, name="c1_sb")
+        c2_sb = keep.tile([P, 2, PACK], F32, name="c2_sb")
+        b_sb = keep.tile([P, N_TILES], F32, name="b_sb")
+        ident = keep.tile([P, P], F32, name="ident")
+        w1_raw = {(a, g): keep.tile([P, PACK, KP], F32, name=f"w1_raw{a}{g}") for a in range(2) for g in range(2)}
+        w1_w = {(a, g): keep.tile([P, KP], U32, name=f"w1_w{a}{g}", align_bytes=64) for a in range(2) for g in range(2)}
+        w1_s = {(a, g): keep.tile([P, KP], U8, name=f"w1_s{a}{g}", align_bytes=64) for a in range(2) for g in range(2)}
+
+        for plane in (tab_s, w2_s, v_s[1], w3_s):
+            nc.vector.memset(plane[:].bitcast(I32), 0)
+        make_identity(nc, ident[:])
+
+        def load_plane(i):
+            a, slot = divmod(i, PACK)
+            rows = xT[a * KP : (a + 1) * KP, :].rearrange("(p i) t -> p i t", i=PACK)
+            nc.sync.dma_start(out=planes[i][:], in_=rows[:, slot, :])
+
+        def load_table(a):
+            nc.sync.dma_start(out=tab_w[a][:], in_=tab_words[a].rearrange("p t i -> p (t i)").bitcast(I32))
+
+        def load_w1(a, g):
+            rows = w1[a * KP : (a + 1) * KP, g * KP : (g + 1) * KP].rearrange("(p j) c -> p j c", j=PACK)
+            nc.sync.dma_start(out=w1_raw[a, g][:], in_=rows)
+
+        def load_scales(plane, scales):
+            for q in range(4):
+                rows = scales[:, 4 * q : 4 * q + 4, :].rearrange("a r c -> r a c")
+                nc.sync.dma_start(out=plane[32 * q : 32 * q + 4, :, :].bitcast(I32), in_=rows.bitcast(I32))
+
+        load_plane(0)
+        nc.sync.dma_start(idx3[:], offs3)
+        nc.sync.dma_start(idx2[:], offs2)
+        load_plane(1)
+        nc.sync.dma_start(idx[:], offs)
+        for q in range(4):
+            nc.sync.dma_start(
+                out=tab_s[32 * q : 32 * q + 8, :].bitcast(I32), in_=tab_scales[:, 4 * q : 4 * q + 4, :].bitcast(I32)
+            )
+        load_plane(2)
+        load_w1(0, 0)
+        load_w1(1, 0)
+        load_plane(3)
+        load_plane(4)
+        load_w1(0, 1)
+        load_plane(5)
+        nc.sync.dma_start(out=c1_sb[:], in_=c1.rearrange("(g p t) -> p g t", g=2, t=PACK))
+        nc.sync.dma_start(out=c2_sb[:], in_=c2.rearrange("(g p t) -> p g t", g=2, t=PACK))
+        load_plane(6)
+        nc.sync.dma_start(out=w2_w[:].bitcast(I32), in_=w2_words.rearrange("a p c -> p a c").bitcast(I32))
+        load_scales(w2_s, w2_scales)
+        load_w1(1, 1)
+        load_plane(7)
+        load_table(0)
+        load_table(1)
+        nc.sync.dma_start(out=w3_w[:], in_=w3_words.rearrange("a p c i -> p a (c i)").bitcast(I32))
+        load_scales(w3_s, w3_scales)
+        with nc.allow_non_contiguous_dma(reason="one bias value to a partition"):
+            nc.sync.dma_start(out=b_sb[:], in_=b.rearrange("(n p) -> p n", p=P))
+
+        picked = [keep.tile([P, HALF], F32, name=f"picked{h}") for h in range(2)]
+        x_f32 = [[keep.tile([P, PACK, HALF], F32, name=f"x_f32_{a}{h}") for h in range(2)] for a in range(2)]
+        x_bf = [keep.tile([P, PACK * S], BF16, name=f"x_bf{a}", align_bytes=64) for a in range(2)]
+        x_w = [keep.tile([P, S], U32, name=f"x_w{a}", align_bytes=64) for a in range(2)]
+        x_s = [keep.tile([P, S], U8, name=f"x_s{a}", align_bytes=64) for a in range(2)]
+
+        def differences(i):
+            a, slot = divmod(i, PACK)
+            cols = [slice(h * HALF // 16, (h + 1) * HALF // 16) for h in range(2)]
+            for h in range(2):
+                nc.vector.tensor_copy(out=picked[h][:], in_=planes[i][:].indirect(idx3[:, cols[h]]))
+            for h in range(2):
+                nc.vector.tensor_tensor(
+                    out=x_f32[a][h][:, slot, :],
+                    in0=planes[i][:].indirect(idx2[:, cols[h]]),
+                    in1=picked[h][:],
+                    op=ALU.subtract,
+                )
+
+        def round_x(a):
+            for h in range(2):
+                nc.scalar.activation(
+                    out=x_bf[a][:, h * PACK * HALF : (h + 1) * PACK * HALF].rearrange("p (c i t) -> p c t i", i=4, t=PACK),
+                    in_=x_f32[a][h][:].rearrange("p t (c i) -> p c t i", i=4),
+                    func=ACT.Copy,
+                )
+
+        def quantise_x(a):
+            nc.vector.quantize_mx(out=x_w[a][:].bitcast(FP8X4), scales=x_s[a][:], in_=x_bf[a][:])
+
+        def quantise_w1(a, g):
+            w1_bf = keep.tile([P, PACK * KP], BF16, name=f"w1_bf{a}{g}", align_bytes=64)
+            nc.scalar.activation(
+                out=w1_bf[:].rearrange("p (t m j) -> p m j t", t=PACK, j=PACK),
+                in_=w1_raw[a, g][:].rearrange("p j (m t) -> p m j t", t=PACK),
+                func=ACT.Copy,
+            )
+            nc.vector.quantize_mx(out=w1_w[a, g][:].bitcast(FP8X4), scales=w1_s[a, g][:], in_=w1_bf[:])
+
+        def gather_table(a):
+            nc.vector.tensor_copy(out=v_w[a][:], in_=tab_w[a][:].bitcast(U32).indirect(idx[:]))
+
+        differences(0)
+        differences(1)
+        nc.vector.tensor_copy(out=v_s[0][:], in_=tab_s[:].indirect(idx[:]))
+        nc.gpsimd.dma_start(out=v_s[1][0:112, :].bitcast(I32), in_=v_s[0][4:116, :].bitcast(I32))
+        differences(2)
+        quantise_w1(0, 0)
+        differences(3)
+        differences(4)
+        quantise_w1(1, 0)
+        round_x(0)
+        quantise_x(0)
+        differences(5)
+        quantise_w1(0, 1)
+        differences(6)
+        quantise_w1(1, 1)
+        differences(7)
+        round_x(1)
+        gather_table(0)
+        quantise_x(1)
+        gather_table(1)
+
+        u = [keep.tile([P, PACK, S], F32, name=f"u{g}") for g in range(2)]
+        for g in range(2):
+            for t in range(PACK):
+                d = psum.tile([P, S], F32, name="d", bufs=4)
+                inner = ring.tile([P, S], F32, name="inner", bufs=3)
+                for a in range(2):
+                    nc.tensor.matmul_mx(
+                        out=d[:],
+                        lhsT=w1_w[a, g][:, t * P : (t + 1) * P].bitcast(FP8X4),
+                        lhsT_scale=w1_s[a, g][:, t * P : (t + 1) * P],
+                        rhs=x_w[a][:].bitcast(FP8X4),
+                        rhs_scale=x_s[a][:],
+                        start=(a == 0),
+                        stop=(a == 1),
+                    )
+                nc.scalar.activation(
+                    out=inner[:], in_=d[:], func=ACT.Identity, scale=c2_sb[:, g, t : t + 1], bias=c1_sb[:, g, t : t + 1]
+                )
+                nc.vector.tensor_tensor(out=u[g][:, t, :], in0=d[:], in1=inner[:], op=ALU.mult)
+
+        m_t = [keep.tile([P, 2, PACK, P], F32, name=f"m_t{q}") for q in range(4)]
+        for q in range(4):
+            for g in range(2):
+                bank = psum.tile([P, KP], F32, name="side", bufs=2)
+                for a in range(2):
+                    nc.tensor.matmul_mx(
+                        out=bank[:],
+                        lhsT=v_w[a][:, q * P : (q + 1) * P].bitcast(FP8X4),
+                        lhsT_scale=v_s[a][:, q * P : (q + 1) * P],
+                        rhs=w2_w[:, a, 2 * g * KP : 2 * (g + 1) * KP].bitcast(FP4X4),
+                        rhs_scale=w2_s[:, a, g * KP : (g + 1) * KP],
+                        start=(a == 0),
+                        stop=(a == 1),
+                    )
+                nc.scalar.activation(
+                    out=m_t[q][:, g, :, :], in_=bank[:].rearrange("p (m t) -> p t m", t=PACK), func=ACT.Copy
+                )
+
+        h_bf = [keep.tile([P, 2, KP], BF16, name=f"h_bf{q}", align_bytes=64) for q in range(4)]
+
+        def add_constant_term(q, g):
+            m = psum.tile([P, PACK, P], F32, name="m", bufs=2)
+            for t in range(PACK):
+                nc.tensor.transpose(m[:, t, :], m_t[q][:, g, t, :], ident[:])
+            nc.vector.tensor_tensor(
+                out=h_bf[q][:, g, :].rearrange("p (c i t) -> p c t i", i=4, t=PACK),
+                in0=m[:].rearrange("p t (c i) -> p c t i", i=4),
+                in1=u[g][:, :, q * P : (q + 1) * P].rearrange("p t (c i) -> p c t i", i=4),
+                op=ALU.add,
+            )
+
+        def damage_indices(q):
+            h_w = ring.tile([P, 2 * P], U32, name="h_w", align_bytes=64)
+            h_s = ring.tile([P, 2 * P], U8, name="h_s", align_bytes=64)
+            nc.vector.quantize_mx(
+                out=h_w[:].bitcast(FP8X4), scales=h_s[:], in_=h_bf[q][:].rearrange("p g c -> p (g c)")
+            )
+            y = psum.tile([P, N_TILES, P], F32, name="d", bufs=4)
+            y_sb = ring.tile([P, N_TILES, P], F32, name="y_sb", bufs=4)
+            for n in range(N_TILES):
+                for g in range(2):
+                    nc.tensor.matmul_mx(
+                        out=y[:, n, :],
+                        lhsT=w3_w[:, g, n * P : (n + 1) * P].bitcast(FP8X4),
+                        lhsT_scale=w3_s[:, g, n * P : (n + 1) * P],
+                        rhs=h_w[:, g * P : (g + 1) * P].bitcast(FP8X4),
+                        rhs_scale=h_s[:, g * P : (g + 1) * P],
+                        start=(g == 0),
+                        stop=(g == 1),
+                    )
+            for n in range(N_TILES):
+                nc.scalar.activation(out=y_sb[:, n, :], in_=y[:, n, :], func=ACT.Identity, bias=b_sb[:, n : n + 1])
+            nc.sync.dma_start(out=out[:, q * P : (q + 1) * P].rearrange("(n p) j -> p n j", p=P), in_=y_sb[:])
+
+        for q in range(4):
+            add_constant_term(q, 0)
+            if q > 0:
+                damage_indices(q - 1)
+            add_constant_term(q, 1)
+        damage_indices(3)

@@ -1,7 +1,6 @@
 from contextlib import ExitStack
 
 import concourse.mybir as mybir
-from concourse.masks import make_identity
 
 K, T, T2, S, H, N = 1024, 2048, 1024, 512, 1024, 384
 FLOPS = 2 * S * (K * H + K * H + H * N)
@@ -44,21 +43,21 @@ def tile_list_frost_risk_map_kernel(
         tab_s = keep.tile([P, T], U8, name="tab_s")
         v_w = [keep.tile([P, S], U32, name=f"v_w{a}", align_bytes=64) for a in range(2)]
         v_s = [keep.tile([P, S], U8, name=f"v_s{a}", align_bytes=64) for a in range(2)]
+        w2_raw = keep.tile([P, 2, 2 * H], U8, name="w2_raw")
         w2_w = keep.tile([P, 2, 2 * H], U8, name="w2_w", align_bytes=64)
-        w2_s = keep.tile([P, 2, H], U8, name="w2_s", align_bytes=64)
+        w2_raw_s = keep.tile([P, H], U8, name="w2_raw_s")
+        w2_s = [keep.tile([P, H], U8, name=f"w2_s{a}", align_bytes=64) for a in range(2)]
         w3_w = keep.tile([P, 2, N], I32, name="w3_w", align_bytes=64)
         w3_s = keep.tile([P, 2, N], U8, name="w3_s", align_bytes=64)
         c1_sb = keep.tile([P, 2, PACK], F32, name="c1_sb")
         c2_sb = keep.tile([P, 2, PACK], F32, name="c2_sb")
         b_sb = keep.tile([P, N_TILES], F32, name="b_sb")
-        ident = keep.tile([P, P], F32, name="ident")
         w1_raw = {(a, g): keep.tile([P, PACK, KP], F32, name=f"w1_raw{a}{g}") for a in range(2) for g in range(2)}
         w1_w = {(a, g): keep.tile([P, KP], U32, name=f"w1_w{a}{g}", align_bytes=64) for a in range(2) for g in range(2)}
         w1_s = {(a, g): keep.tile([P, KP], U8, name=f"w1_s{a}{g}", align_bytes=64) for a in range(2) for g in range(2)}
 
-        for plane in (tab_s, w2_s, v_s[1], w3_s):
+        for plane in (tab_s, w2_raw_s, v_s[1], w2_s[1], w3_s):
             nc.vector.memset(plane[:].bitcast(I32), 0)
-        make_identity(nc, ident[:])
 
         def load_plane(i):
             a, slot = divmod(i, PACK)
@@ -72,6 +71,12 @@ def tile_list_frost_risk_map_kernel(
             rows = w1[a * KP : (a + 1) * KP, g * KP : (g + 1) * KP].rearrange("(p j) c -> p j c", j=PACK)
             nc.sync.dma_start(out=w1_raw[a, g][:], in_=rows)
 
+        def load_packed_scales(plane, scales):
+            for q in range(4):
+                nc.sync.dma_start(
+                    out=plane[32 * q : 32 * q + 8, :].bitcast(I32), in_=scales[:, 4 * q : 4 * q + 4, :].bitcast(I32)
+                )
+
         def load_scales(plane, scales):
             for q in range(4):
                 rows = scales[:, 4 * q : 4 * q + 4, :].rearrange("a r c -> r a c")
@@ -82,10 +87,8 @@ def tile_list_frost_risk_map_kernel(
         nc.sync.dma_start(idx2[:], offs2)
         load_plane(1)
         nc.sync.dma_start(idx[:], offs)
-        for q in range(4):
-            nc.sync.dma_start(
-                out=tab_s[32 * q : 32 * q + 8, :].bitcast(I32), in_=tab_scales[:, 4 * q : 4 * q + 4, :].bitcast(I32)
-            )
+        load_packed_scales(tab_s, tab_scales)
+        load_packed_scales(w2_raw_s, w2_scales)
         load_plane(2)
         load_w1(0, 0)
         load_w1(1, 0)
@@ -95,17 +98,6 @@ def tile_list_frost_risk_map_kernel(
         load_plane(5)
         nc.sync.dma_start(out=c1_sb[:], in_=c1.rearrange("(g p t) -> p g t", g=2, t=PACK))
         nc.sync.dma_start(out=c2_sb[:], in_=c2.rearrange("(g p t) -> p g t", g=2, t=PACK))
-        load_plane(6)
-        nc.sync.dma_start(out=w2_w[:].bitcast(I32), in_=w2_words.rearrange("a p c -> p a c").bitcast(I32))
-        load_scales(w2_s, w2_scales)
-        load_w1(1, 1)
-        load_plane(7)
-        load_table(0)
-        load_table(1)
-        nc.sync.dma_start(out=w3_w[:], in_=w3_words.rearrange("a p c i -> p a (c i)").bitcast(I32))
-        load_scales(w3_s, w3_scales)
-        with nc.allow_non_contiguous_dma(reason="one bias value to a partition"):
-            nc.sync.dma_start(out=b_sb[:], in_=b.rearrange("(n p) -> p n", p=P))
 
         picked = [keep.tile([P, HALF], F32, name=f"picked{h}") for h in range(2)]
         x_f32 = [[keep.tile([P, PACK, HALF], F32, name=f"x_f32_{a}{h}") for h in range(2)] for a in range(2)]
@@ -152,7 +144,23 @@ def tile_list_frost_risk_map_kernel(
         differences(0)
         differences(1)
         nc.vector.tensor_copy(out=v_s[0][:], in_=tab_s[:].indirect(idx[:]))
-        nc.gpsimd.dma_start(out=v_s[1][0:112, :].bitcast(I32), in_=v_s[0][4:116, :].bitcast(I32))
+        nc.vector.tensor_copy(
+            out=w2_s[0][:].rearrange("p (g t m) -> p g t m", g=2, t=PACK),
+            in_=w2_raw_s[:].rearrange("p (g m t) -> p g t m", g=2, t=PACK),
+        )
+        load_plane(6)
+        nc.sync.dma_start(out=w2_raw[:].bitcast(I32), in_=w2_words.rearrange("a p c -> p a c").bitcast(I32))
+        load_w1(1, 1)
+        nc.sync.dma_start(out=v_s[1][0:112, :].bitcast(I32), in_=v_s[0][4:116, :].bitcast(I32))
+        nc.sync.dma_start(out=w2_s[1][0:112, :].bitcast(I32), in_=w2_s[0][4:116, :].bitcast(I32))
+        load_plane(7)
+        load_table(0)
+        load_table(1)
+        nc.sync.dma_start(out=w3_w[:], in_=w3_words.rearrange("a p c i -> p a (c i)").bitcast(I32))
+        load_scales(w3_s, w3_scales)
+        with nc.allow_non_contiguous_dma(reason="one bias value to a partition"):
+            nc.sync.dma_start(out=b_sb[:], in_=b.rearrange("(n p) -> p n", p=P))
+
         differences(2)
         quantise_w1(0, 0)
         differences(3)
@@ -163,6 +171,10 @@ def tile_list_frost_risk_map_kernel(
         differences(5)
         quantise_w1(0, 1)
         differences(6)
+        nc.vector.tensor_copy(
+            out=w2_w[:].rearrange("p a c -> p (a c)").bitcast(U16).rearrange("p (g t m) -> p g t m", t=PACK, m=P),
+            in_=w2_raw[:].rearrange("p a c -> p (a c)").bitcast(U16).rearrange("p (g m t) -> p g t m", t=PACK, m=P),
+        )
         quantise_w1(1, 1)
         differences(7)
         round_x(1)
@@ -173,7 +185,7 @@ def tile_list_frost_risk_map_kernel(
         u = [keep.tile([P, PACK, S], F32, name=f"u{g}") for g in range(2)]
         for g in range(2):
             for t in range(PACK):
-                d = psum.tile([P, S], F32, name="d", bufs=4)
+                d = psum.tile([P, S], F32, name="bank", bufs=8)
                 inner = ring.tile([P, S], F32, name="inner", bufs=3)
                 for a in range(2):
                     nc.tensor.matmul_mx(
@@ -190,30 +202,22 @@ def tile_list_frost_risk_map_kernel(
                 )
                 nc.vector.tensor_tensor(out=u[g][:, t, :], in0=d[:], in1=inner[:], op=ALU.mult)
 
-        m_t = [keep.tile([P, 2, PACK, P], F32, name=f"m_t{q}") for q in range(4)]
-        for q in range(4):
-            for g in range(2):
-                bank = psum.tile([P, KP], F32, name="side", bufs=2)
-                for a in range(2):
-                    nc.tensor.matmul_mx(
-                        out=bank[:],
-                        lhsT=v_w[a][:, q * P : (q + 1) * P].bitcast(FP8X4),
-                        lhsT_scale=v_s[a][:, q * P : (q + 1) * P],
-                        rhs=w2_w[:, a, 2 * g * KP : 2 * (g + 1) * KP].bitcast(FP4X4),
-                        rhs_scale=w2_s[:, a, g * KP : (g + 1) * KP],
-                        start=(a == 0),
-                        stop=(a == 1),
-                    )
-                nc.scalar.activation(
-                    out=m_t[q][:, g, :, :], in_=bank[:].rearrange("p (m t) -> p t m", t=PACK), func=ACT.Copy
-                )
-
         h_bf = [keep.tile([P, 2, KP], BF16, name=f"h_bf{q}", align_bytes=64) for q in range(4)]
 
         def add_constant_term(q, g):
-            m = psum.tile([P, PACK, P], F32, name="m", bufs=2)
+            m = psum.tile([P, PACK, P], F32, name="bank", bufs=8)
             for t in range(PACK):
-                nc.tensor.transpose(m[:, t, :], m_t[q][:, g, t, :], ident[:])
+                c0 = g * KP + t * P
+                for a in range(2):
+                    nc.tensor.matmul_mx(
+                        out=m[:, t, :],
+                        lhsT=w2_w[:, a, 2 * c0 : 2 * (c0 + P)].bitcast(FP4X4),
+                        lhsT_scale=w2_s[a][:, c0 : c0 + P],
+                        rhs=v_w[a][:, q * P : (q + 1) * P].bitcast(FP8X4),
+                        rhs_scale=v_s[a][:, q * P : (q + 1) * P],
+                        start=(a == 0),
+                        stop=(a == 1),
+                    )
             nc.vector.tensor_tensor(
                 out=h_bf[q][:, g, :].rearrange("p (c i t) -> p c t i", i=4, t=PACK),
                 in0=m[:].rearrange("p t (c i) -> p c t i", i=4),
@@ -227,7 +231,7 @@ def tile_list_frost_risk_map_kernel(
             nc.vector.quantize_mx(
                 out=h_w[:].bitcast(FP8X4), scales=h_s[:], in_=h_bf[q][:].rearrange("p g c -> p (g c)")
             )
-            y = psum.tile([P, N_TILES, P], F32, name="d", bufs=4)
+            y = psum.tile([P, N_TILES, P], F32, name="bank", bufs=8)
             y_sb = ring.tile([P, N_TILES, P], F32, name="y_sb", bufs=4)
             for n in range(N_TILES):
                 for g in range(2):

@@ -1,6 +1,7 @@
 from contextlib import ExitStack
 
 import concourse.mybir as mybir
+from concourse.masks import make_identity
 
 K, T, T2, S, H, N = 1024, 2048, 1024, 512, 1024, 384
 FLOPS = 2 * S * (K * H + K * H + H * N)
@@ -43,21 +44,27 @@ def tile_list_frost_risk_map_kernel(
         tab_s = keep.tile([P, T], U8, name="tab_s")
         v_w = [keep.tile([P, S], U32, name=f"v_w{a}", align_bytes=64) for a in range(2)]
         v_s = [keep.tile([P, S], U8, name=f"v_s{a}", align_bytes=64) for a in range(2)]
-        w2_raw = keep.tile([P, 2, 2 * H], U8, name="w2_raw")
         w2_w = keep.tile([P, 2, 2 * H], U8, name="w2_w", align_bytes=64)
-        w2_raw_s = keep.tile([P, H], U8, name="w2_raw_s")
-        w2_s = [keep.tile([P, H], U8, name=f"w2_s{a}", align_bytes=64) for a in range(2)]
+        w2_s = keep.tile([P, 2, H], U8, name="w2_s", align_bytes=64)
         w3_w = keep.tile([P, 2, N], I32, name="w3_w", align_bytes=64)
         w3_s = keep.tile([P, 2, N], U8, name="w3_s", align_bytes=64)
         c1_sb = keep.tile([P, 2, PACK], F32, name="c1_sb")
         c2_sb = keep.tile([P, 2, PACK], F32, name="c2_sb")
         b_sb = keep.tile([P, N_TILES], F32, name="b_sb")
-        w1_raw = {(a, g): keep.tile([P, PACK, KP], F32, name=f"w1_raw{a}{g}") for a in range(2) for g in range(2)}
-        w1_w = {(a, g): keep.tile([P, KP], U32, name=f"w1_w{a}{g}", align_bytes=64) for a in range(2) for g in range(2)}
+        ident = keep.tile([P, P], F32, name="ident")
+        w1_raw = {(a, g): keep.tile([P, PACK, KP], F32, name=f"w1_raw{a}{g}", align_bytes=64) for a in range(2) for g in range(2)}
+        w1_w = {}
         w1_s = {(a, g): keep.tile([P, KP], U8, name=f"w1_s{a}{g}", align_bytes=64) for a in range(2) for g in range(2)}
 
-        for plane in (tab_s, w2_raw_s, v_s[1], w2_s[1], w3_s):
+        for plane in (tab_s, w2_s, v_s[1], w3_s):
             nc.vector.memset(plane[:].bitcast(I32), 0)
+        make_identity(nc, ident[:])
+
+        banks_taken = []
+
+        def next_bank(shape):
+            banks_taken.append(shape)
+            return psum.tile(shape, F32, name=f"bank{(len(banks_taken) - 1) % 8}")
 
         def load_plane(i):
             a, slot = divmod(i, PACK)
@@ -71,186 +78,238 @@ def tile_list_frost_risk_map_kernel(
             rows = w1[a * KP : (a + 1) * KP, g * KP : (g + 1) * KP].rearrange("(p j) c -> p j c", j=PACK)
             nc.sync.dma_start(out=w1_raw[a, g][:], in_=rows)
 
-        def load_packed_scales(plane, scales):
-            for q in range(4):
-                nc.sync.dma_start(
-                    out=plane[32 * q : 32 * q + 8, :].bitcast(I32), in_=scales[:, 4 * q : 4 * q + 4, :].bitcast(I32)
-                )
-
         def load_scales(plane, scales):
             for q in range(4):
                 rows = scales[:, 4 * q : 4 * q + 4, :].rearrange("a r c -> r a c")
                 nc.sync.dma_start(out=plane[32 * q : 32 * q + 4, :, :].bitcast(I32), in_=rows.bitcast(I32))
 
-        load_plane(0)
-        nc.sync.dma_start(idx3[:], offs3)
-        nc.sync.dma_start(idx2[:], offs2)
-        load_plane(1)
-        nc.sync.dma_start(idx[:], offs)
-        load_packed_scales(tab_s, tab_scales)
-        load_packed_scales(w2_raw_s, w2_scales)
-        load_plane(2)
-        load_w1(0, 0)
-        load_w1(1, 0)
-        load_plane(3)
-        load_plane(4)
-        load_w1(0, 1)
-        load_plane(5)
-        nc.sync.dma_start(out=c1_sb[:], in_=c1.rearrange("(g p t) -> p g t", g=2, t=PACK))
-        nc.sync.dma_start(out=c2_sb[:], in_=c2.rearrange("(g p t) -> p g t", g=2, t=PACK))
+        picked = [keep.tile([P, HALF], F32, name=f"picked{n}") for n in range(2)]
+        x0 = keep.tile([P, PACK, S], F32, name="x0")
+        x1 = [keep.tile([P, PACK, HALF], F32, name=f"x1_{h}") for h in range(2)]
+        x0_w = keep.tile([P, S], U32, name="x0_w", align_bytes=64)
+        x0_s = keep.tile([P, S], U8, name="x0_s", align_bytes=64)
+        x1_w = [keep.tile([P, HALF], U32, name=f"x1_w{h}", align_bytes=64) for h in range(2)]
+        x1_s = [keep.tile([P, HALF], U8, name=f"x1_s{h}", align_bytes=64) for h in range(2)]
 
-        picked = [keep.tile([P, HALF], F32, name=f"picked{h}") for h in range(2)]
-        x_f32 = [[keep.tile([P, PACK, HALF], F32, name=f"x_f32_{a}{h}") for h in range(2)] for a in range(2)]
-        x_bf = [keep.tile([P, PACK * S], BF16, name=f"x_bf{a}", align_bytes=64) for a in range(2)]
-        x_w = [keep.tile([P, S], U32, name=f"x_w{a}", align_bytes=64) for a in range(2)]
-        x_s = [keep.tile([P, S], U8, name=f"x_s{a}", align_bytes=64) for a in range(2)]
-
-        def differences(i):
-            a, slot = divmod(i, PACK)
-            cols = [slice(h * HALF // 16, (h + 1) * HALF // 16) for h in range(2)]
-            for h in range(2):
-                nc.vector.tensor_copy(out=picked[h][:], in_=planes[i][:].indirect(idx3[:, cols[h]]))
-            for h in range(2):
+        def differences(i, first, width, outs, lower):
+            cols = [slice((first + n * width) // 16, (first + (n + 1) * width) // 16) for n in range(2)]
+            for n in range(2):
+                nc.vector.tensor_copy(out=lower[n], in_=planes[i][:].indirect(idx3[:, cols[n]]))
+            for n in range(2):
                 nc.vector.tensor_tensor(
-                    out=x_f32[a][h][:, slot, :],
-                    in0=planes[i][:].indirect(idx2[:, cols[h]]),
-                    in1=picked[h][:],
-                    op=ALU.subtract,
+                    out=outs[n], in0=planes[i][:].indirect(idx2[:, cols[n]]), in1=lower[n], op=ALU.subtract
                 )
 
-        def round_x(a):
-            for h in range(2):
-                nc.scalar.activation(
-                    out=x_bf[a][:, h * PACK * HALF : (h + 1) * PACK * HALF].rearrange("p (c i t) -> p c t i", i=4, t=PACK),
-                    in_=x_f32[a][h][:].rearrange("p t (c i) -> p c t i", i=4),
-                    func=ACT.Copy,
-                )
+        def whole_plane(i):
+            if i < PACK:
+                outs = [x0[:, i, h * HALF : (h + 1) * HALF] for h in range(2)]
+            else:
+                outs = [x1[h][:, i - PACK, :] for h in range(2)]
+            differences(i, 0, HALF, outs, [picked[n][:] for n in range(2)])
 
-        def quantise_x(a):
-            nc.vector.quantize_mx(out=x_w[a][:].bitcast(FP8X4), scales=x_s[a][:], in_=x_bf[a][:])
+        def half_plane(i, h, lower):
+            outs = [x1[h][:, i - PACK, n * QUARTER : (n + 1) * QUARTER] for n in range(2)]
+            differences(i, h * HALF, QUARTER, outs, lower)
 
-        def quantise_w1(a, g):
+        def quantise_x(x_f32, x_w, x_s, name, tag):
+            x_bf = keep.tile([P, PACK * x_f32.shape[2]], BF16, name=name, tag=tag, align_bytes=64)
+            nc.scalar.activation(
+                out=x_bf[:].rearrange("p (c i t) -> p c t i", i=4, t=PACK),
+                in_=x_f32[:].rearrange("p t (c i) -> p c t i", i=4),
+                func=ACT.Copy,
+            )
+            nc.vector.quantize_mx(out=x_w[:].bitcast(FP8X4), scales=x_s[:], in_=x_bf[:])
+
+        def round_w1(a, g):
             w1_bf = keep.tile([P, PACK * KP], BF16, name=f"w1_bf{a}{g}", align_bytes=64)
             nc.scalar.activation(
                 out=w1_bf[:].rearrange("p (t m j) -> p m j t", t=PACK, j=PACK),
                 in_=w1_raw[a, g][:].rearrange("p j (m t) -> p m j t", t=PACK),
                 func=ACT.Copy,
             )
+            return w1_bf
+
+        def quantise_w1(a, g, w1_bf):
+            w1_w[a, g] = keep.tile([P, KP], U32, name=f"w1_w{a}{g}", align_bytes=64)
             nc.vector.quantize_mx(out=w1_w[a, g][:].bitcast(FP8X4), scales=w1_s[a, g][:], in_=w1_bf[:])
 
         def gather_table(a):
             nc.vector.tensor_copy(out=v_w[a][:], in_=tab_w[a][:].bitcast(U32).indirect(idx[:]))
 
-        differences(0)
-        differences(1)
+        load_plane(0)
+        nc.sync.dma_start(idx3[:], offs3)
+        nc.sync.dma_start(idx2[:], offs2)
+        load_plane(1)
+        load_w1(0, 0)
+        load_plane(2)
+        nc.sync.dma_start(idx[:], offs)
+        for q in range(4):
+            nc.sync.dma_start(
+                out=tab_s[32 * q : 32 * q + 8, :].bitcast(I32), in_=tab_scales[:, 4 * q : 4 * q + 4, :].bitcast(I32)
+            )
+        load_w1(1, 0)
+        load_plane(3)
+        load_w1(0, 1)
+
+        whole_plane(0)
+        whole_plane(1)
         nc.vector.tensor_copy(out=v_s[0][:], in_=tab_s[:].indirect(idx[:]))
-        nc.vector.tensor_copy(
-            out=w2_s[0][:].rearrange("p (g t m) -> p g t m", g=2, t=PACK),
-            in_=w2_raw_s[:].rearrange("p (g m t) -> p g t m", g=2, t=PACK),
-        )
-        load_plane(6)
-        nc.sync.dma_start(out=w2_raw[:].bitcast(I32), in_=w2_words.rearrange("a p c -> p a c").bitcast(I32))
-        load_w1(1, 1)
-        nc.sync.dma_start(out=v_s[1][0:112, :].bitcast(I32), in_=v_s[0][4:116, :].bitcast(I32))
-        nc.sync.dma_start(out=w2_s[1][0:112, :].bitcast(I32), in_=w2_s[0][4:116, :].bitcast(I32))
-        load_plane(7)
+
         load_table(0)
         load_table(1)
+        nc.sync.dma_start(out=w2_w[:].bitcast(I32), in_=w2_words.rearrange("a p c -> p a c").bitcast(I32))
+        load_scales(w2_s, w2_scales)
+        nc.sync.dma_start(out=v_s[1][0:112, :].bitcast(I32), in_=v_s[0][4:116, :].bitcast(I32))
+        load_plane(4)
+        load_plane(5)
+        load_w1(1, 1)
+        load_plane(6)
+        load_plane(7)
+        nc.sync.dma_start(out=c1_sb[:], in_=c1.rearrange("(g p t) -> p g t", g=2, t=PACK))
+        nc.sync.dma_start(out=c2_sb[:], in_=c2.rearrange("(g p t) -> p g t", g=2, t=PACK))
         nc.sync.dma_start(out=w3_w[:], in_=w3_words.rearrange("a p c i -> p a (c i)").bitcast(I32))
         load_scales(w3_s, w3_scales)
         with nc.allow_non_contiguous_dma(reason="one bias value to a partition"):
             nc.sync.dma_start(out=b_sb[:], in_=b.rearrange("(n p) -> p n", p=P))
 
-        differences(2)
-        quantise_w1(0, 0)
-        differences(3)
-        differences(4)
-        quantise_w1(1, 0)
-        round_x(0)
-        quantise_x(0)
-        differences(5)
-        quantise_w1(0, 1)
-        differences(6)
-        nc.vector.tensor_copy(
-            out=w2_w[:].rearrange("p a c -> p (a c)").bitcast(U16).rearrange("p (g t m) -> p g t m", t=PACK, m=P),
-            in_=w2_raw[:].rearrange("p a c -> p (a c)").bitcast(U16).rearrange("p (g m t) -> p g t m", t=PACK, m=P),
-        )
-        quantise_w1(1, 1)
-        differences(7)
-        round_x(1)
+        whole_plane(2)
+        quantise_w1(0, 0, round_w1(0, 0))
+        whole_plane(3)
+        quantise_w1(1, 0, round_w1(1, 0))
         gather_table(0)
-        quantise_x(1)
+        quantise_w1(0, 1, round_w1(0, 1))
         gather_table(1)
+        quantise_x(x0, x0_w, x0_s, "x0_bf", "w1_raw01")
 
-        u = [keep.tile([P, PACK, S], F32, name=f"u{g}") for g in range(2)]
-        for g in range(2):
-            for t in range(PACK):
-                d = psum.tile([P, S], F32, name="bank", bufs=8)
-                inner = ring.tile([P, S], F32, name="inner", bufs=3)
+        m_t = [keep.tile([P, 2, PACK, P], F32, name=f"m_t{q}") for q in range(4)]
+        for q in range(4):
+            for g in range(2):
+                bank = next_bank([P, KP])
                 for a in range(2):
                     nc.tensor.matmul_mx(
-                        out=d[:],
-                        lhsT=w1_w[a, g][:, t * P : (t + 1) * P].bitcast(FP8X4),
-                        lhsT_scale=w1_s[a, g][:, t * P : (t + 1) * P],
-                        rhs=x_w[a][:].bitcast(FP8X4),
-                        rhs_scale=x_s[a][:],
+                        out=bank[:],
+                        lhsT=v_w[a][:, q * P : (q + 1) * P].bitcast(FP8X4),
+                        lhsT_scale=v_s[a][:, q * P : (q + 1) * P],
+                        rhs=w2_w[:, a, 2 * g * KP : 2 * (g + 1) * KP].bitcast(FP4X4),
+                        rhs_scale=w2_s[:, a, g * KP : (g + 1) * KP],
                         start=(a == 0),
                         stop=(a == 1),
                     )
                 nc.scalar.activation(
-                    out=inner[:], in_=d[:], func=ACT.Identity, scale=c2_sb[:, g, t : t + 1], bias=c1_sb[:, g, t : t + 1]
+                    out=m_t[q][:, g, :, :], in_=bank[:].rearrange("p (m t) -> p t m", t=PACK), func=ACT.Copy
                 )
-                nc.vector.tensor_tensor(out=u[g][:, t, :], in0=d[:], in1=inner[:], op=ALU.mult)
+
+        u = {(h, g): keep.tile([P, PACK, HALF], F32, name=f"u{h}{g}") for h in range(2) for g in range(2)}
+
+        def quadratic_part(h):
+            x_w = [x0_w[:, h * HALF : (h + 1) * HALF], x1_w[h][:]]
+            x_s = [x0_s[:, h * HALF : (h + 1) * HALF], x1_s[h][:]]
+            for g in range(2):
+                for pair in range(2):
+                    d = next_bank([P, 2, HALF])
+                    inner = ring.tile([P, 2, HALF], F32, name="inner", bufs=4)
+                    for s in range(2):
+                        t = 2 * pair + s
+                        for a in range(2):
+                            nc.tensor.matmul_mx(
+                                out=d[:, s, :],
+                                lhsT=w1_w[a, g][:, t * P : (t + 1) * P].bitcast(FP8X4),
+                                lhsT_scale=w1_s[a, g][:, t * P : (t + 1) * P],
+                                rhs=x_w[a].bitcast(FP8X4),
+                                rhs_scale=x_s[a],
+                                start=(a == 0),
+                                stop=(a == 1),
+                            )
+                    for s in range(2):
+                        t = 2 * pair + s
+                        nc.scalar.activation(
+                            out=inner[:, s, :],
+                            in_=d[:, s, :],
+                            func=ACT.Identity,
+                            scale=c2_sb[:, g, t : t + 1],
+                            bias=c1_sb[:, g, t : t + 1],
+                        )
+                    nc.vector.tensor_tensor(
+                        out=u[h, g][:, 2 * pair : 2 * pair + 2, :], in0=d[:], in1=inner[:], op=ALU.mult
+                    )
+
+        whole_plane(4)
+        last_w1_bf = round_w1(1, 1)
+        whole_plane(5)
+        quarters = [picked[n][:, 0:QUARTER] for n in range(2)]
+        half_plane(6, 0, quarters)
+        picked_7 = keep.tile([P, 2, QUARTER], F32, name="picked_7", tag="w1_w11", align_bytes=64)
+        half_plane(7, 0, [picked_7[:, n, :] for n in range(2)])
+        half_plane(6, 1, [picked_7[:, n, :] for n in range(2)])
+        quantise_w1(1, 1, last_w1_bf)
+        quantise_x(x1[0], x1_w[0], x1_s[0], "x1_bf0", "x1_bf0")
+        last_picked = keep.tile([P, 2, QUARTER], F32, name="last_picked", tag="x1_bf0", align_bytes=64)
+        half_plane(7, 1, [last_picked[:, n, :] for n in range(2)])
+        quadratic_part(0)
+        quantise_x(x1[1], x1_w[1], x1_s[1], "x1_bf1", "x1_bf1")
+        quadratic_part(1)
 
         h_bf = [keep.tile([P, 2, KP], BF16, name=f"h_bf{q}", align_bytes=64) for q in range(4)]
+        h_w = [keep.tile([P, 2, P], U32, name=f"h_w{q}", align_bytes=64) for q in range(4)]
+        h_s = [keep.tile([P, 2, P], U8, name=f"h_s{q}", align_bytes=64) for q in range(4)]
+        y_sb = [keep.tile([P, N_TILES, P], F32, name=f"y_sb{q}") for q in range(4)]
 
         def add_constant_term(q, g):
-            m = psum.tile([P, PACK, P], F32, name="bank", bufs=8)
+            m = next_bank([P, PACK, P])
             for t in range(PACK):
-                c0 = g * KP + t * P
-                for a in range(2):
-                    nc.tensor.matmul_mx(
-                        out=m[:, t, :],
-                        lhsT=w2_w[:, a, 2 * c0 : 2 * (c0 + P)].bitcast(FP4X4),
-                        lhsT_scale=w2_s[a][:, c0 : c0 + P],
-                        rhs=v_w[a][:, q * P : (q + 1) * P].bitcast(FP8X4),
-                        rhs_scale=v_s[a][:, q * P : (q + 1) * P],
-                        start=(a == 0),
-                        stop=(a == 1),
-                    )
+                nc.tensor.transpose(m[:, t, :], m_t[q][:, g, t, :], ident[:])
+            j0 = (q % 2) * P
             nc.vector.tensor_tensor(
                 out=h_bf[q][:, g, :].rearrange("p (c i t) -> p c t i", i=4, t=PACK),
                 in0=m[:].rearrange("p t (c i) -> p c t i", i=4),
-                in1=u[g][:, :, q * P : (q + 1) * P].rearrange("p t (c i) -> p c t i", i=4),
+                in1=u[q // 2, g][:, :, j0 : j0 + P].rearrange("p t (c i) -> p c t i", i=4),
                 op=ALU.add,
             )
 
-        def damage_indices(q):
-            h_w = ring.tile([P, 2 * P], U32, name="h_w", align_bytes=64)
-            h_s = ring.tile([P, 2 * P], U8, name="h_s", align_bytes=64)
-            nc.vector.quantize_mx(
-                out=h_w[:].bitcast(FP8X4), scales=h_s[:], in_=h_bf[q][:].rearrange("p g c -> p (g c)")
+        def last_product(y, q, n, g):
+            nc.tensor.matmul_mx(
+                out=y,
+                lhsT=w3_w[:, g, n * P : (n + 1) * P].bitcast(FP8X4),
+                lhsT_scale=w3_s[:, g, n * P : (n + 1) * P],
+                rhs=h_w[q][:, g, :].bitcast(FP8X4),
+                rhs_scale=h_s[q][:, g, :],
+                start=(g == 0),
+                stop=(g == 1),
             )
-            y = psum.tile([P, N_TILES, P], F32, name="bank", bufs=8)
-            y_sb = ring.tile([P, N_TILES, P], F32, name="y_sb", bufs=4)
+
+        def damage_indices(q):
+            nc.vector.quantize_mx(
+                out=h_w[q][:].rearrange("p g c -> p (g c)").bitcast(FP8X4),
+                scales=h_s[q][:].rearrange("p g c -> p (g c)"),
+                in_=h_bf[q][:].rearrange("p g c -> p (g c)"),
+            )
+            y = next_bank([P, N_TILES, P])
             for n in range(N_TILES):
                 for g in range(2):
-                    nc.tensor.matmul_mx(
-                        out=y[:, n, :],
-                        lhsT=w3_w[:, g, n * P : (n + 1) * P].bitcast(FP8X4),
-                        lhsT_scale=w3_s[:, g, n * P : (n + 1) * P],
-                        rhs=h_w[:, g * P : (g + 1) * P].bitcast(FP8X4),
-                        rhs_scale=h_s[:, g * P : (g + 1) * P],
-                        start=(g == 0),
-                        stop=(g == 1),
-                    )
+                    last_product(y[:, n, :], q, n, g)
             for n in range(N_TILES):
-                nc.scalar.activation(out=y_sb[:, n, :], in_=y[:, n, :], func=ACT.Identity, bias=b_sb[:, n : n + 1])
-            nc.sync.dma_start(out=out[:, q * P : (q + 1) * P].rearrange("(n p) j -> p n j", p=P), in_=y_sb[:])
+                nc.scalar.activation(out=y_sb[q][:, n, :], in_=y[:, n, :], func=ACT.Identity, bias=b_sb[:, n : n + 1])
+            nc.sync.dma_start(out=out[:, q * P : (q + 1) * P].rearrange("(n p) j -> p n j", p=P), in_=y_sb[q][:])
 
-        for q in range(4):
+        for q in range(3):
             add_constant_term(q, 0)
             if q > 0:
                 damage_indices(q - 1)
             add_constant_term(q, 1)
-        damage_indices(3)
+        q = 3
+        add_constant_term(q, 0)
+        damage_indices(2)
+        ys = [next_bank([P, P]) for n in range(N_TILES)]
+        nc.vector.quantize_mx(out=h_w[q][:, 0, :].bitcast(FP8X4), scales=h_s[q][:, 0, :], in_=h_bf[q][:, 0, :])
+        for n in range(N_TILES):
+            last_product(ys[n][:], q, n, 0)
+        add_constant_term(q, 1)
+        nc.vector.quantize_mx(out=h_w[q][:, 1, :].bitcast(FP8X4), scales=h_s[q][:, 1, :], in_=h_bf[q][:, 1, :])
+        for n in range(N_TILES):
+            last_product(ys[n][:], q, n, 1)
+        for n in range(N_TILES):
+            if n == 1:
+                nc.scalar.activation(out=y_sb[q][:, n, :], in_=ys[n][:], func=ACT.Identity, bias=b_sb[:, n : n + 1])
+            else:
+                nc.vector.tensor_scalar_add(out=y_sb[q][:, n, :], in0=ys[n][:], scalar1=b_sb[:, n : n + 1])
+        nc.sync.dma_start(out=out[:, q * P : (q + 1) * P].rearrange("(n p) j -> p n j", p=P), in_=y_sb[q][:])

@@ -20,9 +20,14 @@ ACT = mybir.ActivationFunctionType
 P = 128
 PACK = 4
 KP = P * PACK
+PASSES = 2
 HALF = S // 2
 QUARTER = S // 4
 N_TILES = N // P
+QUADRANTS = 4
+STRIPE = 16
+RUN = 4
+ALIGN = 256
 
 
 def tile_list_frost_risk_map_kernel(
@@ -32,237 +37,169 @@ def tile_list_frost_risk_map_kernel(
     with ExitStack() as ctx:
         lists = ctx.enter_context(tc.tile_pool(name="lists", bufs=1))
         keep = ctx.enter_context(tc.tile_pool(name="keep", bufs=1))
-        ring = ctx.enter_context(tc.tile_pool(name="ring", bufs=2))
         psum = ctx.enter_context(tc.psum_pool(name="psum", bufs=1))
 
-        idx = lists.tile([P, S // 16], U16, name="idx")
-        idx2 = lists.tile([P, S // 16], U16, name="idx2")
-        idx3 = lists.tile([P, S // 16], U16, name="idx3")
+        def held(name, shape, dtype, tag=""):
+            return keep.tile(shape, dtype, name=name, tag=tag, align_bytes=ALIGN)
 
-        planes = [keep.tile([P, T2], F32, name=f"plane{i}") for i in range(2 * PACK)]
-        tab_w = [keep.tile([P, T], I32, name=f"tab_w{a}") for a in range(2)]
-        tab_s = keep.tile([P, T], U8, name="tab_s")
-        v_w = [keep.tile([P, S], U32, name=f"v_w{a}", align_bytes=64) for a in range(2)]
-        v_s = [keep.tile([P, S], U8, name=f"v_s{a}", align_bytes=64) for a in range(2)]
-        w2_w = keep.tile([P, 2, 2 * H], U8, name="w2_w", align_bytes=64)
-        w2_s = keep.tile([P, 2, H], U8, name="w2_s", align_bytes=64)
-        w3_w = keep.tile([P, 2, N], I32, name="w3_w", align_bytes=64)
-        w3_s = keep.tile([P, 2, N], U8, name="w3_s", align_bytes=64)
-        c1_sb = keep.tile([P, 2, PACK], F32, name="c1_sb")
-        c2_sb = keep.tile([P, 2, PACK], F32, name="c2_sb")
-        b_sb = keep.tile([P, N_TILES], F32, name="b_sb")
-        ident = keep.tile([P, P], F32, name="ident")
-        w1_raw = {(a, g): keep.tile([P, PACK, KP], F32, name=f"w1_raw{a}{g}", align_bytes=64) for a in range(2) for g in range(2)}
-        w1_w = {}
-        w1_s = {(a, g): keep.tile([P, KP], U8, name=f"w1_s{a}{g}", align_bytes=64) for a in range(2) for g in range(2)}
+        def bank(number, shape):
+            return psum.tile(shape, F32, name=f"bank{number}")
 
-        for plane in (tab_s, w2_s, v_s[1], w3_s):
-            nc.vector.memset(plane[:].bitcast(I32), 0)
+        idx = lists.tile([P, S // STRIPE], U16, name="idx")
+        idx2 = lists.tile([P, S // STRIPE], U16, name="idx2")
+        idx3 = lists.tile([P, S // STRIPE], U16, name="idx3")
+
+        rows = [held(f"rows{n}", [P, T2], F32) for n in range(PASSES * PACK)]
+        tab_w = [held(f"tab_w{a}", [P, T], I32) for a in range(PASSES)]
+        tab_s = held("tab_s", [P, T], U8)
+        v_w = [held(f"v_w{a}", [P, S], U32) for a in range(PASSES)]
+        v_s = [held(f"v_s{a}", [P, S], U8) for a in range(PASSES)]
+        w2_w = held("w2_w", [P, PASSES, 2 * H], U8)
+        w2_s = held("w2_s", [P, PASSES, H], U8)
+        w3_w = held("w3_w", [P, PASSES, N], I32)
+        w3_s = held("w3_s", [P, PASSES, N], U8)
+        c1_sb = held("c1_sb", [P, PASSES, PACK], F32)
+        c2_sb = held("c2_sb", [P, PASSES, PACK], F32)
+        b_sb = held("b_sb", [P, N_TILES], F32)
+        ident = held("ident", [P, P], F32)
+        w1_pass0 = held("w1_pass0", [P, PACK, H], F32)
+        w1_pass1 = [held(f"w1_pass1_{g}", [P, PACK, KP], F32) for g in range(PASSES)]
+        w1_w = {(a, g): held(f"w1_w{a}{g}", [P, KP], U32) for a in range(PASSES) for g in range(PASSES)}
+        w1_s = {(a, g): held(f"w1_s{a}{g}", [P, KP], U8) for a in range(PASSES) for g in range(PASSES)}
+        lower = [held(f"lower{n}", [P, HALF], F32) for n in range(2)]
+        x0 = held("x0", [P, PACK, S], F32)
+        x1 = [held(f"x1_{h}", [P, PACK, HALF], F32) for h in range(2)]
+        x0_w, x0_s = held("x0_w", [P, S], U32), held("x0_s", [P, S], U8)
+        x1_w = [held(f"x1_w{h}", [P, HALF], U32) for h in range(2)]
+        x1_s = [held(f"x1_s{h}", [P, HALF], U8) for h in range(2)]
+        m_t = [held(f"m_t{q}", [P, PASSES, PACK, P], F32) for q in range(4)]
+        quad = {(h, g): held(f"quad{h}{g}", [P, PACK, HALF], F32) for h in range(2) for g in range(PASSES)}
+        h_bf = [held(f"h_bf{q}", [P, PASSES, KP], BF16) for q in range(4)]
+        h_w = [held(f"h_w{q}", [P, PASSES, P], U32) for q in range(4)]
+        h_s = [held(f"h_s{q}", [P, PASSES, P], U8) for q in range(4)]
+        y_sb = [held(f"y_sb{q}", [P, N_TILES, P], F32) for q in range(4)]
+
+        for scales in (tab_s, w2_s, v_s[1], w3_s):
+            nc.vector.memset(scales[:].bitcast(I32), 0)
         make_identity(nc, ident[:])
 
-        banks_taken = []
-
-        def next_bank(shape):
-            banks_taken.append(shape)
-            return psum.tile(shape, F32, name=f"bank{(len(banks_taken) - 1) % 8}")
-
-        def load_plane(i):
-            a, slot = divmod(i, PACK)
-            rows = xT[a * KP : (a + 1) * KP, :].rearrange("(p i) t -> p i t", i=PACK)
-            nc.sync.dma_start(out=planes[i][:], in_=rows[:, slot, :])
+        def load_rows(n):
+            a, i = divmod(n, PACK)
+            nc.sync.dma_start(out=rows[n][:], in_=xT[a * KP : (a + 1) * KP, :].rearrange("(p i) t -> p i t", i=PACK)[:, i, :])
 
         def load_table(a):
             nc.sync.dma_start(out=tab_w[a][:], in_=tab_words[a].rearrange("p t i -> p (t i)").bitcast(I32))
 
-        def load_w1(a, g):
-            rows = w1[a * KP : (a + 1) * KP, g * KP : (g + 1) * KP].rearrange("(p j) c -> p j c", j=PACK)
-            nc.sync.dma_start(out=w1_raw[a, g][:], in_=rows)
+        def load_w1_pass1(g):
+            part = w1[KP : 2 * KP, g * KP : (g + 1) * KP]
+            nc.sync.dma_start(out=w1_pass1[g][:], in_=part.rearrange("(p i) c -> p i c", i=PACK))
 
-        def load_scales(plane, scales):
-            for q in range(4):
-                rows = scales[:, 4 * q : 4 * q + 4, :].rearrange("a r c -> r a c")
-                nc.sync.dma_start(out=plane[32 * q : 32 * q + 4, :, :].bitcast(I32), in_=rows.bitcast(I32))
+        def load_scales(tile, scales):
+            for n in range(QUADRANTS):
+                part = scales[:, 4 * n : 4 * n + 4, :].rearrange("a r c -> r a c")
+                nc.sync.dma_start(out=tile[32 * n : 32 * n + 4, :, :].bitcast(I32), in_=part.bitcast(I32))
 
-        picked = [keep.tile([P, HALF], F32, name=f"picked{n}") for n in range(2)]
-        x0 = keep.tile([P, PACK, S], F32, name="x0")
-        x1 = [keep.tile([P, PACK, HALF], F32, name=f"x1_{h}") for h in range(2)]
-        x0_w = keep.tile([P, S], U32, name="x0_w", align_bytes=64)
-        x0_s = keep.tile([P, S], U8, name="x0_s", align_bytes=64)
-        x1_w = [keep.tile([P, HALF], U32, name=f"x1_w{h}", align_bytes=64) for h in range(2)]
-        x1_s = [keep.tile([P, HALF], U8, name=f"x1_s{h}", align_bytes=64) for h in range(2)]
-
-        def differences(i, first, width, outs, lower):
-            cols = [slice((first + n * width) // 16, (first + (n + 1) * width) // 16) for n in range(2)]
-            for n in range(2):
-                nc.vector.tensor_copy(out=lower[n], in_=planes[i][:].indirect(idx3[:, cols[n]]))
-            for n in range(2):
+        def differences(n, first, width, outs, scratch):
+            cols = [slice((first + e * width) // STRIPE, (first + (e + 1) * width) // STRIPE) for e in range(2)]
+            for e in range(2):
+                nc.vector.tensor_copy(out=scratch[e], in_=rows[n][:].indirect(idx3[:, cols[e]]))
+            for e in range(2):
                 nc.vector.tensor_tensor(
-                    out=outs[n], in0=planes[i][:].indirect(idx2[:, cols[n]]), in1=lower[n], op=ALU.subtract
+                    out=outs[e], in0=rows[n][:].indirect(idx2[:, cols[e]]), in1=scratch[e], op=ALU.subtract
                 )
 
-        def whole_plane(i):
-            if i < PACK:
-                outs = [x0[:, i, h * HALF : (h + 1) * HALF] for h in range(2)]
-            else:
-                outs = [x1[h][:, i - PACK, :] for h in range(2)]
-            differences(i, 0, HALF, outs, [picked[n][:] for n in range(2)])
+        def all_columns(n):
+            a, i = divmod(n, PACK)
+            outs = [x0[:, i, h * HALF : (h + 1) * HALF] if a == 0 else x1[h][:, i, :] for h in range(2)]
+            differences(n, 0, HALF, outs, [lower[e][:] for e in range(2)])
 
-        def half_plane(i, h, lower):
-            outs = [x1[h][:, i - PACK, n * QUARTER : (n + 1) * QUARTER] for n in range(2)]
-            differences(i, h * HALF, QUARTER, outs, lower)
+        def half_of_columns(n, h, scratch):
+            outs = [x1[h][:, n - PACK, e * QUARTER : (e + 1) * QUARTER] for e in range(2)]
+            differences(n, h * HALF, QUARTER, outs, scratch)
 
-        def quantise_x(x_f32, x_w, x_s, name, tag):
-            x_bf = keep.tile([P, PACK * x_f32.shape[2]], BF16, name=name, tag=tag, align_bytes=64)
+        def quantise_x(x_f32, x_w, x_s, name):
+            x_bf = held(name, [P, PACK * x_f32.shape[2]], BF16)
             nc.scalar.activation(
-                out=x_bf[:].rearrange("p (c i t) -> p c t i", i=4, t=PACK),
-                in_=x_f32[:].rearrange("p t (c i) -> p c t i", i=4),
+                out=x_bf[:].rearrange("p (c e i) -> p c i e", e=RUN, i=PACK),
+                in_=x_f32[:].rearrange("p i (c e) -> p c i e", e=RUN),
                 func=ACT.Copy,
             )
             nc.vector.quantize_mx(out=x_w[:].bitcast(FP8X4), scales=x_s[:], in_=x_bf[:])
 
         def round_w1(a, g):
-            w1_bf = keep.tile([P, PACK * KP], BF16, name=f"w1_bf{a}{g}", align_bytes=64)
+            w1_bf = held(f"w1_bf{a}{g}", [P, PACK * KP], BF16)
+            part = w1_pass0[:, :, g * KP : (g + 1) * KP] if a == 0 else w1_pass1[g][:]
             nc.scalar.activation(
-                out=w1_bf[:].rearrange("p (t m j) -> p m j t", t=PACK, j=PACK),
-                in_=w1_raw[a, g][:].rearrange("p j (m t) -> p m j t", t=PACK),
+                out=w1_bf[:].rearrange("p (t m i) -> p m i t", t=PACK, i=PACK),
+                in_=part.rearrange("p i (m t) -> p m i t", t=PACK),
                 func=ACT.Copy,
             )
             return w1_bf
 
         def quantise_w1(a, g, w1_bf):
-            w1_w[a, g] = keep.tile([P, KP], U32, name=f"w1_w{a}{g}", align_bytes=64)
             nc.vector.quantize_mx(out=w1_w[a, g][:].bitcast(FP8X4), scales=w1_s[a, g][:], in_=w1_bf[:])
 
-        def gather_table(a):
+        def gather_words(a):
             nc.vector.tensor_copy(out=v_w[a][:], in_=tab_w[a][:].bitcast(U32).indirect(idx[:]))
 
-        load_plane(0)
-        nc.sync.dma_start(idx3[:], offs3)
-        nc.sync.dma_start(idx2[:], offs2)
-        load_plane(1)
-        load_w1(0, 0)
-        load_plane(2)
-        nc.sync.dma_start(idx[:], offs)
-        for q in range(4):
-            nc.sync.dma_start(
-                out=tab_s[32 * q : 32 * q + 8, :].bitcast(I32), in_=tab_scales[:, 4 * q : 4 * q + 4, :].bitcast(I32)
-            )
-        load_w1(1, 0)
-        load_plane(3)
-        load_w1(0, 1)
-
-        whole_plane(0)
-        whole_plane(1)
-        nc.vector.tensor_copy(out=v_s[0][:], in_=tab_s[:].indirect(idx[:]))
-
-        load_table(0)
-        load_table(1)
-        nc.sync.dma_start(out=w2_w[:].bitcast(I32), in_=w2_words.rearrange("a p c -> p a c").bitcast(I32))
-        load_scales(w2_s, w2_scales)
-        nc.sync.dma_start(out=v_s[1][0:112, :].bitcast(I32), in_=v_s[0][4:116, :].bitcast(I32))
-        load_plane(4)
-        load_plane(5)
-        load_w1(1, 1)
-        load_plane(6)
-        load_plane(7)
-        nc.sync.dma_start(out=c1_sb[:], in_=c1.rearrange("(g p t) -> p g t", g=2, t=PACK))
-        nc.sync.dma_start(out=c2_sb[:], in_=c2.rearrange("(g p t) -> p g t", g=2, t=PACK))
-        nc.sync.dma_start(out=w3_w[:], in_=w3_words.rearrange("a p c i -> p a (c i)").bitcast(I32))
-        load_scales(w3_s, w3_scales)
-        with nc.allow_non_contiguous_dma(reason="one bias value to a partition"):
-            nc.sync.dma_start(out=b_sb[:], in_=b.rearrange("(n p) -> p n", p=P))
-
-        whole_plane(2)
-        quantise_w1(0, 0, round_w1(0, 0))
-        whole_plane(3)
-        quantise_w1(1, 0, round_w1(1, 0))
-        gather_table(0)
-        quantise_w1(0, 1, round_w1(0, 1))
-        gather_table(1)
-        quantise_x(x0, x0_w, x0_s, "x0_bf", "w1_raw01")
-
-        m_t = [keep.tile([P, 2, PACK, P], F32, name=f"m_t{q}") for q in range(4)]
-        for q in range(4):
-            for g in range(2):
-                bank = next_bank([P, KP])
-                for a in range(2):
-                    nc.tensor.matmul_mx(
-                        out=bank[:],
-                        lhsT=v_w[a][:, q * P : (q + 1) * P].bitcast(FP8X4),
-                        lhsT_scale=v_s[a][:, q * P : (q + 1) * P],
-                        rhs=w2_w[:, a, 2 * g * KP : 2 * (g + 1) * KP].bitcast(FP4X4),
-                        rhs_scale=w2_s[:, a, g * KP : (g + 1) * KP],
-                        start=(a == 0),
-                        stop=(a == 1),
-                    )
-                nc.scalar.activation(
-                    out=m_t[q][:, g, :, :], in_=bank[:].rearrange("p (m t) -> p t m", t=PACK), func=ACT.Copy
+        def hardiness_transposed(q, g):
+            sums = bank(PASSES * q + g, [P, KP])
+            for a in range(PASSES):
+                nc.tensor.matmul_mx(
+                    out=sums[:],
+                    lhsT=v_w[a][:, q * P : (q + 1) * P].bitcast(FP8X4),
+                    lhsT_scale=v_s[a][:, q * P : (q + 1) * P],
+                    rhs=w2_w[:, a, 2 * g * KP : 2 * (g + 1) * KP].bitcast(FP4X4),
+                    rhs_scale=w2_s[:, a, g * KP : (g + 1) * KP],
+                    start=(a == 0),
+                    stop=(a == PASSES - 1),
                 )
+            nc.scalar.activation(out=m_t[q][:, g, :, :], in_=sums[:].rearrange("p (m t) -> p t m", t=PACK), func=ACT.Copy)
 
-        u = {(h, g): keep.tile([P, PACK, HALF], F32, name=f"u{h}{g}") for h in range(2) for g in range(2)}
+        def hardiness(q, g, number):
+            m = bank(number, [P, PACK, P])
+            for t in range(PACK):
+                nc.tensor.transpose(m[:, t, :], m_t[q][:, g, t, :], ident[:])
+            return m
 
-        def quadratic_part(h):
+        def quadratic_terms(h):
             x_w = [x0_w[:, h * HALF : (h + 1) * HALF], x1_w[h][:]]
             x_s = [x0_s[:, h * HALF : (h + 1) * HALF], x1_s[h][:]]
-            for g in range(2):
+            for g in range(PASSES):
                 for pair in range(2):
-                    d = next_bank([P, 2, HALF])
-                    inner = ring.tile([P, 2, HALF], F32, name="inner", bufs=4)
-                    for s in range(2):
-                        t = 2 * pair + s
-                        for a in range(2):
+                    d = bank(2 * g + pair, [P, 2, HALF])
+                    inner = held(f"inner{g}{pair}", [P, 2, HALF], F32)
+                    for e in range(2):
+                        t = 2 * pair + e
+                        for a in range(PASSES):
                             nc.tensor.matmul_mx(
-                                out=d[:, s, :],
+                                out=d[:, e, :],
                                 lhsT=w1_w[a, g][:, t * P : (t + 1) * P].bitcast(FP8X4),
                                 lhsT_scale=w1_s[a, g][:, t * P : (t + 1) * P],
                                 rhs=x_w[a].bitcast(FP8X4),
                                 rhs_scale=x_s[a],
                                 start=(a == 0),
-                                stop=(a == 1),
+                                stop=(a == PASSES - 1),
                             )
-                    for s in range(2):
-                        t = 2 * pair + s
+                    for e in range(2):
+                        t = 2 * pair + e
                         nc.scalar.activation(
-                            out=inner[:, s, :],
-                            in_=d[:, s, :],
+                            out=inner[:, e, :],
+                            in_=d[:, e, :],
                             func=ACT.Identity,
                             scale=c2_sb[:, g, t : t + 1],
                             bias=c1_sb[:, g, t : t + 1],
                         )
                     nc.vector.tensor_tensor(
-                        out=u[h, g][:, 2 * pair : 2 * pair + 2, :], in0=d[:], in1=inner[:], op=ALU.mult
+                        out=quad[h, g][:, 2 * pair : 2 * pair + 2, :], in0=d[:], in1=inner[:], op=ALU.mult
                     )
 
-        whole_plane(4)
-        last_w1_bf = round_w1(1, 1)
-        whole_plane(5)
-        quarters = [picked[n][:, 0:QUARTER] for n in range(2)]
-        half_plane(6, 0, quarters)
-        picked_7 = keep.tile([P, 2, QUARTER], F32, name="picked_7", tag="w1_w11", align_bytes=64)
-        half_plane(7, 0, [picked_7[:, n, :] for n in range(2)])
-        half_plane(6, 1, [picked_7[:, n, :] for n in range(2)])
-        quantise_w1(1, 1, last_w1_bf)
-        quantise_x(x1[0], x1_w[0], x1_s[0], "x1_bf0", "x1_bf0")
-        last_picked = keep.tile([P, 2, QUARTER], F32, name="last_picked", tag="x1_bf0", align_bytes=64)
-        half_plane(7, 1, [last_picked[:, n, :] for n in range(2)])
-        quadratic_part(0)
-        quantise_x(x1[1], x1_w[1], x1_s[1], "x1_bf1", "x1_bf1")
-        quadratic_part(1)
-
-        h_bf = [keep.tile([P, 2, KP], BF16, name=f"h_bf{q}", align_bytes=64) for q in range(4)]
-        h_w = [keep.tile([P, 2, P], U32, name=f"h_w{q}", align_bytes=64) for q in range(4)]
-        h_s = [keep.tile([P, 2, P], U8, name=f"h_s{q}", align_bytes=64) for q in range(4)]
-        y_sb = [keep.tile([P, N_TILES, P], F32, name=f"y_sb{q}") for q in range(4)]
-
-        def add_constant_term(q, g):
-            m = next_bank([P, PACK, P])
-            for t in range(PACK):
-                nc.tensor.transpose(m[:, t, :], m_t[q][:, g, t, :], ident[:])
-            j0 = (q % 2) * P
+        def add_hardiness(q, g, m):
+            j0 = (q % 2) * QUARTER
             nc.vector.tensor_tensor(
-                out=h_bf[q][:, g, :].rearrange("p (c i t) -> p c t i", i=4, t=PACK),
-                in0=m[:].rearrange("p t (c i) -> p c t i", i=4),
-                in1=u[q // 2, g][:, :, j0 : j0 + P].rearrange("p t (c i) -> p c t i", i=4),
+                out=h_bf[q][:, g, :].rearrange("p (c e t) -> p c t e", e=RUN, t=PACK),
+                in0=m[:].rearrange("p t (c e) -> p c t e", e=RUN),
+                in1=quad[q // 2, g][:, :, j0 : j0 + QUARTER].rearrange("p t (c e) -> p c t e", e=RUN),
                 op=ALU.add,
             )
 
@@ -274,42 +211,113 @@ def tile_list_frost_risk_map_kernel(
                 rhs=h_w[q][:, g, :].bitcast(FP8X4),
                 rhs_scale=h_s[q][:, g, :],
                 start=(g == 0),
-                stop=(g == 1),
+                stop=(g == PASSES - 1),
             )
 
-        def damage_indices(q):
+        def store(q):
+            nc.sync.dma_start(out=out[:, q * P : (q + 1) * P].rearrange("(n p) j -> p n j", p=P), in_=y_sb[q][:])
+
+        def damage_indices(q, number):
             nc.vector.quantize_mx(
                 out=h_w[q][:].rearrange("p g c -> p (g c)").bitcast(FP8X4),
                 scales=h_s[q][:].rearrange("p g c -> p (g c)"),
                 in_=h_bf[q][:].rearrange("p g c -> p (g c)"),
             )
-            y = next_bank([P, N_TILES, P])
+            y = bank(number, [P, N_TILES, P])
             for n in range(N_TILES):
-                for g in range(2):
+                for g in range(PASSES):
                     last_product(y[:, n, :], q, n, g)
             for n in range(N_TILES):
                 nc.scalar.activation(out=y_sb[q][:, n, :], in_=y[:, n, :], func=ACT.Identity, bias=b_sb[:, n : n + 1])
-            nc.sync.dma_start(out=out[:, q * P : (q + 1) * P].rearrange("(n p) j -> p n j", p=P), in_=y_sb[q][:])
+            store(q)
 
-        for q in range(3):
-            add_constant_term(q, 0)
-            if q > 0:
-                damage_indices(q - 1)
-            add_constant_term(q, 1)
-        q = 3
-        add_constant_term(q, 0)
-        damage_indices(2)
-        ys = [next_bank([P, P]) for n in range(N_TILES)]
-        nc.vector.quantize_mx(out=h_w[q][:, 0, :].bitcast(FP8X4), scales=h_s[q][:, 0, :], in_=h_bf[q][:, 0, :])
-        for n in range(N_TILES):
-            last_product(ys[n][:], q, n, 0)
-        add_constant_term(q, 1)
-        nc.vector.quantize_mx(out=h_w[q][:, 1, :].bitcast(FP8X4), scales=h_s[q][:, 1, :], in_=h_bf[q][:, 1, :])
-        for n in range(N_TILES):
-            last_product(ys[n][:], q, n, 1)
-        for n in range(N_TILES):
-            if n == 1:
-                nc.scalar.activation(out=y_sb[q][:, n, :], in_=ys[n][:], func=ACT.Identity, bias=b_sb[:, n : n + 1])
-            else:
-                nc.vector.tensor_scalar_add(out=y_sb[q][:, n, :], in0=ys[n][:], scalar1=b_sb[:, n : n + 1])
-        nc.sync.dma_start(out=out[:, q * P : (q + 1) * P].rearrange("(n p) j -> p n j", p=P), in_=y_sb[q][:])
+        load_rows(0)
+        nc.sync.dma_start(idx3[:], offs3)
+        nc.sync.dma_start(idx2[:], offs2)
+        load_rows(1)
+        load_rows(2)
+        nc.sync.dma_start(out=w1_pass0[:], in_=w1[0:KP, :].rearrange("(p i) c -> p i c", i=PACK))
+        nc.sync.dma_start(idx[:], offs)
+        for n in range(QUADRANTS):
+            nc.sync.dma_start(
+                out=tab_s[32 * n : 32 * n + 8, :].bitcast(I32), in_=tab_scales[:, 4 * n : 4 * n + 4, :].bitcast(I32)
+            )
+        load_rows(3)
+        load_table(0)
+        load_table(1)
+        nc.sync.dma_start(out=w2_w[:].bitcast(I32), in_=w2_words.rearrange("a p c -> p a c").bitcast(I32))
+        load_scales(w2_s, w2_scales)
+
+        for n in range(3):
+            all_columns(n)
+        nc.vector.tensor_copy(out=v_s[0][:], in_=tab_s[:].indirect(idx[:]))
+
+        nc.sync.dma_start(out=v_s[1][0:112, :].bitcast(I32), in_=v_s[0][4:116, :].bitcast(I32))
+        load_rows(4)
+        load_rows(5)
+        load_w1_pass1(0)
+        load_rows(6)
+        load_rows(7)
+        load_w1_pass1(1)
+        nc.sync.dma_start(out=c1_sb[:], in_=c1.rearrange("(g p t) -> p g t", g=PASSES, t=PACK))
+        nc.sync.dma_start(out=c2_sb[:], in_=c2.rearrange("(g p t) -> p g t", g=PASSES, t=PACK))
+        nc.sync.dma_start(out=w3_w[:], in_=w3_words.rearrange("a p c i -> p a (c i)").bitcast(I32))
+        load_scales(w3_s, w3_scales)
+        with nc.allow_non_contiguous_dma(reason="one bias value to a partition"):
+            nc.sync.dma_start(out=b_sb[:], in_=b.rearrange("(n p) -> p n", p=P))
+
+        quantise_w1(0, 0, round_w1(0, 0))
+        all_columns(3)
+        w1_bf_01 = round_w1(0, 1)
+        gather_words(0)
+        quantise_w1(0, 1, w1_bf_01)
+        gather_words(1)
+        quantise_x(x0, x0_w, x0_s, "x0_bf")
+        for q in range(4):
+            for g in range(PASSES):
+                hardiness_transposed(q, g)
+
+        all_columns(4)
+        all_columns(5)
+        w1_bf_10 = round_w1(1, 0)
+        quarters = [lower[e][:, 0:QUARTER] for e in range(2)]
+        half_of_columns(6, 0, quarters)
+        half_of_columns(7, 0, quarters)
+        half_of_columns(6, 1, quarters)
+        quantise_w1(1, 0, w1_bf_10)
+        quantise_x(x1[0], x1_w[0], x1_s[0], "x1_bf0")
+        w1_bf_11 = round_w1(1, 1)
+        last_lower = held("last_lower", [P, 2, QUARTER], F32, tag="x1_bf0")
+        half_of_columns(7, 1, [last_lower[:, e, :] for e in range(2)])
+        quantise_w1(1, 1, w1_bf_11)
+
+        m = {(q, g): hardiness(q, g, 4 + PASSES * q + g) for q in range(2) for g in range(PASSES)}
+        quadratic_terms(0)
+        quantise_x(x1[1], x1_w[1], x1_s[1], "x1_bf1")
+
+        add_hardiness(0, 0, m[0, 0])
+        add_hardiness(1, 0, m[1, 0])
+        add_hardiness(0, 1, m[0, 1])
+        add_hardiness(1, 1, m[1, 1])
+        damage_indices(0, 5)
+        damage_indices(1, 7)
+        quadratic_terms(1)
+        for q, g, number in ((2, 0, 4), (3, 0, 6), (2, 1, 0), (3, 1, 1)):
+            m[q, g] = hardiness(q, g, number)
+        add_hardiness(2, 0, m[2, 0])
+        add_hardiness(2, 1, m[2, 1])
+        add_hardiness(3, 0, m[3, 0])
+        damage_indices(2, 4)
+
+        last = 3
+        ys = [bank(number, [P, P]) for number in (2, 3, 5)]
+        for g in range(PASSES):
+            if g == 1:
+                add_hardiness(last, g, m[last, g])
+            nc.vector.quantize_mx(out=h_w[last][:, g, :].bitcast(FP8X4), scales=h_s[last][:, g, :], in_=h_bf[last][:, g, :])
+            for n in range(N_TILES):
+                last_product(ys[n][:], last, n, g)
+        nc.vector.tensor_scalar_add(out=y_sb[last][:, 0, :], in0=ys[0][:], scalar1=b_sb[:, 0:1])
+        nc.scalar.activation(out=y_sb[last][:, 1, :], in_=ys[1][:], func=ACT.Identity, bias=b_sb[:, 1:2])
+        nc.vector.tensor_scalar_add(out=y_sb[last][:, 2, :], in0=ys[2][:], scalar1=b_sb[:, 2:3])
+        store(last)

@@ -52,6 +52,7 @@ def tile_list_frost_risk_map_kernel(
         rows = [held(f"rows{n}", [P, T2], F32) for n in range(PASSES * PACK)]
         tab_w = [held(f"tab_w{a}", [P, T], I32) for a in range(PASSES)]
         tab_s = held("tab_s", [P, T], U8)
+        v_rows = held("v_rows", [P, S], U8)
         v_w = [held(f"v_w{a}", [P, S], U32) for a in range(PASSES)]
         v_s = [held(f"v_s{a}", [P, S], U8) for a in range(PASSES)]
         w2_w = held("w2_w", [P, PASSES, 2 * H], U8)
@@ -79,8 +80,8 @@ def tile_list_frost_risk_map_kernel(
         h_s = [held(f"h_s{q}", [P, PASSES, P], U8) for q in range(4)]
         y_sb = [held(f"y_sb{q}", [P, N_TILES, P], F32) for q in range(4)]
 
-        for scales in (tab_s, w2_s, v_s[1], w3_s):
-            nc.vector.memset(scales[:].bitcast(I32), 0)
+        for part in (tab_s[32:64, :], tab_s[64:P, :], v_s[0][:], v_s[1][:], w2_s[:], w3_s[:]):
+            nc.vector.memset(part.bitcast(I32), 0)
         make_identity(nc, ident[:])
 
         def load_rows(n):
@@ -98,6 +99,11 @@ def tile_list_frost_risk_map_kernel(
             for n in range(QUADRANTS):
                 part = scales[:, 4 * n : 4 * n + 4, :].rearrange("a r c -> r a c")
                 nc.sync.dma_start(out=tile[32 * n : 32 * n + 4, :, :].bitcast(I32), in_=part.bitcast(I32))
+
+        def place_gathered_scales(a):
+            for n in range(QUADRANTS):
+                part = v_rows[16 * a + 4 * n : 16 * a + 4 * n + 4, :]
+                nc.sync.dma_start(out=v_s[a][32 * n : 32 * n + 4, :].bitcast(I32), in_=part.bitcast(I32))
 
         def differences(n, first, width, outs, scratch):
             cols = [slice((first + e * width) // STRIPE, (first + (e + 1) * width) // STRIPE) for e in range(2)]
@@ -117,8 +123,8 @@ def tile_list_frost_risk_map_kernel(
             outs = [x1[h][:, n - PACK, e * QUARTER : (e + 1) * QUARTER] for e in range(2)]
             differences(n, h * HALF, QUARTER, outs, scratch)
 
-        def quantise_x(x_f32, x_w, x_s, name):
-            x_bf = held(name, [P, PACK * x_f32.shape[2]], BF16)
+        def quantise_x(x_f32, x_w, x_s, name, tag=""):
+            x_bf = held(name, [P, PACK * x_f32.shape[2]], BF16, tag=tag)
             nc.scalar.activation(
                 out=x_bf[:].rearrange("p (c e i) -> p c i e", e=RUN, i=PACK),
                 in_=x_f32[:].rearrange("p i (c e) -> p c i e", e=RUN),
@@ -214,9 +220,6 @@ def tile_list_frost_risk_map_kernel(
                 stop=(g == PASSES - 1),
             )
 
-        def store(q):
-            nc.sync.dma_start(out=out[:, q * P : (q + 1) * P].rearrange("(n p) j -> p n j", p=P), in_=y_sb[q][:])
-
         def damage_indices(q, number):
             nc.vector.quantize_mx(
                 out=h_w[q][:].rearrange("p g c -> p (g c)").bitcast(FP8X4),
@@ -229,31 +232,23 @@ def tile_list_frost_risk_map_kernel(
                     last_product(y[:, n, :], q, n, g)
             for n in range(N_TILES):
                 nc.scalar.activation(out=y_sb[q][:, n, :], in_=y[:, n, :], func=ACT.Identity, bias=b_sb[:, n : n + 1])
-            store(q)
+            nc.sync.dma_start(out=out[:, q * P : (q + 1) * P].rearrange("(n p) j -> p n j", p=P), in_=y_sb[q][:])
 
+        nc.sync.dma_start(out=tab_s[0:32, :].bitcast(I32), in_=tab_scales.rearrange("a n t -> (a n) t").bitcast(I32))
+        nc.sync.dma_start(idx[:], offs)
         load_rows(0)
         nc.sync.dma_start(idx3[:], offs3)
         nc.sync.dma_start(idx2[:], offs2)
-        load_rows(1)
-        load_rows(2)
+        for n in range(1, PACK):
+            load_rows(n)
         nc.sync.dma_start(out=w1_pass0[:], in_=w1[0:KP, :].rearrange("(p i) c -> p i c", i=PACK))
-        nc.sync.dma_start(idx[:], offs)
-        for n in range(QUADRANTS):
-            nc.sync.dma_start(
-                out=tab_s[32 * n : 32 * n + 8, :].bitcast(I32), in_=tab_scales[:, 4 * n : 4 * n + 4, :].bitcast(I32)
-            )
-        load_rows(3)
-        load_table(0)
-        load_table(1)
+        nc.vector.tensor_copy(out=v_rows[:], in_=tab_s[:].indirect(idx[:]))
+        for a in range(PASSES):
+            load_table(a)
+            place_gathered_scales(a)
+        load_rows(4)
         nc.sync.dma_start(out=w2_w[:].bitcast(I32), in_=w2_words.rearrange("a p c -> p a c").bitcast(I32))
         load_scales(w2_s, w2_scales)
-
-        for n in range(3):
-            all_columns(n)
-        nc.vector.tensor_copy(out=v_s[0][:], in_=tab_s[:].indirect(idx[:]))
-
-        nc.sync.dma_start(out=v_s[1][0:112, :].bitcast(I32), in_=v_s[0][4:116, :].bitcast(I32))
-        load_rows(4)
         load_rows(5)
         load_w1_pass1(0)
         load_rows(6)
@@ -266,20 +261,20 @@ def tile_list_frost_risk_map_kernel(
         with nc.allow_non_contiguous_dma(reason="one bias value to a partition"):
             nc.sync.dma_start(out=b_sb[:], in_=b.rearrange("(n p) -> p n", p=P))
 
-        quantise_w1(0, 0, round_w1(0, 0))
-        all_columns(3)
-        w1_bf_01 = round_w1(0, 1)
-        gather_words(0)
-        quantise_w1(0, 1, w1_bf_01)
-        gather_words(1)
-        quantise_x(x0, x0_w, x0_s, "x0_bf")
+        for n in range(PACK):
+            all_columns(n)
+        w1_bf_0 = [round_w1(0, g) for g in range(PASSES)]
+        for a in range(PASSES):
+            gather_words(a)
+            quantise_w1(0, a, w1_bf_0[a])
+        all_columns(4)
+        quantise_x(x0, x0_w, x0_s, "x0_bf", tag="w1_pass0")
+        w1_bf_10 = round_w1(1, 0)
         for q in range(4):
             for g in range(PASSES):
                 hardiness_transposed(q, g)
 
-        all_columns(4)
         all_columns(5)
-        w1_bf_10 = round_w1(1, 0)
         quarters = [lower[e][:, 0:QUARTER] for e in range(2)]
         half_of_columns(6, 0, quarters)
         half_of_columns(7, 0, quarters)
@@ -320,4 +315,5 @@ def tile_list_frost_risk_map_kernel(
         nc.vector.tensor_scalar_add(out=y_sb[last][:, 0, :], in0=ys[0][:], scalar1=b_sb[:, 0:1])
         nc.scalar.activation(out=y_sb[last][:, 1, :], in_=ys[1][:], func=ACT.Identity, bias=b_sb[:, 1:2])
         nc.vector.tensor_scalar_add(out=y_sb[last][:, 2, :], in0=ys[2][:], scalar1=b_sb[:, 2:3])
-        store(last)
+        for n, queue in enumerate((nc.sync, nc.scalar, nc.sync)):
+            queue.dma_start(out=out[n * P : (n + 1) * P, last * P : (last + 1) * P], in_=y_sb[last][:, n, :])

@@ -67,18 +67,19 @@ def tile_list_frost_risk_map_kernel(
         w1_pass1 = [held(f"w1_pass1_{g}", [P, PACK, KP], F32) for g in range(PASSES)]
         w1_w = {(a, g): held(f"w1_w{a}{g}", [P, KP], U32) for a in range(PASSES) for g in range(PASSES)}
         w1_s = {(a, g): held(f"w1_s{a}{g}", [P, KP], U8) for a in range(PASSES) for g in range(PASSES)}
+        w1_bf = {(a, g): held(f"w1_bf{a}{g}", [P, PACK * KP], BF16) for a in range(PASSES) for g in range(PASSES)}
         lower = [held(f"lower{n}", [P, HALF], F32) for n in range(2)]
         x0 = held("x0", [P, PACK, S], F32)
         x1 = [held(f"x1_{h}", [P, PACK, HALF], F32) for h in range(2)]
         x0_w, x0_s = held("x0_w", [P, S], U32), held("x0_s", [P, S], U8)
-        x1_w = [held(f"x1_w{h}", [P, HALF], U32) for h in range(2)]
-        x1_s = [held(f"x1_s{h}", [P, HALF], U8) for h in range(2)]
-        m_t = [held(f"m_t{q}", [P, PASSES, PACK, P], F32) for q in range(4)]
-        quad = {(h, g): held(f"quad{h}{g}", [P, PACK, HALF], F32) for h in range(2) for g in range(PASSES)}
-        h_bf = [held(f"h_bf{q}", [P, PASSES, KP], BF16) for q in range(4)]
-        h_w = [held(f"h_w{q}", [P, PASSES, P], U32) for q in range(4)]
-        h_s = [held(f"h_s{q}", [P, PASSES, P], U8) for q in range(4)]
-        y_sb = [held(f"y_sb{q}", [P, N_TILES, P], F32) for q in range(4)]
+        x1_w, x1_s = held("x1_w", [P, S], U32), held("x1_s", [P, S], U8)
+        m_t = {(q, g): held(f"m_t{q}{g}", [P, PACK, P], F32) for q in range(4) for g in range(PASSES)}
+        quad = {(g, h): held(f"quad{g}{h}", [P, PACK, HALF], F32) for g in range(PASSES) for h in range(2)}
+        h_bf = [held(f"h_bf{g}", [P, PACK * S], BF16) for g in range(PASSES)]
+        h_w = [held(f"h_w{g}", [P, S], U32) for g in range(PASSES)]
+        h_s = [held(f"h_s{g}", [P, S], U8) for g in range(PASSES)]
+        y_half = held("y_half", [P, N_TILES, HALF], F32)
+        y_sb = {q: held(f"y_sb{q}", [P, N_TILES, P], F32) for q in (2, 3)}
 
         for part in (tab_s[32:64, :], tab_s[64:P, :], v_s[0][:], v_s[1][:], w2_s[:], w3_s[:]):
             nc.vector.memset(part.bitcast(I32), 0)
@@ -96,14 +97,14 @@ def tile_list_frost_risk_map_kernel(
             nc.sync.dma_start(out=w1_pass1[g][:], in_=part.rearrange("(p i) c -> p i c", i=PACK))
 
         def load_scales(tile, scales):
-            for n in range(QUADRANTS):
-                part = scales[:, 4 * n : 4 * n + 4, :].rearrange("a r c -> r a c")
-                nc.sync.dma_start(out=tile[32 * n : 32 * n + 4, :, :].bitcast(I32), in_=part.bitcast(I32))
+            for r in range(4):
+                part = scales[:, r:16:4, :].rearrange("a n c -> n a c")
+                nc.sync.dma_start(out=tile[r:P:32, :, :].bitcast(I32), in_=part.bitcast(I32))
 
         def place_gathered_scales(a):
-            for n in range(QUADRANTS):
-                part = v_rows[16 * a + 4 * n : 16 * a + 4 * n + 4, :]
-                nc.sync.dma_start(out=v_s[a][32 * n : 32 * n + 4, :].bitcast(I32), in_=part.bitcast(I32))
+            for r in range(4):
+                part = v_rows[16 * a + r : 16 * a + 16 : 4, :]
+                nc.sync.dma_start(out=v_s[a][r:P:32, :].bitcast(I32), in_=part.bitcast(I32))
 
         def differences(n, first, width, outs, scratch):
             cols = [slice((first + e * width) // STRIPE, (first + (e + 1) * width) // STRIPE) for e in range(2)]
@@ -123,33 +124,35 @@ def tile_list_frost_risk_map_kernel(
             outs = [x1[h][:, n - PACK, e * QUARTER : (e + 1) * QUARTER] for e in range(2)]
             differences(n, h * HALF, QUARTER, outs, scratch)
 
-        def quantise_x(x_f32, x_w, x_s, name, tag=""):
+        def round_x(x_f32, name, tag="", on_vector=False):
             x_bf = held(name, [P, PACK * x_f32.shape[2]], BF16, tag=tag)
-            nc.scalar.activation(
-                out=x_bf[:].rearrange("p (c e i) -> p c i e", e=RUN, i=PACK),
-                in_=x_f32[:].rearrange("p i (c e) -> p c i e", e=RUN),
-                func=ACT.Copy,
-            )
-            nc.vector.quantize_mx(out=x_w[:].bitcast(FP8X4), scales=x_s[:], in_=x_bf[:])
+            dst = x_bf[:].rearrange("p (c e i) -> p c i e", e=RUN, i=PACK)
+            src = x_f32[:].rearrange("p i (c e) -> p c i e", e=RUN)
+            if on_vector:
+                nc.vector.tensor_copy(out=dst, in_=src)
+            else:
+                nc.scalar.activation(out=dst, in_=src, func=ACT.Copy)
+            return x_bf
 
-        def round_w1(a, g):
-            w1_bf = held(f"w1_bf{a}{g}", [P, PACK * KP], BF16)
+        def quantise(bf, words, scales):
+            nc.vector.quantize_mx(out=words.bitcast(FP8X4), scales=scales, in_=bf)
+
+        def round_w1(a, g, m0, m1):
             part = w1_pass0[:, :, g * KP : (g + 1) * KP] if a == 0 else w1_pass1[g][:]
             nc.scalar.activation(
-                out=w1_bf[:].rearrange("p (t m i) -> p m i t", t=PACK, i=PACK),
-                in_=part.rearrange("p i (m t) -> p m i t", t=PACK),
+                out=w1_bf[a, g][:].rearrange("p (t m i) -> p m i t", t=PACK, i=PACK)[:, m0:m1, :, :],
+                in_=part.rearrange("p i (m t) -> p m i t", t=PACK)[:, m0:m1, :, :],
                 func=ACT.Copy,
             )
-            return w1_bf
 
-        def quantise_w1(a, g, w1_bf):
-            nc.vector.quantize_mx(out=w1_w[a, g][:].bitcast(FP8X4), scales=w1_s[a, g][:], in_=w1_bf[:])
+        def quantise_w1(a, g):
+            quantise(w1_bf[a, g][:], w1_w[a, g][:], w1_s[a, g][:])
 
         def gather_words(a):
             nc.vector.tensor_copy(out=v_w[a][:], in_=tab_w[a][:].bitcast(U32).indirect(idx[:]))
 
         def hardiness_transposed(q, g):
-            sums = bank(PASSES * q + g, [P, KP])
+            sums = bank(4 * g + q, [P, KP])
             for a in range(PASSES):
                 nc.tensor.matmul_mx(
                     out=sums[:],
@@ -160,79 +163,89 @@ def tile_list_frost_risk_map_kernel(
                     start=(a == 0),
                     stop=(a == PASSES - 1),
                 )
-            nc.scalar.activation(out=m_t[q][:, g, :, :], in_=sums[:].rearrange("p (m t) -> p t m", t=PACK), func=ACT.Copy)
+            nc.scalar.activation(out=m_t[q, g][:], in_=sums[:].rearrange("p (m t) -> p t m", t=PACK), func=ACT.Copy)
 
         def hardiness(q, g, number):
             m = bank(number, [P, PACK, P])
             for t in range(PACK):
-                nc.tensor.transpose(m[:, t, :], m_t[q][:, g, t, :], ident[:])
+                nc.tensor.transpose(m[:, t, :], m_t[q, g][:, t, :], ident[:])
             return m
 
-        def quadratic_terms(h):
-            x_w = [x0_w[:, h * HALF : (h + 1) * HALF], x1_w[h][:]]
-            x_s = [x0_s[:, h * HALF : (h + 1) * HALF], x1_s[h][:]]
-            for g in range(PASSES):
-                for pair in range(2):
-                    d = bank(2 * g + pair, [P, 2, HALF])
-                    inner = held(f"inner{g}{pair}", [P, 2, HALF], F32)
-                    for e in range(2):
-                        t = 2 * pair + e
-                        for a in range(PASSES):
-                            nc.tensor.matmul_mx(
-                                out=d[:, e, :],
-                                lhsT=w1_w[a, g][:, t * P : (t + 1) * P].bitcast(FP8X4),
-                                lhsT_scale=w1_s[a, g][:, t * P : (t + 1) * P],
-                                rhs=x_w[a].bitcast(FP8X4),
-                                rhs_scale=x_s[a],
-                                start=(a == 0),
-                                stop=(a == PASSES - 1),
-                            )
-                    for e in range(2):
-                        t = 2 * pair + e
-                        nc.scalar.activation(
-                            out=inner[:, e, :],
-                            in_=d[:, e, :],
-                            func=ACT.Identity,
-                            scale=c2_sb[:, g, t : t + 1],
-                            bias=c1_sb[:, g, t : t + 1],
-                        )
-                    nc.vector.tensor_tensor(
-                        out=quad[h, g][:, 2 * pair : 2 * pair + 2, :], in0=d[:], in1=inner[:], op=ALU.mult
-                    )
+        def response(d, g, t, cols):
+            for a, (x_w, x_s) in enumerate(((x0_w, x0_s), (x1_w, x1_s))):
+                nc.tensor.matmul_mx(
+                    out=d,
+                    lhsT=w1_w[a, g][:, t * P : (t + 1) * P].bitcast(FP8X4),
+                    lhsT_scale=w1_s[a, g][:, t * P : (t + 1) * P],
+                    rhs=x_w[:, cols].bitcast(FP8X4),
+                    rhs_scale=x_s[:, cols],
+                    start=(a == 0),
+                    stop=(a == PASSES - 1),
+                )
+
+        def inner_step(inner, d, g, t):
+            nc.scalar.activation(
+                out=inner, in_=d, func=ACT.Identity, scale=c2_sb[:, g, t : t + 1], bias=c1_sb[:, g, t : t + 1]
+            )
+
+        def inner_pair(g, h, pair, number):
+            d = bank(number, [P, 2, HALF])
+            inner = held(f"inner{g}{h}{pair}", [P, 2, HALF], F32)
+            for e in range(2):
+                response(d[:, e, :], g, 2 * pair + e, slice(h * HALF, (h + 1) * HALF))
+            for e in range(2):
+                inner_step(inner[:, e, :], d[:, e, :], g, 2 * pair + e)
+            return d, inner
+
+        def outer_pair(g, h, pair, d, inner, cols=slice(0, HALF)):
+            nc.vector.tensor_tensor(
+                out=quad[g, h][:, 2 * pair : 2 * pair + 2, cols], in0=d[:, :, cols], in1=inner[:, :, cols], op=ALU.mult
+            )
+
+        def quadratic_half(g, h, numbers):
+            for pair in range(2):
+                outer_pair(g, h, pair, *inner_pair(g, h, pair, numbers[pair]))
 
         def add_hardiness(q, g, m):
-            j0 = (q % 2) * QUARTER
+            terms = quad[g, q // 2][:, :, (q % 2) * QUARTER : (q % 2 + 1) * QUARTER]
             nc.vector.tensor_tensor(
-                out=h_bf[q][:, g, :].rearrange("p (c e t) -> p c t e", e=RUN, t=PACK),
+                out=h_bf[g][:, q * KP : (q + 1) * KP].rearrange("p (c e t) -> p c t e", e=RUN, t=PACK),
                 in0=m[:].rearrange("p t (c e) -> p c t e", e=RUN),
-                in1=quad[q // 2, g][:, :, j0 : j0 + QUARTER].rearrange("p t (c e) -> p c t e", e=RUN),
+                in1=terms.rearrange("p t (c e) -> p c t e", e=RUN),
                 op=ALU.add,
             )
 
-        def last_product(y, q, n, g):
+        def quantise_h(g, q0, q1):
+            quantise(h_bf[g][:, q0 * KP : q1 * KP], h_w[g][:, q0 * P : q1 * P], h_s[g][:, q0 * P : q1 * P])
+
+        def last_product(y, cols, n, g):
             nc.tensor.matmul_mx(
                 out=y,
                 lhsT=w3_w[:, g, n * P : (n + 1) * P].bitcast(FP8X4),
                 lhsT_scale=w3_s[:, g, n * P : (n + 1) * P],
-                rhs=h_w[q][:, g, :].bitcast(FP8X4),
-                rhs_scale=h_s[q][:, g, :],
+                rhs=h_w[g][:, cols].bitcast(FP8X4),
+                rhs_scale=h_s[g][:, cols],
                 start=(g == 0),
                 stop=(g == PASSES - 1),
             )
 
         def damage_indices(q, number):
-            nc.vector.quantize_mx(
-                out=h_w[q][:].rearrange("p g c -> p (g c)").bitcast(FP8X4),
-                scales=h_s[q][:].rearrange("p g c -> p (g c)"),
-                in_=h_bf[q][:].rearrange("p g c -> p (g c)"),
-            )
             y = bank(number, [P, N_TILES, P])
             for n in range(N_TILES):
                 for g in range(PASSES):
-                    last_product(y[:, n, :], q, n, g)
+                    last_product(y[:, n, :], slice(q * P, (q + 1) * P), n, g)
             for n in range(N_TILES):
                 nc.scalar.activation(out=y_sb[q][:, n, :], in_=y[:, n, :], func=ACT.Identity, bias=b_sb[:, n : n + 1])
             nc.sync.dma_start(out=out[:, q * P : (q + 1) * P].rearrange("(n p) j -> p n j", p=P), in_=y_sb[q][:])
+
+        def damage_indices_half(numbers):
+            ys = [bank(numbers[0], [P, 2, HALF]), bank(numbers[1], [P, 1, HALF])]
+            for n in range(N_TILES):
+                for g in range(PASSES):
+                    last_product(ys[n // 2][:, n % 2, :], slice(0, HALF), n, g)
+            for n in range(N_TILES):
+                nc.scalar.activation(out=y_half[:, n, :], in_=ys[n // 2][:, n % 2, :], func=ACT.Identity, bias=b_sb[:, n : n + 1])
+            nc.sync.dma_start(out=out[:, 0:HALF].rearrange("(n p) j -> p n j", p=P), in_=y_half[:])
 
         nc.sync.dma_start(out=tab_s[0:32, :].bitcast(I32), in_=tab_scales.rearrange("a n t -> (a n) t").bitcast(I32))
         nc.sync.dma_start(idx[:], offs)
@@ -263,55 +276,71 @@ def tile_list_frost_risk_map_kernel(
 
         for n in range(PACK):
             all_columns(n)
-        w1_bf_0 = [round_w1(0, g) for g in range(PASSES)]
+        for g in range(PASSES):
+            round_w1(0, g, 0, P)
         for a in range(PASSES):
             gather_words(a)
-            quantise_w1(0, a, w1_bf_0[a])
+            quantise_w1(0, a)
         all_columns(4)
-        quantise_x(x0, x0_w, x0_s, "x0_bf", tag="w1_pass0")
-        w1_bf_10 = round_w1(1, 0)
-        for q in range(4):
-            for g in range(PASSES):
+        quantise(round_x(x0, "x0_bf", tag="w1_pass0")[:], x0_w[:], x0_s[:])
+        round_w1(1, 0, 0, P)
+        for g in range(PASSES):
+            for q in range(4):
                 hardiness_transposed(q, g)
+        m = {(q, 0): hardiness(q, 0, q) for q in range(4)}
 
         all_columns(5)
         quarters = [lower[e][:, 0:QUARTER] for e in range(2)]
         half_of_columns(6, 0, quarters)
         half_of_columns(7, 0, quarters)
-        half_of_columns(6, 1, quarters)
-        quantise_w1(1, 0, w1_bf_10)
-        quantise_x(x1[0], x1_w[0], x1_s[0], "x1_bf0")
-        w1_bf_11 = round_w1(1, 1)
-        last_lower = held("last_lower", [P, 2, QUARTER], F32, tag="x1_bf0")
-        half_of_columns(7, 1, [last_lower[:, e, :] for e in range(2)])
-        quantise_w1(1, 1, w1_bf_11)
+        quantise_w1(1, 0)
+        x1_bf0 = round_x(x1[0], "x1_bf")
+        second = slice(HALF // STRIPE, S // STRIPE)
+        for e in range(2):
+            nc.vector.tensor_copy(out=lower[e][:], in_=rows[6 + e][:].indirect(idx3[:, second]))
+        for e in range(2):
+            nc.vector.tensor_tensor(
+                out=x1[1][:, 2 + e, :], in0=rows[6 + e][:].indirect(idx2[:, second]), in1=lower[e][:], op=ALU.subtract
+            )
+        quantise(x1_bf0[:], x1_w[:, 0:HALF], x1_s[:, 0:HALF])
+        x1_bf1 = round_x(x1[1], "x1_bf1", tag="x1_bf", on_vector=True)
+        quantise(x1_bf1[:], x1_w[:, HALF:S], x1_s[:, HALF:S])
 
-        m = {(q, g): hardiness(q, g, 4 + PASSES * q + g) for q in range(2) for g in range(PASSES)}
-        quadratic_terms(0)
-        quantise_x(x1[1], x1_w[1], x1_s[1], "x1_bf1")
-
+        round_w1(1, 1, 0, P // 2)
+        quadratic_half(0, 0, (4, 5))
+        round_w1(1, 1, P // 2, P)
         add_hardiness(0, 0, m[0, 0])
         add_hardiness(1, 0, m[1, 0])
+        quantise_w1(1, 1)
+        quadratic_half(0, 1, (6, 7))
+        add_hardiness(2, 0, m[2, 0])
+        add_hardiness(3, 0, m[3, 0])
+        quadratic_half(1, 0, (4, 5))
+        quantise_h(0, 0, 4)
+        pairs = [inner_pair(1, 1, pair, pair) for pair in range(2)]
+        for q, number in enumerate((6, 7, 2, 3)):
+            m[q, 1] = hardiness(q, 1, number)
         add_hardiness(0, 1, m[0, 1])
         add_hardiness(1, 1, m[1, 1])
-        damage_indices(0, 5)
-        damage_indices(1, 7)
-        quadratic_terms(1)
-        for q, g, number in ((2, 0, 4), (3, 0, 6), (2, 1, 0), (3, 1, 1)):
-            m[q, g] = hardiness(q, g, number)
-        add_hardiness(2, 0, m[2, 0])
+        first, final = slice(0, QUARTER), slice(QUARTER, HALF)
+        outer_pair(1, 1, 0, *pairs[0], first)
+        quantise_h(1, 0, 2)
+        outer_pair(1, 1, 1, *pairs[1], first)
+        damage_indices_half((4, 5))
+        outer_pair(1, 1, 0, *pairs[0], final)
         add_hardiness(2, 1, m[2, 1])
-        add_hardiness(3, 0, m[3, 0])
-        damage_indices(2, 4)
+        outer_pair(1, 1, 1, *pairs[1], final)
+        quantise_h(1, 2, 3)
+        add_hardiness(3, 1, m[3, 1])
+        damage_indices(2, 6)
 
         last = 3
-        ys = [bank(number, [P, P]) for number in (2, 3, 5)]
+        ys = [bank(number, [P, P]) for number in (7, 0, 1)]
         for g in range(PASSES):
             if g == 1:
-                add_hardiness(last, g, m[last, g])
-            nc.vector.quantize_mx(out=h_w[last][:, g, :].bitcast(FP8X4), scales=h_s[last][:, g, :], in_=h_bf[last][:, g, :])
+                quantise_h(1, last, last + 1)
             for n in range(N_TILES):
-                last_product(ys[n][:], last, n, g)
+                last_product(ys[n][:], slice(last * P, S), n, g)
         nc.vector.tensor_scalar_add(out=y_sb[last][:, 0, :], in0=ys[0][:], scalar1=b_sb[:, 0:1])
         nc.scalar.activation(out=y_sb[last][:, 1, :], in_=ys[1][:], func=ACT.Identity, bias=b_sb[:, 1:2])
         nc.vector.tensor_scalar_add(out=y_sb[last][:, 2, :], in0=ys[2][:], scalar1=b_sb[:, 2:3])

@@ -74,7 +74,7 @@ def tile_list_frost_risk_map_kernel(
         x0_w, x0_s = held("x0_w", [P, S], U32), held("x0_s", [P, S], U8)
         x1_w, x1_s = held("x1_w", [P, S], U32), held("x1_s", [P, S], U8)
         m_t = {(q, g): held(f"m_t{q}{g}", [P, PACK, P], F32) for q in range(4) for g in range(PASSES)}
-        quad = {(g, h): held(f"quad{g}{h}", [P, PACK, HALF], F32) for g in range(PASSES) for h in range(2)}
+        quad = {(g, h): held(f"quad{g}{h}", [P, 2, HALF, 2], F32) for g in range(PASSES) for h in range(2)}
         h_bf = [held(f"h_bf{g}", [P, PACK * S], BF16) for g in range(PASSES)]
         h_w = [held(f"h_w{g}", [P, S], U32) for g in range(PASSES)]
         h_s = [held(f"h_s{g}", [P, S], U8) for g in range(PASSES)]
@@ -129,7 +129,7 @@ def tile_list_frost_risk_map_kernel(
             dst = x_bf[:].rearrange("p (c e i) -> p c i e", e=RUN, i=PACK)
             src = x_f32[:].rearrange("p i (c e) -> p c i e", e=RUN)
             if on_vector:
-                nc.vector.tensor_copy(out=dst, in_=src)
+                nc.vector.tensor_copy(out=x_bf[:].rearrange("p (c i) -> p c i", i=PACK), in_=x_f32[:].rearrange("p i c -> p c i"))
             else:
                 nc.scalar.activation(out=dst, in_=src, func=ACT.Copy)
             return x_bf
@@ -199,7 +199,10 @@ def tile_list_frost_risk_map_kernel(
 
         def outer_pair(g, h, pair, d, inner, cols=slice(0, HALF)):
             nc.vector.tensor_tensor(
-                out=quad[g, h][:, 2 * pair : 2 * pair + 2, cols], in0=d[:, :, cols], in1=inner[:, :, cols], op=ALU.mult
+                out=quad[g, h][:, pair, cols, :],
+                in0=d[:, :, cols].rearrange("p e j -> p j e"),
+                in1=inner[:, :, cols].rearrange("p e j -> p j e"),
+                op=ALU.mult,
             )
 
         def quadratic_half(g, h, numbers):
@@ -207,11 +210,11 @@ def tile_list_frost_risk_map_kernel(
                 outer_pair(g, h, pair, *inner_pair(g, h, pair, numbers[pair]))
 
         def add_hardiness(q, g, m):
-            terms = quad[g, q // 2][:, :, (q % 2) * QUARTER : (q % 2 + 1) * QUARTER]
+            terms = quad[g, q // 2][:, :, (q % 2) * QUARTER : (q % 2 + 1) * QUARTER, :]
             nc.vector.tensor_tensor(
-                out=h_bf[g][:, q * KP : (q + 1) * KP].rearrange("p (c e t) -> p c t e", e=RUN, t=PACK),
-                in0=m[:].rearrange("p t (c e) -> p c t e", e=RUN),
-                in1=terms.rearrange("p t (c e) -> p c t e", e=RUN),
+                out=h_bf[g][:, q * KP : (q + 1) * KP].rearrange("p (j r e) -> p j r e", r=2, e=2),
+                in0=m[:].rearrange("p (r e) j -> p j r e", e=2),
+                in1=terms.rearrange("p r j e -> p j r e"),
                 op=ALU.add,
             )
 

@@ -63,21 +63,31 @@ def tile_list_frost_risk_map_kernel(
         c2_sb = held("c2_sb", [P, PASSES, PACK], F32)
         b_sb = held("b_sb", [P, N_TILES], F32)
         ident = held("ident", [P, P], F32)
-        w1_pass0 = held("w1_pass0", [P, PACK, H], F32)
-        w1_pass1 = [held(f"w1_pass1_{g}", [P, PACK, KP], F32) for g in range(PASSES)]
-        w1_w = {(a, g): held(f"w1_w{a}{g}", [P, KP], U32) for a in range(PASSES) for g in range(PASSES)}
-        w1_s = {(a, g): held(f"w1_s{a}{g}", [P, KP], U8) for a in range(PASSES) for g in range(PASSES)}
-        w1_bf = {(a, g): held(f"w1_bf{a}{g}", [P, PACK * KP], BF16) for a in range(PASSES) for g in range(PASSES)}
+        w1_f32 = {(a, g): held(f"w1_f32_{a}{g}", [P, PACK, KP], F32) for a in range(PASSES) for g in range(PASSES)}
+        scratch7 = held("scratch7", [P, QUARTER], F32, tag="w1_w10")
+        w1_w0, w1_s0 = held("w1_w0", [P, H], U32, tag="tab_w1"), held("w1_s0", [P, H], U8)
+        w1_w = {(0, g): w1_w0[:, g * KP : (g + 1) * KP] for g in range(PASSES)}
+        w1_s = {(0, g): w1_s0[:, g * KP : (g + 1) * KP] for g in range(PASSES)}
+        for g in range(PASSES):
+            w1_w[1, g] = held(f"w1_w1{g}", [P, KP], U32)[:]
+            w1_s[1, g] = held(f"w1_s1{g}", [P, KP], U8)[:]
+        w1_bf0 = held("w1_bf0", [P, PASSES * PACK * KP], BF16)
+        w1_bf = {(0, g): w1_bf0[:, g * PACK * KP : (g + 1) * PACK * KP] for g in range(PASSES)}
+        for g in range(PASSES):
+            w1_bf[1, g] = held(f"w1_bf1{g}", [P, PACK * KP], BF16)[:]
         lower = [held(f"lower{n}", [P, HALF], F32) for n in range(2)]
         x0 = held("x0", [P, PACK, S], F32)
         x1 = [held(f"x1_{h}", [P, PACK, HALF], F32) for h in range(2)]
+        scratch4 = held("scratch4", [P, HALF], F32, tag="x0_w")
         x0_w, x0_s = held("x0_w", [P, S], U32), held("x0_s", [P, S], U8)
         x1_w, x1_s = held("x1_w", [P, S], U32), held("x1_s", [P, S], U8)
-        m_t = {(q, g): held(f"m_t{q}{g}", [P, PACK, P], F32) for q in range(4) for g in range(PASSES)}
+        m_t0 = held("m_t0", [P, 4, PACK, P], F32)
+        m_t1 = held("m_t1", [P, 4, PACK, P], F32, tag="w1_f32_10")
+        m_t = {(q, g): (m_t0, m_t1)[g][:, q, :, :] for q in range(4) for g in range(PASSES)}
         quad = {(g, h): held(f"quad{g}{h}", [P, 2, HALF, 2], F32) for g in range(PASSES) for h in range(2)}
-        h_bf = [held(f"h_bf{g}", [P, PACK * S], BF16) for g in range(PASSES)]
-        h_w = [held(f"h_w{g}", [P, S], U32) for g in range(PASSES)]
-        h_s = [held(f"h_s{g}", [P, S], U8) for g in range(PASSES)]
+        h_bf = {(g, q): held(f"h_bf{g}{q}", [P, n * KP], BF16) for g in range(PASSES) for q, n in ((0, 2), (2, 2))}
+        h_w = {(g, h): held(f"h_w{g}{h}", [P, HALF], U32) for g, h in ((1, 0), (1, 1))}
+        h_s = {(g, h): held(f"h_s{g}{h}", [P, HALF], U8) for g in range(PASSES) for h in range(2)}
         y_half = held("y_half", [P, N_TILES, HALF], F32)
         y_sb = {q: held(f"y_sb{q}", [P, N_TILES, P], F32) for q in (2, 3)}
 
@@ -92,9 +102,9 @@ def tile_list_frost_risk_map_kernel(
         def load_table(a):
             nc.sync.dma_start(out=tab_w[a][:], in_=tab_words[a].rearrange("p t i -> p (t i)").bitcast(I32))
 
-        def load_w1_pass1(g):
-            part = w1[KP : 2 * KP, g * KP : (g + 1) * KP]
-            nc.sync.dma_start(out=w1_pass1[g][:], in_=part.rearrange("(p i) c -> p i c", i=PACK))
+        def load_w1(a, g):
+            part = w1[a * KP : (a + 1) * KP, g * KP : (g + 1) * KP]
+            nc.sync.dma_start(out=w1_f32[a, g][:], in_=part.rearrange("(p i) c -> p i c", i=PACK))
 
         def load_scales(tile, scales):
             for r in range(4):
@@ -118,7 +128,7 @@ def tile_list_frost_risk_map_kernel(
         def all_columns(n):
             a, i = divmod(n, PACK)
             outs = [x0[:, i, h * HALF : (h + 1) * HALF] if a == 0 else x1[h][:, i, :] for h in range(2)]
-            differences(n, 0, HALF, outs, [lower[e][:] for e in range(2)])
+            differences(n, 0, HALF, outs, [scratch4[:] if n == PACK else lower[0][:], lower[1][:]])
 
         def half_of_columns(n, h, scratch):
             outs = [x1[h][:, n - PACK, e * QUARTER : (e + 1) * QUARTER] for e in range(2)]
@@ -138,15 +148,15 @@ def tile_list_frost_risk_map_kernel(
             nc.vector.quantize_mx(out=words.bitcast(FP8X4), scales=scales, in_=bf)
 
         def round_w1(a, g, m0, m1):
-            part = w1_pass0[:, :, g * KP : (g + 1) * KP] if a == 0 else w1_pass1[g][:]
+            part = w1_f32[a, g][:]
             nc.scalar.activation(
-                out=w1_bf[a, g][:].rearrange("p (t m i) -> p m i t", t=PACK, i=PACK)[:, m0:m1, :, :],
+                out=w1_bf[a, g].rearrange("p (t m i) -> p m i t", t=PACK, i=PACK)[:, m0:m1, :, :],
                 in_=part.rearrange("p i (m t) -> p m i t", t=PACK)[:, m0:m1, :, :],
                 func=ACT.Copy,
             )
 
         def quantise_w1(a, g):
-            quantise(w1_bf[a, g][:], w1_w[a, g][:], w1_s[a, g][:])
+            quantise(w1_bf[a, g], w1_w[a, g], w1_s[a, g])
 
         def gather_words(a):
             nc.vector.tensor_copy(out=v_w[a][:], in_=tab_w[a][:].bitcast(U32).indirect(idx[:]))
@@ -163,7 +173,7 @@ def tile_list_frost_risk_map_kernel(
                     start=(a == 0),
                     stop=(a == PASSES - 1),
                 )
-            nc.scalar.activation(out=m_t[q, g][:], in_=sums[:].rearrange("p (m t) -> p t m", t=PACK), func=ACT.Copy)
+            nc.scalar.activation(out=m_t[q, g], in_=sums[:].rearrange("p (m t) -> p t m", t=PACK), func=ACT.Copy)
 
         def hardiness(q, g, number):
             m = bank(number, [P, PACK, P])
@@ -209,69 +219,82 @@ def tile_list_frost_risk_map_kernel(
             for pair in range(2):
                 outer_pair(g, h, pair, *inner_pair(g, h, pair, numbers[pair]))
 
+        def add_hardiness_sbuf(q, m_sb):
+            terms = quad[0, q // 2][:, :, (q % 2) * QUARTER : (q % 2 + 1) * QUARTER, :]
+            nc.gpsimd.tensor_tensor(
+                out=h_bf[0, q - q % 2][:, (q % 2) * KP : (q % 2 + 1) * KP].rearrange("p (j r e) -> p j r e", r=2, e=2),
+                in0=m_sb[:].rearrange("p j (r e) -> p j r e", e=2),
+                in1=terms.rearrange("p r j e -> p j r e"),
+                op=ALU.add,
+            )
+
+        def hardiness_in_sbuf(q):
+            m = hardiness(q, 0, q)
+            m_sb = held(f"m_sb{q}", [P, P, PACK], F32, tag=f"rows{q}")
+            nc.scalar.activation(out=m_sb[:], in_=m[:].rearrange("p t j -> p j t"), func=ACT.Copy)
+            return m_sb
+
         def add_hardiness(q, g, m):
             terms = quad[g, q // 2][:, :, (q % 2) * QUARTER : (q % 2 + 1) * QUARTER, :]
             nc.vector.tensor_tensor(
-                out=h_bf[g][:, q * KP : (q + 1) * KP].rearrange("p (j r e) -> p j r e", r=2, e=2),
+                out=h_bf[g, q - q % 2][:, (q % 2) * KP : (q % 2 + 1) * KP].rearrange("p (j r e) -> p j r e", r=2, e=2),
                 in0=m[:].rearrange("p (r e) j -> p j r e", e=2),
                 in1=terms.rearrange("p r j e -> p j r e"),
                 op=ALU.add,
             )
 
         def quantise_h(g, q0, q1):
-            quantise(h_bf[g][:, q0 * KP : q1 * KP], h_w[g][:, q0 * P : q1 * P], h_s[g][:, q0 * P : q1 * P])
+            h = q0 // 2
+            cols = slice(q0 * P - h * HALF, q1 * P - h * HALF)
+            quantise(h_bf[g, 2 * h][:, (q0 - 2 * h) * KP : (q1 - 2 * h) * KP], h_w[g, h][:, cols], h_s[g, h][:, cols])
 
-        def last_product(y, cols, n, g):
+        def last_product(y, cols, n, g, start, stop):
+            h = cols.start // HALF
+            within = slice(cols.start - h * HALF, cols.stop - h * HALF)
             nc.tensor.matmul_mx(
                 out=y,
                 lhsT=w3_w[:, g, n * P : (n + 1) * P].bitcast(FP8X4),
                 lhsT_scale=w3_s[:, g, n * P : (n + 1) * P],
-                rhs=h_w[g][:, cols].bitcast(FP8X4),
-                rhs_scale=h_s[g][:, cols],
-                start=(g == 0),
-                stop=(g == PASSES - 1),
+                rhs=h_w[g, h][:, within].bitcast(FP8X4),
+                rhs_scale=h_s[g, h][:, within],
+                start=start,
+                stop=stop,
             )
 
-        def damage_indices(q, number):
-            y = bank(number, [P, N_TILES, P])
-            for n in range(N_TILES):
-                for g in range(PASSES):
-                    last_product(y[:, n, :], slice(q * P, (q + 1) * P), n, g)
-            for n in range(N_TILES):
-                nc.scalar.activation(out=y_sb[q][:, n, :], in_=y[:, n, :], func=ACT.Identity, bias=b_sb[:, n : n + 1])
-            nc.sync.dma_start(out=out[:, q * P : (q + 1) * P].rearrange("(n p) j -> p n j", p=P), in_=y_sb[q][:])
+        def damage_pass(ys, cols, g):
+            for n, (y, first, final) in enumerate(ys):
+                last_product(y, cols, n, g, start=(g == 0 and first), stop=(g == 1 and final))
 
-        def damage_indices_half(numbers):
-            ys = [bank(numbers[0], [P, 2, HALF]), bank(numbers[1], [P, 1, HALF])]
-            for n in range(N_TILES):
-                for g in range(PASSES):
-                    last_product(ys[n // 2][:, n % 2, :], slice(0, HALF), n, g)
-            for n in range(N_TILES):
-                nc.scalar.activation(out=y_half[:, n, :], in_=ys[n // 2][:, n % 2, :], func=ACT.Identity, bias=b_sb[:, n : n + 1])
-            nc.sync.dma_start(out=out[:, 0:HALF].rearrange("(n p) j -> p n j", p=P), in_=y_half[:])
+        def add_bias_and_store(ys, y_out, cols):
+            for n, (y, first, final) in enumerate(ys):
+                nc.scalar.activation(out=y_out[:, n, :], in_=y, func=ACT.Identity, bias=b_sb[:, n : n + 1])
+            nc.sync.dma_start(out=out[:, cols].rearrange("(n p) j -> p n j", p=P), in_=y_out[:])
 
         nc.sync.dma_start(out=tab_s[0:32, :].bitcast(I32), in_=tab_scales.rearrange("a n t -> (a n) t").bitcast(I32))
         nc.sync.dma_start(idx[:], offs)
         load_rows(0)
         nc.sync.dma_start(idx3[:], offs3)
         nc.sync.dma_start(idx2[:], offs2)
-        for n in range(1, PACK):
-            load_rows(n)
-        nc.sync.dma_start(out=w1_pass0[:], in_=w1[0:KP, :].rearrange("(p i) c -> p i c", i=PACK))
-        nc.vector.tensor_copy(out=v_rows[:], in_=tab_s[:].indirect(idx[:]))
-        for a in range(PASSES):
-            load_table(a)
-            place_gathered_scales(a)
-        load_rows(4)
-        nc.sync.dma_start(out=w2_w[:].bitcast(I32), in_=w2_words.rearrange("a p c -> p a c").bitcast(I32))
+        load_rows(1)
+        load_w1(0, 0)
+        load_rows(2)
         load_scales(w2_s, w2_scales)
-        load_rows(5)
-        load_w1_pass1(0)
-        load_rows(6)
-        load_rows(7)
-        load_w1_pass1(1)
+        load_w1(0, 1)
+        load_rows(3)
+        nc.vector.tensor_copy(out=v_rows[:], in_=tab_s[:].indirect(idx[:]))
+        place_gathered_scales(0)
+        load_table(0)
         nc.sync.dma_start(out=c1_sb[:], in_=c1.rearrange("(g p t) -> p g t", g=PASSES, t=PACK))
         nc.sync.dma_start(out=c2_sb[:], in_=c2.rearrange("(g p t) -> p g t", g=PASSES, t=PACK))
+        place_gathered_scales(1)
+        load_table(1)
+        nc.sync.dma_start(out=w2_w[:].bitcast(I32), in_=w2_words.rearrange("a p c -> p a c").bitcast(I32))
+        load_rows(4)
+        load_rows(5)
+        load_w1(1, 0)
+        load_rows(6)
+        load_rows(7)
+        load_w1(1, 1)
         nc.sync.dma_start(out=w3_w[:], in_=w3_words.rearrange("a p c i -> p a (c i)").bitcast(I32))
         load_scales(w3_s, w3_scales)
         with nc.allow_non_contiguous_dma(reason="one bias value to a partition"):
@@ -283,19 +306,21 @@ def tile_list_frost_risk_map_kernel(
             round_w1(0, g, 0, P)
         for a in range(PASSES):
             gather_words(a)
-            quantise_w1(0, a)
+        quantise(w1_bf0[:], w1_w0[:], w1_s0[:])
         all_columns(4)
-        quantise(round_x(x0, "x0_bf", tag="w1_pass0")[:], x0_w[:], x0_s[:])
+        quantise(round_x(x0, "x0_bf")[:], x0_w[:], x0_s[:])
         round_w1(1, 0, 0, P)
         for g in range(PASSES):
             for q in range(4):
                 hardiness_transposed(q, g)
-        m = {(q, 0): hardiness(q, 0, q) for q in range(4)}
+        m = {(q, 0): hardiness_in_sbuf(q) for q in range(4)}
+        for q in range(4):
+            m[q, 1] = hardiness(q, 1, q)
 
         all_columns(5)
         quarters = [lower[e][:, 0:QUARTER] for e in range(2)]
         half_of_columns(6, 0, quarters)
-        half_of_columns(7, 0, quarters)
+        half_of_columns(7, 0, [quarters[0], scratch7[:]])
         quantise_w1(1, 0)
         x1_bf0 = round_x(x1[0], "x1_bf")
         second = slice(HALF // STRIPE, S // STRIPE)
@@ -309,41 +334,47 @@ def tile_list_frost_risk_map_kernel(
         x1_bf1 = round_x(x1[1], "x1_bf1", tag="x1_bf", on_vector=True)
         quantise(x1_bf1[:], x1_w[:, HALF:S], x1_s[:, HALF:S])
 
-        round_w1(1, 1, 0, P // 2)
-        quadratic_half(0, 0, (4, 5))
-        round_w1(1, 1, P // 2, P)
-        add_hardiness(0, 0, m[0, 0])
-        add_hardiness(1, 0, m[1, 0])
+        round_w1(1, 1, 0, P)
         quantise_w1(1, 1)
+        quadratic_half(0, 0, (4, 5))
+        add_hardiness_sbuf(0, m[0, 0])
+        add_hardiness_sbuf(1, m[1, 0])
         quadratic_half(0, 1, (6, 7))
-        add_hardiness(2, 0, m[2, 0])
-        add_hardiness(3, 0, m[3, 0])
+        add_hardiness_sbuf(2, m[2, 0])
+        add_hardiness_sbuf(3, m[3, 0])
         quadratic_half(1, 0, (4, 5))
-        quantise_h(0, 0, 4)
-        pairs = [inner_pair(1, 1, pair, pair) for pair in range(2)]
-        for q, number in enumerate((6, 7, 2, 3)):
-            m[q, 1] = hardiness(q, 1, number)
+        pairs = [inner_pair(1, 1, pair, 6 + pair) for pair in range(2)]
+        two, one = bank(4, [P, 2, HALF]), bank(5, [P, HALF])
+        ys_half = [(two[:, 0, :], True, False), (two[:, 1, :], False, True), (one[:], True, True)]
         add_hardiness(0, 1, m[0, 1])
         add_hardiness(1, 1, m[1, 1])
         first, final = slice(0, QUARTER), slice(QUARTER, HALF)
         outer_pair(1, 1, 0, *pairs[0], first)
+        h_w[0, 0] = held("h_w00", [P, HALF], U32, tag="quad10")
+        quantise_h(0, 0, 2)
+        damage_pass(ys_half, slice(0, HALF), 0)
         quantise_h(1, 0, 2)
         outer_pair(1, 1, 1, *pairs[1], first)
-        damage_indices_half((4, 5))
+        damage_pass(ys_half, slice(0, HALF), 1)
+        add_bias_and_store(ys_half, y_half, slice(0, HALF))
         outer_pair(1, 1, 0, *pairs[0], final)
         add_hardiness(2, 1, m[2, 1])
+        h_w[0, 1] = held("h_w01", [P, HALF], U32, tag="inner110")
+        quantise_h(0, 2, 4)
+        three = bank(0, [P, N_TILES, P])
+        ys_third = [(three[:, n, :], n == 0, n == N_TILES - 1) for n in range(N_TILES)]
+        damage_pass(ys_third, slice(HALF, HALF + QUARTER), 0)
+        last = 3
+        ys = [bank(number, [P, P]) for number in (1, 2, 6)]
+        ys_last = [(y[:], True, True) for y in ys]
+        damage_pass(ys_last, slice(last * P, S), 0)
         outer_pair(1, 1, 1, *pairs[1], final)
         quantise_h(1, 2, 3)
         add_hardiness(3, 1, m[3, 1])
-        damage_indices(2, 6)
-
-        last = 3
-        ys = [bank(number, [P, P]) for number in (7, 0, 1)]
-        for g in range(PASSES):
-            if g == 1:
-                quantise_h(1, last, last + 1)
-            for n in range(N_TILES):
-                last_product(ys[n][:], slice(last * P, S), n, g)
+        damage_pass(ys_third, slice(HALF, HALF + QUARTER), 1)
+        add_bias_and_store(ys_third, y_sb[2], slice(HALF, HALF + QUARTER))
+        quantise_h(1, last, last + 1)
+        damage_pass(ys_last, slice(last * P, S), 1)
         nc.vector.tensor_scalar_add(out=y_sb[last][:, 0, :], in0=ys[0][:], scalar1=b_sb[:, 0:1])
         nc.scalar.activation(out=y_sb[last][:, 1, :], in_=ys[1][:], func=ACT.Identity, bias=b_sb[:, 1:2])
         nc.vector.tensor_scalar_add(out=y_sb[last][:, 2, :], in0=ys[2][:], scalar1=b_sb[:, 2:3])

@@ -63,9 +63,12 @@ def tile_list_frost_risk_map_kernel(
         c2_sb = held("c2_sb", [P, PASSES, PACK], F32)
         b_sb = held("b_sb", [P, N_TILES], F32)
         ident = held("ident", [P, P], F32)
-        w1_f32 = {(a, g): held(f"w1_f32_{a}{g}", [P, PACK, KP], F32) for a in range(PASSES) for g in range(PASSES)}
-        scratch7 = held("scratch7", [P, QUARTER], F32, tag="w1_w10")
-        w1_w0, w1_s0 = held("w1_w0", [P, H], U32, tag="tab_w1"), held("w1_s0", [P, H], U8)
+        w1_pass0 = held("w1_pass0", [P, PACK, H], F32)
+        w1_f32 = {(0, g): w1_pass0[:, :, g * KP : (g + 1) * KP] for g in range(PASSES)}
+        for g in range(PASSES):
+            w1_f32[1, g] = held(f"w1_f32_1{g}", [P, PACK, KP], F32)[:]
+        scratch7 = held("scratch7", [P, HALF], F32, tag="w1_w10")
+        w1_w0, w1_s0 = held("w1_w0", [P, H], U32), held("w1_s0", [P, H], U8)
         w1_w = {(0, g): w1_w0[:, g * KP : (g + 1) * KP] for g in range(PASSES)}
         w1_s = {(0, g): w1_s0[:, g * KP : (g + 1) * KP] for g in range(PASSES)}
         for g in range(PASSES):
@@ -75,10 +78,9 @@ def tile_list_frost_risk_map_kernel(
         w1_bf = {(0, g): w1_bf0[:, g * PACK * KP : (g + 1) * PACK * KP] for g in range(PASSES)}
         for g in range(PASSES):
             w1_bf[1, g] = held(f"w1_bf1{g}", [P, PACK * KP], BF16)[:]
-        lower = [held(f"lower{n}", [P, HALF], F32) for n in range(2)]
+        lower = [held(f"lower{n}", [P, S], F32) for n in range(2)]
         x0 = held("x0", [P, PACK, S], F32)
         x1 = [held(f"x1_{h}", [P, PACK, HALF], F32) for h in range(2)]
-        scratch4 = held("scratch4", [P, HALF], F32, tag="x0_w")
         x0_w, x0_s = held("x0_w", [P, S], U32), held("x0_s", [P, S], U8)
         x1_w, x1_s = held("x1_w", [P, S], U32), held("x1_s", [P, S], U8)
         m_t0 = held("m_t0", [P, 4, PACK, P], F32)
@@ -86,7 +88,7 @@ def tile_list_frost_risk_map_kernel(
         m_t = {(q, g): (m_t0, m_t1)[g][:, q, :, :] for q in range(4) for g in range(PASSES)}
         quad = {(g, h): held(f"quad{g}{h}", [P, 2, HALF, 2], F32) for g in range(PASSES) for h in range(2)}
         h_bf = {(g, q): held(f"h_bf{g}{q}", [P, n * KP], BF16) for g in range(PASSES) for q, n in ((0, 2), (2, 2))}
-        h_w = {(g, h): held(f"h_w{g}{h}", [P, HALF], U32) for g, h in ((1, 0), (1, 1))}
+        h_w = {(g, h): held(f"h_w{g}{h}", [P, HALF], U32) for g in range(PASSES) for h in range(2)}
         h_s = {(g, h): held(f"h_s{g}{h}", [P, HALF], U8) for g in range(PASSES) for h in range(2)}
         y_half = held("y_half", [P, N_TILES, HALF], F32)
         y_sb = {q: held(f"y_sb{q}", [P, N_TILES, P], F32) for q in (2, 3)}
@@ -95,16 +97,21 @@ def tile_list_frost_risk_map_kernel(
             nc.vector.memset(part.bitcast(I32), 0)
         make_identity(nc, ident[:])
 
-        def load_rows(n):
+        def load_rows(n, cols=slice(0, T2)):
             a, i = divmod(n, PACK)
-            nc.sync.dma_start(out=rows[n][:], in_=xT[a * KP : (a + 1) * KP, :].rearrange("(p i) t -> p i t", i=PACK)[:, i, :])
+            nc.sync.dma_start(out=rows[n][:, cols], in_=xT[a * KP : (a + 1) * KP, :].rearrange("(p i) t -> p i t", i=PACK)[:, i, cols])
+
+        def load_pair(n):
+            load_rows(n, slice(0, T2 - P))
+            load_rows(n + 1)
+            load_rows(n, slice(T2 - P, T2))
 
         def load_table(a):
             nc.sync.dma_start(out=tab_w[a][:], in_=tab_words[a].rearrange("p t i -> p (t i)").bitcast(I32))
 
         def load_w1(a, g):
             part = w1[a * KP : (a + 1) * KP, g * KP : (g + 1) * KP]
-            nc.sync.dma_start(out=w1_f32[a, g][:], in_=part.rearrange("(p i) c -> p i c", i=PACK))
+            nc.sync.dma_start(out=w1_f32[a, g], in_=part.rearrange("(p i) c -> p i c", i=PACK))
 
         def load_scales(tile, scales):
             for r in range(4):
@@ -128,11 +135,16 @@ def tile_list_frost_risk_map_kernel(
         def all_columns(n):
             a, i = divmod(n, PACK)
             outs = [x0[:, i, h * HALF : (h + 1) * HALF] if a == 0 else x1[h][:, i, :] for h in range(2)]
-            differences(n, 0, HALF, outs, [scratch4[:] if n == PACK else lower[0][:], lower[1][:]])
+            differences(n, 0, HALF, outs, [lower[e][:, 0:HALF] for e in range(2)])
 
-        def half_of_columns(n, h, scratch):
-            outs = [x1[h][:, n - PACK, e * QUARTER : (e + 1) * QUARTER] for e in range(2)]
-            differences(n, h * HALF, QUARTER, outs, scratch)
+        def pair_of_tiles(n, first, width, outs, scratch):
+            cols = slice(first // STRIPE, (first + width) // STRIPE)
+            for e in (1, 0):
+                nc.vector.tensor_copy(out=scratch[e], in_=rows[n + e][:].indirect(idx3[:, cols]))
+            for e in (1, 0):
+                nc.vector.tensor_tensor(
+                    out=outs[e], in0=rows[n + e][:].indirect(idx2[:, cols]), in1=scratch[e], op=ALU.subtract
+                )
 
         def round_x(x_f32, name, tag="", on_vector=False):
             x_bf = held(name, [P, PACK * x_f32.shape[2]], BF16, tag=tag)
@@ -148,7 +160,7 @@ def tile_list_frost_risk_map_kernel(
             nc.vector.quantize_mx(out=words.bitcast(FP8X4), scales=scales, in_=bf)
 
         def round_w1(a, g, m0, m1):
-            part = w1_f32[a, g][:]
+            part = w1_f32[a, g]
             nc.scalar.activation(
                 out=w1_bf[a, g].rearrange("p (t m i) -> p m i t", t=PACK, i=PACK)[:, m0:m1, :, :],
                 in_=part.rearrange("p i (m t) -> p m i t", t=PACK)[:, m0:m1, :, :],
@@ -219,21 +231,6 @@ def tile_list_frost_risk_map_kernel(
             for pair in range(2):
                 outer_pair(g, h, pair, *inner_pair(g, h, pair, numbers[pair]))
 
-        def add_hardiness_sbuf(q, m_sb):
-            terms = quad[0, q // 2][:, :, (q % 2) * QUARTER : (q % 2 + 1) * QUARTER, :]
-            nc.gpsimd.tensor_tensor(
-                out=h_bf[0, q - q % 2][:, (q % 2) * KP : (q % 2 + 1) * KP].rearrange("p (j r e) -> p j r e", r=2, e=2),
-                in0=m_sb[:].rearrange("p j (r e) -> p j r e", e=2),
-                in1=terms.rearrange("p r j e -> p j r e"),
-                op=ALU.add,
-            )
-
-        def hardiness_in_sbuf(q):
-            m = hardiness(q, 0, q)
-            m_sb = held(f"m_sb{q}", [P, P, PACK], F32, tag=f"rows{q}")
-            nc.scalar.activation(out=m_sb[:], in_=m[:].rearrange("p t j -> p j t"), func=ACT.Copy)
-            return m_sb
-
         def add_hardiness(q, g, m):
             terms = quad[g, q // 2][:, :, (q % 2) * QUARTER : (q % 2 + 1) * QUARTER, :]
             nc.vector.tensor_tensor(
@@ -276,60 +273,47 @@ def tile_list_frost_risk_map_kernel(
         nc.sync.dma_start(idx3[:], offs3)
         nc.sync.dma_start(idx2[:], offs2)
         load_rows(1)
-        load_w1(0, 0)
-        load_rows(2)
-        load_scales(w2_s, w2_scales)
-        load_w1(0, 1)
-        load_rows(3)
+        load_pair(2)
+        nc.sync.dma_start(out=w1_pass0[:], in_=w1[0:KP, :].rearrange("(p i) c -> p i c", i=PACK))
         nc.vector.tensor_copy(out=v_rows[:], in_=tab_s[:].indirect(idx[:]))
-        place_gathered_scales(0)
-        load_table(0)
-        nc.sync.dma_start(out=c1_sb[:], in_=c1.rearrange("(g p t) -> p g t", g=PASSES, t=PACK))
-        nc.sync.dma_start(out=c2_sb[:], in_=c2.rearrange("(g p t) -> p g t", g=PASSES, t=PACK))
-        place_gathered_scales(1)
-        load_table(1)
-        nc.sync.dma_start(out=w2_w[:].bitcast(I32), in_=w2_words.rearrange("a p c -> p a c").bitcast(I32))
+        for a in range(PASSES):
+            load_table(a)
+            place_gathered_scales(a)
         load_rows(4)
+        nc.sync.dma_start(out=w2_w[:].bitcast(I32), in_=w2_words.rearrange("a p c -> p a c").bitcast(I32))
+        load_scales(w2_s, w2_scales)
         load_rows(5)
         load_w1(1, 0)
-        load_rows(6)
-        load_rows(7)
+        load_pair(6)
         load_w1(1, 1)
+        nc.sync.dma_start(out=c1_sb[:], in_=c1.rearrange("(g p t) -> p g t", g=PASSES, t=PACK))
+        nc.sync.dma_start(out=c2_sb[:], in_=c2.rearrange("(g p t) -> p g t", g=PASSES, t=PACK))
         nc.sync.dma_start(out=w3_w[:], in_=w3_words.rearrange("a p c i -> p a (c i)").bitcast(I32))
         load_scales(w3_s, w3_scales)
         with nc.allow_non_contiguous_dma(reason="one bias value to a partition"):
             nc.sync.dma_start(out=b_sb[:], in_=b.rearrange("(n p) -> p n", p=P))
 
-        for n in range(PACK):
+        for n in range(2):
             all_columns(n)
+        pair_of_tiles(2, 0, S, [x0[:, 2 + e, :] for e in range(2)], [lower[e][:] for e in range(2)])
         for g in range(PASSES):
             round_w1(0, g, 0, P)
         for a in range(PASSES):
             gather_words(a)
-        quantise(w1_bf0[:], w1_w0[:], w1_s0[:])
+            quantise_w1(0, a)
         all_columns(4)
-        quantise(round_x(x0, "x0_bf")[:], x0_w[:], x0_s[:])
+        quantise(round_x(x0, "x0_bf", tag="w1_pass0")[:], x0_w[:], x0_s[:])
         round_w1(1, 0, 0, P)
         for g in range(PASSES):
             for q in range(4):
                 hardiness_transposed(q, g)
-        m = {(q, 0): hardiness_in_sbuf(q) for q in range(4)}
-        for q in range(4):
-            m[q, 1] = hardiness(q, 1, q)
+        m = {(q, 0): hardiness(q, 0, q) for q in range(4)}
 
         all_columns(5)
-        quarters = [lower[e][:, 0:QUARTER] for e in range(2)]
-        half_of_columns(6, 0, quarters)
-        half_of_columns(7, 0, [quarters[0], scratch7[:]])
+        pair_of_tiles(6, 0, HALF, [x1[0][:, 2 + e, :] for e in range(2)], [scratch7[:], lower[1][:, 0:HALF]])
         quantise_w1(1, 0)
         x1_bf0 = round_x(x1[0], "x1_bf")
-        second = slice(HALF // STRIPE, S // STRIPE)
-        for e in range(2):
-            nc.vector.tensor_copy(out=lower[e][:], in_=rows[6 + e][:].indirect(idx3[:, second]))
-        for e in range(2):
-            nc.vector.tensor_tensor(
-                out=x1[1][:, 2 + e, :], in0=rows[6 + e][:].indirect(idx2[:, second]), in1=lower[e][:], op=ALU.subtract
-            )
+        pair_of_tiles(6, HALF, HALF, [x1[1][:, 2 + e, :] for e in range(2)], [lower[e][:, 0:HALF] for e in range(2)])
         quantise(x1_bf0[:], x1_w[:, 0:HALF], x1_s[:, 0:HALF])
         x1_bf1 = round_x(x1[1], "x1_bf1", tag="x1_bf", on_vector=True)
         quantise(x1_bf1[:], x1_w[:, HALF:S], x1_s[:, HALF:S])
@@ -337,12 +321,17 @@ def tile_list_frost_risk_map_kernel(
         round_w1(1, 1, 0, P)
         quantise_w1(1, 1)
         quadratic_half(0, 0, (4, 5))
-        add_hardiness_sbuf(0, m[0, 0])
-        add_hardiness_sbuf(1, m[1, 0])
+        add_hardiness(0, 0, m[0, 0])
+        add_hardiness(1, 0, m[1, 0])
+        for q in range(2):
+            m[q, 1] = hardiness(q, 1, q)
         quadratic_half(0, 1, (6, 7))
-        add_hardiness_sbuf(2, m[2, 0])
-        add_hardiness_sbuf(3, m[3, 0])
+        add_hardiness(2, 0, m[2, 0])
+        add_hardiness(3, 0, m[3, 0])
+        for q in range(2, 4):
+            m[q, 1] = hardiness(q, 1, q)
         quadratic_half(1, 0, (4, 5))
+        quantise_h(0, 0, 2)
         pairs = [inner_pair(1, 1, pair, 6 + pair) for pair in range(2)]
         two, one = bank(4, [P, 2, HALF]), bank(5, [P, HALF])
         ys_half = [(two[:, 0, :], True, False), (two[:, 1, :], False, True), (one[:], True, True)]
@@ -350,8 +339,6 @@ def tile_list_frost_risk_map_kernel(
         add_hardiness(1, 1, m[1, 1])
         first, final = slice(0, QUARTER), slice(QUARTER, HALF)
         outer_pair(1, 1, 0, *pairs[0], first)
-        h_w[0, 0] = held("h_w00", [P, HALF], U32, tag="quad10")
-        quantise_h(0, 0, 2)
         damage_pass(ys_half, slice(0, HALF), 0)
         quantise_h(1, 0, 2)
         outer_pair(1, 1, 1, *pairs[1], first)
@@ -359,7 +346,6 @@ def tile_list_frost_risk_map_kernel(
         add_bias_and_store(ys_half, y_half, slice(0, HALF))
         outer_pair(1, 1, 0, *pairs[0], final)
         add_hardiness(2, 1, m[2, 1])
-        h_w[0, 1] = held("h_w01", [P, HALF], U32, tag="inner110")
         quantise_h(0, 2, 4)
         three = bank(0, [P, N_TILES, P])
         ys_third = [(three[:, n, :], n == 0, n == N_TILES - 1) for n in range(N_TILES)]

@@ -88,7 +88,7 @@ def tile_list_frost_risk_map_kernel(
         m_t = {(q, g): (m_t0, m_t1)[g][:, q, :, :] for q in range(4) for g in range(PASSES)}
         quad = {(g, h): held(f"quad{g}{h}", [P, 2, HALF, 2], F32) for g in range(PASSES) for h in range(2)}
         h_bf = {(g, q): held(f"h_bf{g}{q}", [P, n * KP], BF16) for g in range(PASSES) for q, n in ((0, 2), (2, 2))}
-        h_w = {(g, h): held(f"h_w{g}{h}", [P, HALF], U32) for g in range(PASSES) for h in range(2)}
+        h_w = {(g, h): held(f"h_w{g}{h}", [P, HALF], U32) for g, h in ((0, 1), (1, 0), (1, 1))}
         h_s = {(g, h): held(f"h_s{g}{h}", [P, HALF], U8) for g in range(PASSES) for h in range(2)}
         y_half = held("y_half", [P, N_TILES, HALF], F32)
         y_sb = {q: held(f"y_sb{q}", [P, N_TILES, P], F32) for q in (2, 3)}
@@ -231,6 +231,21 @@ def tile_list_frost_risk_map_kernel(
             for pair in range(2):
                 outer_pair(g, h, pair, *inner_pair(g, h, pair, numbers[pair]))
 
+        def add_hardiness_sbuf(q, m_sb):
+            terms = quad[0, 0][:, :, q * QUARTER : (q + 1) * QUARTER, :]
+            nc.gpsimd.tensor_tensor(
+                out=h_bf[0, 0][:, q * KP : (q + 1) * KP].rearrange("p (j r e) -> p j r e", r=2, e=2),
+                in0=m_sb[:].rearrange("p j (r e) -> p j r e", e=2),
+                in1=terms.rearrange("p r j e -> p j r e"),
+                op=ALU.add,
+            )
+
+        def hardiness_in_sbuf(q):
+            m = hardiness(q, 0, q)
+            m_sb = held(f"m_sb{q}", [P, P, PACK], F32, tag=f"rows{q}")
+            nc.scalar.activation(out=m_sb[:], in_=m[:].rearrange("p t j -> p j t"), func=ACT.Copy)
+            return m_sb
+
         def add_hardiness(q, g, m):
             terms = quad[g, q // 2][:, :, (q % 2) * QUARTER : (q % 2 + 1) * QUARTER, :]
             nc.vector.tensor_tensor(
@@ -307,7 +322,9 @@ def tile_list_frost_risk_map_kernel(
         for g in range(PASSES):
             for q in range(4):
                 hardiness_transposed(q, g)
-        m = {(q, 0): hardiness(q, 0, q) for q in range(4)}
+        m = {(q, 0): hardiness_in_sbuf(q) if q < 2 else hardiness(q, 0, q) for q in range(4)}
+        for q in range(2):
+            m[q, 1] = hardiness(q, 1, q)
 
         all_columns(5)
         pair_of_tiles(6, 0, HALF, [x1[0][:, 2 + e, :] for e in range(2)], [scratch7[:], lower[1][:, 0:HALF]])
@@ -321,17 +338,14 @@ def tile_list_frost_risk_map_kernel(
         round_w1(1, 1, 0, P)
         quantise_w1(1, 1)
         quadratic_half(0, 0, (4, 5))
-        add_hardiness(0, 0, m[0, 0])
-        add_hardiness(1, 0, m[1, 0])
-        for q in range(2):
-            m[q, 1] = hardiness(q, 1, q)
+        add_hardiness_sbuf(0, m[0, 0])
+        add_hardiness_sbuf(1, m[1, 0])
         quadratic_half(0, 1, (6, 7))
         add_hardiness(2, 0, m[2, 0])
         add_hardiness(3, 0, m[3, 0])
         for q in range(2, 4):
             m[q, 1] = hardiness(q, 1, q)
         quadratic_half(1, 0, (4, 5))
-        quantise_h(0, 0, 2)
         pairs = [inner_pair(1, 1, pair, 6 + pair) for pair in range(2)]
         two, one = bank(4, [P, 2, HALF]), bank(5, [P, HALF])
         ys_half = [(two[:, 0, :], True, False), (two[:, 1, :], False, True), (one[:], True, True)]
@@ -339,6 +353,8 @@ def tile_list_frost_risk_map_kernel(
         add_hardiness(1, 1, m[1, 1])
         first, final = slice(0, QUARTER), slice(QUARTER, HALF)
         outer_pair(1, 1, 0, *pairs[0], first)
+        h_w[0, 0] = held("h_w00", [P, HALF], U32, tag="quad10")
+        quantise_h(0, 0, 2)
         damage_pass(ys_half, slice(0, HALF), 0)
         quantise_h(1, 0, 2)
         outer_pair(1, 1, 1, *pairs[1], first)

@@ -68,8 +68,8 @@ def tile_list_frost_risk_map_kernel(
         for g in range(PASSES):
             w1_f32[1, g] = held(f"w1_f32_1{g}", [P, PACK, KP], F32)[:]
         scratch7 = held("scratch7", [P, HALF], F32, tag="w1_w10")
-        w1_w0, w1_s0 = held("w1_w0", [P, H], U32), held("w1_s0", [P, H], U8)
-        w1_w = {(0, g): w1_w0[:, g * KP : (g + 1) * KP] for g in range(PASSES)}
+        w1_s0 = held("w1_s0", [P, H], U8)
+        w1_w = {(0, 0): held("w1_w00", [P, KP], U32)[:], (0, 1): held("w1_w01", [P, KP], U32, tag="tab_w1")[:]}
         w1_s = {(0, g): w1_s0[:, g * KP : (g + 1) * KP] for g in range(PASSES)}
         for g in range(PASSES):
             w1_w[1, g] = held(f"w1_w1{g}", [P, KP], U32)[:]
@@ -88,7 +88,7 @@ def tile_list_frost_risk_map_kernel(
         m_t = {(q, g): (m_t0, m_t1)[g][:, q, :, :] for q in range(4) for g in range(PASSES)}
         quad = {(g, h): held(f"quad{g}{h}", [P, 2, HALF, 2], F32) for g in range(PASSES) for h in range(2)}
         h_bf = {(g, q): held(f"h_bf{g}{q}", [P, n * KP], BF16) for g in range(PASSES) for q, n in ((0, 2), (2, 2))}
-        h_w = {(g, h): held(f"h_w{g}{h}", [P, HALF], U32) for g, h in ((0, 1), (1, 0), (1, 1))}
+        h_w = {(g, h): held(f"h_w{g}{h}", [P, HALF], U32) for g, h in ((1, 0), (1, 1))}
         h_s = {(g, h): held(f"h_s{g}{h}", [P, HALF], U8) for g in range(PASSES) for h in range(2)}
         y_half = held("y_half", [P, N_TILES, HALF], F32)
         y_sb = {q: held(f"y_sb{q}", [P, N_TILES, P], F32) for q in (2, 3)}
@@ -232,9 +232,9 @@ def tile_list_frost_risk_map_kernel(
                 outer_pair(g, h, pair, *inner_pair(g, h, pair, numbers[pair]))
 
         def add_hardiness_sbuf(q, m_sb):
-            terms = quad[0, 0][:, :, q * QUARTER : (q + 1) * QUARTER, :]
+            terms = quad[0, q // 2][:, :, (q % 2) * QUARTER : (q % 2 + 1) * QUARTER, :]
             nc.gpsimd.tensor_tensor(
-                out=h_bf[0, 0][:, q * KP : (q + 1) * KP].rearrange("p (j r e) -> p j r e", r=2, e=2),
+                out=h_bf[0, q - q % 2][:, (q % 2) * KP : (q % 2 + 1) * KP].rearrange("p (j r e) -> p j r e", r=2, e=2),
                 in0=m_sb[:].rearrange("p j (r e) -> p j r e", e=2),
                 in1=terms.rearrange("p r j e -> p j r e"),
                 op=ALU.add,
@@ -294,9 +294,9 @@ def tile_list_frost_risk_map_kernel(
         for a in range(PASSES):
             load_table(a)
             place_gathered_scales(a)
-        load_rows(4)
         nc.sync.dma_start(out=w2_w[:].bitcast(I32), in_=w2_words.rearrange("a p c -> p a c").bitcast(I32))
         load_scales(w2_s, w2_scales)
+        load_rows(4)
         load_rows(5)
         load_w1(1, 0)
         load_pair(6)
@@ -322,8 +322,8 @@ def tile_list_frost_risk_map_kernel(
         for g in range(PASSES):
             for q in range(4):
                 hardiness_transposed(q, g)
-        m = {(q, 0): hardiness_in_sbuf(q) if q < 2 else hardiness(q, 0, q) for q in range(4)}
-        for q in range(2):
+        m = {(q, 0): hardiness_in_sbuf(q) if q < 3 else hardiness(q, 0, q) for q in range(4)}
+        for q in range(3):
             m[q, 1] = hardiness(q, 1, q)
 
         all_columns(5)
@@ -341,28 +341,28 @@ def tile_list_frost_risk_map_kernel(
         add_hardiness_sbuf(0, m[0, 0])
         add_hardiness_sbuf(1, m[1, 0])
         quadratic_half(0, 1, (6, 7))
-        add_hardiness(2, 0, m[2, 0])
+        add_hardiness_sbuf(2, m[2, 0])
         add_hardiness(3, 0, m[3, 0])
-        for q in range(2, 4):
-            m[q, 1] = hardiness(q, 1, q)
+        m[3, 1] = hardiness(3, 1, 3)
         quadratic_half(1, 0, (4, 5))
         pairs = [inner_pair(1, 1, pair, 6 + pair) for pair in range(2)]
         two, one = bank(4, [P, 2, HALF]), bank(5, [P, HALF])
         ys_half = [(two[:, 0, :], True, False), (two[:, 1, :], False, True), (one[:], True, True)]
         add_hardiness(0, 1, m[0, 1])
+        h_w[0, 0] = held("h_w00", [P, HALF], U32, tag="inner101")
+        quantise_h(0, 0, 2)
+        damage_pass(ys_half, slice(0, HALF), 0)
         add_hardiness(1, 1, m[1, 1])
         first, final = slice(0, QUARTER), slice(QUARTER, HALF)
         outer_pair(1, 1, 0, *pairs[0], first)
-        h_w[0, 0] = held("h_w00", [P, HALF], U32, tag="quad10")
-        quantise_h(0, 0, 2)
-        damage_pass(ys_half, slice(0, HALF), 0)
         quantise_h(1, 0, 2)
         outer_pair(1, 1, 1, *pairs[1], first)
+        h_w[0, 1] = held("h_w01", [P, HALF], U32, tag="h_bf10")
+        quantise_h(0, 2, 4)
         damage_pass(ys_half, slice(0, HALF), 1)
         add_bias_and_store(ys_half, y_half, slice(0, HALF))
         outer_pair(1, 1, 0, *pairs[0], final)
         add_hardiness(2, 1, m[2, 1])
-        quantise_h(0, 2, 4)
         three = bank(0, [P, N_TILES, P])
         ys_third = [(three[:, n, :], n == 0, n == N_TILES - 1) for n in range(N_TILES)]
         damage_pass(ys_third, slice(HALF, HALF + QUARTER), 0)

@@ -67,12 +67,11 @@ def tile_list_frost_risk_map_kernel(
         w1_f32 = {(0, g): w1_pass0[:, :, g * KP : (g + 1) * KP] for g in range(PASSES)}
         for g in range(PASSES):
             w1_f32[1, g] = held(f"w1_f32_1{g}", [P, PACK, KP], F32)[:]
-        scratch7 = held("scratch7", [P, HALF], F32, tag="w1_w10")
         w1_s0 = held("w1_s0", [P, H], U8)
-        w1_w = {(0, 0): held("w1_w00", [P, KP], U32)[:], (0, 1): held("w1_w01", [P, KP], U32, tag="tab_w1")[:]}
+        codes0 = held("codes0", [P, KP + S], U32, tag="tab_w1")
+        w1_w = {(0, 0): held("w1_w00", [P, KP], U32)[:], (0, 1): codes0[:, 0:KP]}
         w1_s = {(0, g): w1_s0[:, g * KP : (g + 1) * KP] for g in range(PASSES)}
         for g in range(PASSES):
-            w1_w[1, g] = held(f"w1_w1{g}", [P, KP], U32)[:]
             w1_s[1, g] = held(f"w1_s1{g}", [P, KP], U8)[:]
         w1_bf0 = held("w1_bf0", [P, PASSES * PACK * KP], BF16)
         w1_bf = {(0, g): w1_bf0[:, g * PACK * KP : (g + 1) * PACK * KP] for g in range(PASSES)}
@@ -81,20 +80,21 @@ def tile_list_frost_risk_map_kernel(
         lower = [held(f"lower{n}", [P, S], F32) for n in range(2)]
         x0 = held("x0", [P, PACK, S], F32)
         x1 = [held(f"x1_{h}", [P, PACK, HALF], F32) for h in range(2)]
-        x0_w, x0_s = held("x0_w", [P, S], U32), held("x0_s", [P, S], U8)
-        x1_w, x1_s = held("x1_w", [P, S], U32), held("x1_s", [P, S], U8)
-        m_t0 = held("m_t0", [P, 4, PACK, P], F32)
-        m_t1 = held("m_t1", [P, 4, PACK, P], F32, tag="w1_f32_10")
-        m_t = {(q, g): (m_t0, m_t1)[g][:, q, :, :] for q in range(4) for g in range(PASSES)}
+        x0_w, x0_s = codes0[:, KP : KP + S], held("x0_s", [P, S], U8)
+        x1_w, x1_s = {}, {h: held(f"x1_s{h}", [P, HALF], U8) for h in range(2)}
+        m_half = {(h, g): held(f"m_t{h}{g}", [P, 2, PACK, P], F32) for h, g in ((0, 0), (0, 1), (1, 0))}
+        m_half[1, 1] = held("m_t11", [P, 2, PACK, P], F32, tag="w1_f32_10")
+        m_t = {(q, g): m_half[q // 2, g][:, q % 2, :, :] for q in range(4) for g in range(PASSES)}
         quad = {(g, h): held(f"quad{g}{h}", [P, 2, HALF, 2], F32) for g in range(PASSES) for h in range(2)}
         h_bf = {(g, q): held(f"h_bf{g}{q}", [P, n * KP], BF16) for g in range(PASSES) for q, n in ((0, 2), (2, 2))}
-        h_w = {(g, h): held(f"h_w{g}{h}", [P, HALF], U32) for g, h in ((1, 0), (1, 1))}
+        h_w = {(g, h): held(f"h_w{g}{h}", [P, HALF], U32) for g, h in ((0, 1), (1, 1))}
         h_s = {(g, h): held(f"h_s{g}{h}", [P, HALF], U8) for g in range(PASSES) for h in range(2)}
         y_half = held("y_half", [P, N_TILES, HALF], F32)
         y_sb = {q: held(f"y_sb{q}", [P, N_TILES, P], F32) for q in (2, 3)}
 
-        for part in (tab_s[32:64, :], tab_s[64:P, :], v_s[0][:], v_s[1][:], w2_s[:], w3_s[:]):
-            nc.vector.memset(part.bitcast(I32), 0)
+        nc.vector.memset(tab_s[64:P, :].bitcast(I32), 0)
+        for part in (tab_s[32:64, :], v_s[0][:], v_s[1][:], w2_s[:], w3_s[:]):
+            nc.gpsimd.memset(part.bitcast(I32), 0)
         make_identity(nc, ident[:])
 
         def load_rows(n, cols=slice(0, T2)):
@@ -113,10 +113,10 @@ def tile_list_frost_risk_map_kernel(
             part = w1[a * KP : (a + 1) * KP, g * KP : (g + 1) * KP]
             nc.sync.dma_start(out=w1_f32[a, g], in_=part.rearrange("(p i) c -> p i c", i=PACK))
 
-        def load_scales(tile, scales):
+        def load_scales(tile, scales, queue):
             for r in range(4):
                 part = scales[:, r:16:4, :].rearrange("a n c -> n a c")
-                nc.sync.dma_start(out=tile[r:P:32, :, :].bitcast(I32), in_=part.bitcast(I32))
+                queue.dma_start(out=tile[r:P:32, :, :].bitcast(I32), in_=part.bitcast(I32))
 
         def place_gathered_scales(a):
             for r in range(4):
@@ -132,10 +132,10 @@ def tile_list_frost_risk_map_kernel(
                     out=outs[e], in0=rows[n][:].indirect(idx2[:, cols[e]]), in1=scratch[e], op=ALU.subtract
                 )
 
-        def all_columns(n):
+        def all_columns(n, scratch=None):
             a, i = divmod(n, PACK)
             outs = [x0[:, i, h * HALF : (h + 1) * HALF] if a == 0 else x1[h][:, i, :] for h in range(2)]
-            differences(n, 0, HALF, outs, [lower[e][:, 0:HALF] for e in range(2)])
+            differences(n, 0, HALF, outs, scratch or [lower[e][:, 0:HALF] for e in range(2)])
 
         def pair_of_tiles(n, first, width, outs, scratch):
             cols = slice(first // STRIPE, (first + width) // STRIPE)
@@ -159,6 +159,12 @@ def tile_list_frost_risk_map_kernel(
         def quantise(bf, words, scales):
             nc.vector.quantize_mx(out=words.bitcast(FP8X4), scales=scales, in_=bf)
 
+        def round_w1_vector(a, g, m0, m1):
+            nc.vector.tensor_copy(
+                out=w1_bf[a, g].rearrange("p (t m i) -> p m i t", t=PACK, i=PACK)[:, m0:m1, :, :],
+                in_=w1_f32[a, g].rearrange("p i (m t) -> p m i t", t=PACK)[:, m0:m1, :, :],
+            )
+
         def round_w1(a, g, m0, m1):
             part = w1_f32[a, g]
             nc.scalar.activation(
@@ -174,16 +180,16 @@ def tile_list_frost_risk_map_kernel(
             nc.vector.tensor_copy(out=v_w[a][:], in_=tab_w[a][:].bitcast(U32).indirect(idx[:]))
 
         def hardiness_transposed(q, g):
-            sums = bank(4 * g + q, [P, KP])
-            for a in range(PASSES):
+            sums = bank(4 * (q // 2) + 2 * g + q % 2, [P, KP])
+            for a in (1, 0):
                 nc.tensor.matmul_mx(
                     out=sums[:],
                     lhsT=v_w[a][:, q * P : (q + 1) * P].bitcast(FP8X4),
                     lhsT_scale=v_s[a][:, q * P : (q + 1) * P],
                     rhs=w2_w[:, a, 2 * g * KP : 2 * (g + 1) * KP].bitcast(FP4X4),
                     rhs_scale=w2_s[:, a, g * KP : (g + 1) * KP],
-                    start=(a == 0),
-                    stop=(a == PASSES - 1),
+                    start=(a == 1),
+                    stop=(a == 0),
                 )
             nc.scalar.activation(out=m_t[q, g], in_=sums[:].rearrange("p (m t) -> p t m", t=PACK), func=ACT.Copy)
 
@@ -193,17 +199,17 @@ def tile_list_frost_risk_map_kernel(
                 nc.tensor.transpose(m[:, t, :], m_t[q, g][:, t, :], ident[:])
             return m
 
-        def response(d, g, t, cols):
-            for a, (x_w, x_s) in enumerate(((x0_w, x0_s), (x1_w, x1_s))):
-                nc.tensor.matmul_mx(
-                    out=d,
-                    lhsT=w1_w[a, g][:, t * P : (t + 1) * P].bitcast(FP8X4),
-                    lhsT_scale=w1_s[a, g][:, t * P : (t + 1) * P],
-                    rhs=x_w[:, cols].bitcast(FP8X4),
-                    rhs_scale=x_s[:, cols],
-                    start=(a == 0),
-                    stop=(a == PASSES - 1),
-                )
+        def response(d, a, g, t, cols, start, stop):
+            x_w, x_s = (x0_w[:, cols], x0_s[:, cols]) if a == 0 else (x1_w[cols.start // HALF][:], x1_s[cols.start // HALF][:])
+            nc.tensor.matmul_mx(
+                out=d,
+                lhsT=w1_w[a, g][:, t * P : (t + 1) * P].bitcast(FP8X4),
+                lhsT_scale=w1_s[a, g][:, t * P : (t + 1) * P],
+                rhs=x_w.bitcast(FP8X4),
+                rhs_scale=x_s,
+                start=start,
+                stop=stop,
+            )
 
         def inner_step(inner, d, g, t):
             nc.scalar.activation(
@@ -213,8 +219,9 @@ def tile_list_frost_risk_map_kernel(
         def inner_pair(g, h, pair, number):
             d = bank(number, [P, 2, HALF])
             inner = held(f"inner{g}{h}{pair}", [P, 2, HALF], F32)
-            for e in range(2):
-                response(d[:, e, :], g, 2 * pair + e, slice(h * HALF, (h + 1) * HALF))
+            for a in range(PASSES):
+                for e in range(2):
+                    response(d[:, e, :], a, g, 2 * pair + e, slice(h * HALF, (h + 1) * HALF), a + e == 0, a + e == 2)
             for e in range(2):
                 inner_step(inner[:, e, :], d[:, e, :], g, 2 * pair + e)
             return d, inner
@@ -231,18 +238,17 @@ def tile_list_frost_risk_map_kernel(
             for pair in range(2):
                 outer_pair(g, h, pair, *inner_pair(g, h, pair, numbers[pair]))
 
-        def add_hardiness_sbuf(q, m_sb):
-            terms = quad[0, q // 2][:, :, (q % 2) * QUARTER : (q % 2 + 1) * QUARTER, :]
+        def add_hardiness_sbuf(q, g, m_sb):
+            terms = quad[g, q // 2][:, :, (q % 2) * QUARTER : (q % 2 + 1) * QUARTER, :]
             nc.gpsimd.tensor_tensor(
-                out=h_bf[0, q - q % 2][:, (q % 2) * KP : (q % 2 + 1) * KP].rearrange("p (j r e) -> p j r e", r=2, e=2),
+                out=h_bf[g, q - q % 2][:, (q % 2) * KP : (q % 2 + 1) * KP].rearrange("p (j r e) -> p j r e", r=2, e=2),
                 in0=m_sb[:].rearrange("p j (r e) -> p j r e", e=2),
                 in1=terms.rearrange("p r j e -> p j r e"),
                 op=ALU.add,
             )
 
-        def hardiness_in_sbuf(q):
-            m = hardiness(q, 0, q)
-            m_sb = held(f"m_sb{q}", [P, P, PACK], F32, tag=f"rows{q}")
+        def hardiness_in_sbuf(q, g, m):
+            m_sb = held(f"m_sb{q}{g}", [P, P, PACK], F32)
             nc.scalar.activation(out=m_sb[:], in_=m[:].rearrange("p t j -> p j t"), func=ACT.Copy)
             return m_sb
 
@@ -280,97 +286,119 @@ def tile_list_frost_risk_map_kernel(
         def add_bias_and_store(ys, y_out, cols):
             for n, (y, first, final) in enumerate(ys):
                 nc.scalar.activation(out=y_out[:, n, :], in_=y, func=ACT.Identity, bias=b_sb[:, n : n + 1])
-            nc.sync.dma_start(out=out[:, cols].rearrange("(n p) j -> p n j", p=P), in_=y_out[:])
+                nc.sync.dma_start(out=out[n * P : (n + 1) * P, cols], in_=y_out[:, n, :])
 
         nc.sync.dma_start(out=tab_s[0:32, :].bitcast(I32), in_=tab_scales.rearrange("a n t -> (a n) t").bitcast(I32))
         nc.sync.dma_start(idx[:], offs)
         load_rows(0)
         nc.sync.dma_start(idx3[:], offs3)
-        nc.sync.dma_start(idx2[:], offs2)
         load_rows(1)
+        nc.sync.dma_start(idx2[:], offs2)
         load_pair(2)
         nc.sync.dma_start(out=w1_pass0[:], in_=w1[0:KP, :].rearrange("(p i) c -> p i c", i=PACK))
         nc.vector.tensor_copy(out=v_rows[:], in_=tab_s[:].indirect(idx[:]))
-        for a in range(PASSES):
-            load_table(a)
-            place_gathered_scales(a)
-        nc.sync.dma_start(out=w2_w[:].bitcast(I32), in_=w2_words.rearrange("a p c -> p a c").bitcast(I32))
-        load_scales(w2_s, w2_scales)
         load_rows(4)
+        for a in range(PASSES):
+            place_gathered_scales(a)
+            load_table(a)
+        nc.sync.dma_start(out=w2_w[:].bitcast(I32), in_=w2_words.rearrange("a p c -> p a c").bitcast(I32))
+        load_scales(w2_s, w2_scales, nc.sync)
         load_rows(5)
+        load_rows(6)
         load_w1(1, 0)
-        load_pair(6)
+        load_rows(7)
         load_w1(1, 1)
         nc.sync.dma_start(out=c1_sb[:], in_=c1.rearrange("(g p t) -> p g t", g=PASSES, t=PACK))
         nc.sync.dma_start(out=c2_sb[:], in_=c2.rearrange("(g p t) -> p g t", g=PASSES, t=PACK))
         nc.sync.dma_start(out=w3_w[:], in_=w3_words.rearrange("a p c i -> p a (c i)").bitcast(I32))
-        load_scales(w3_s, w3_scales)
+        load_scales(w3_s, w3_scales, nc.sync)
         with nc.allow_non_contiguous_dma(reason="one bias value to a partition"):
             nc.sync.dma_start(out=b_sb[:], in_=b.rearrange("(n p) -> p n", p=P))
 
-        for n in range(2):
-            all_columns(n)
-        pair_of_tiles(2, 0, S, [x0[:, 2 + e, :] for e in range(2)], [lower[e][:] for e in range(2)])
+        for e in range(2):
+            nc.vector.tensor_copy(out=lower[e][:], in_=rows[e][:].indirect(idx3[:]))
+        for e in range(2):
+            nc.vector.tensor_tensor(out=x0[:, e, :], in0=rows[e][:].indirect(idx2[:]), in1=lower[e][:], op=ALU.subtract)
+        pair_of_tiles(2, 0, S, [x0[:, 2 + e, :] for e in range(2)], [lower[1 - e][:] for e in range(2)])
         for g in range(PASSES):
             round_w1(0, g, 0, P)
+        all_columns(4)
+        quantise_w1(0, 0)
         for a in range(PASSES):
             gather_words(a)
-            quantise_w1(0, a)
-        all_columns(4)
-        quantise(round_x(x0, "x0_bf", tag="w1_pass0")[:], x0_w[:], x0_s[:])
-        round_w1(1, 0, 0, P)
-        for g in range(PASSES):
-            for q in range(4):
-                hardiness_transposed(q, g)
-        m = {(q, 0): hardiness_in_sbuf(q) if q < 3 else hardiness(q, 0, q) for q in range(4)}
-        for q in range(3):
-            m[q, 1] = hardiness(q, 1, q)
-
+        quantise_w1(0, 1)
+        x0_bf = round_x(x0, "x0_bf", tag="w1_pass0")
+        quantise(x0_bf[:], x0_w, x0_s[:])
         all_columns(5)
-        pair_of_tiles(6, 0, HALF, [x1[0][:, 2 + e, :] for e in range(2)], [scratch7[:], lower[1][:, 0:HALF]])
-        quantise_w1(1, 0)
-        x1_bf0 = round_x(x1[0], "x1_bf")
-        pair_of_tiles(6, HALF, HALF, [x1[1][:, 2 + e, :] for e in range(2)], [lower[e][:, 0:HALF] for e in range(2)])
-        quantise(x1_bf0[:], x1_w[:, 0:HALF], x1_s[:, 0:HALF])
-        x1_bf1 = round_x(x1[1], "x1_bf1", tag="x1_bf", on_vector=True)
-        quantise(x1_bf1[:], x1_w[:, HALF:S], x1_s[:, HALF:S])
+        for h in range(2):
+            for g in range(PASSES):
+                if (h, g) == (1, 1):
+                    round_w1(1, 0, 0, P)
+                for q in (2 * h, 2 * h + 1):
+                    hardiness_transposed(q, g)
+        m = {(q, g): hardiness(q, g, 2 * g + q) for g in range(PASSES) for q in range(2)}
 
-        round_w1(1, 1, 0, P)
+        all_columns(6)
+        round_w1(1, 1, 0, P // 2)
+        lower7 = held("lower7", [P, HALF], F32, tag="w1_w10")
+        all_columns(7, [lower7[:], lower[1][:, 0:HALF]])
+        x1_bf0 = round_x(x1[0], "x1_bf0", on_vector=True)
+        x1_w[0] = held("x1_w0", [P, HALF], U32)
+        quantise(x1_bf0[:], x1_w[0][:], x1_s[0][:])
+        w1_w[1, 0] = held("w1_w10", [P, KP], U32)[:]
+        quantise_w1(1, 0)
+        x1_bf1 = round_x(x1[1], "x1_bf1", tag="w1_bf10", on_vector=True)
+        round_w1_vector(1, 1, P // 2, P)
+        x1_w[1] = held("x1_w1", [P, HALF], U32)
+        quantise(x1_bf1[:], x1_w[1][:], x1_s[1][:])
+        w1_w[1, 1] = held("w1_w11", [P, KP], U32)[:]
         quantise_w1(1, 1)
-        quadratic_half(0, 0, (4, 5))
-        add_hardiness_sbuf(0, m[0, 0])
-        add_hardiness_sbuf(1, m[1, 0])
-        quadratic_half(0, 1, (6, 7))
-        add_hardiness_sbuf(2, m[2, 0])
-        add_hardiness(3, 0, m[3, 0])
-        m[3, 1] = hardiness(3, 1, 3)
-        quadratic_half(1, 0, (4, 5))
-        pairs = [inner_pair(1, 1, pair, 6 + pair) for pair in range(2)]
-        two, one = bank(4, [P, 2, HALF]), bank(5, [P, HALF])
+        m_sb = {(q, g): hardiness_in_sbuf(q, g, m[q, g]) for q, g in ((1, 0), (0, 1))}
+        pairs = {(0, 0): [inner_pair(0, 0, pair, 4 + pair) for pair in range(2)]}
+        m_sb[1, 1] = hardiness_in_sbuf(1, 1, m[1, 1])
+        pairs[1, 0] = [inner_pair(1, 0, pair, 6 + pair) for pair in range(2)]
+        pairs[0, 1] = [inner_pair(0, 1, pair, 1 + pair) for pair in range(2)]
+        for pair in range(2):
+            outer_pair(0, 0, pair, *pairs[0, 0][pair])
+        add_hardiness_sbuf(1, 0, m_sb[1, 0])
+        add_hardiness(0, 0, m[0, 0])
+        pairs[1, 1] = [inner_pair(1, 1, pair, 3 + pair) for pair in range(2)]
+        m[2, 0] = hardiness(2, 0, 5)
+        m[3, 0] = hardiness(3, 0, 0)
+        for pair in range(2):
+            outer_pair(1, 0, pair, *pairs[1, 0][pair])
+            if pair == 0:
+                h_w[0, 0] = held("h_w00", [P, HALF], U32, tag="inner100")
+                quantise_h(0, 0, 2)
+        for q in (2, 3):
+            m[q, 1] = hardiness(q, 1, 4 + q)
+        for q in range(2):
+            add_hardiness_sbuf(q, 1, m_sb[q, 1])
+        for pair in range(2):
+            outer_pair(0, 1, pair, *pairs[0, 1][pair])
+        two, one = bank(1, [P, 2, HALF]), bank(2, [P, HALF])
         ys_half = [(two[:, 0, :], True, False), (two[:, 1, :], False, True), (one[:], True, True)]
-        add_hardiness(0, 1, m[0, 1])
-        h_w[0, 0] = held("h_w00", [P, HALF], U32, tag="inner101")
-        quantise_h(0, 0, 2)
         damage_pass(ys_half, slice(0, HALF), 0)
-        add_hardiness(1, 1, m[1, 1])
+        add_hardiness(2, 0, m[2, 0])
+        add_hardiness(3, 0, m[3, 0])
         first, final = slice(0, QUARTER), slice(QUARTER, HALF)
-        outer_pair(1, 1, 0, *pairs[0], first)
+        outer_pair(1, 1, 0, *pairs[1, 1][0], first)
+        h_w[1, 0] = held("h_w10", [P, HALF], U32)
         quantise_h(1, 0, 2)
-        outer_pair(1, 1, 1, *pairs[1], first)
-        h_w[0, 1] = held("h_w01", [P, HALF], U32, tag="h_bf10")
         quantise_h(0, 2, 4)
+        outer_pair(1, 1, 1, *pairs[1, 1][1], first)
         damage_pass(ys_half, slice(0, HALF), 1)
         add_bias_and_store(ys_half, y_half, slice(0, HALF))
-        outer_pair(1, 1, 0, *pairs[0], final)
+        outer_pair(1, 1, 0, *pairs[1, 1][0], final)
         add_hardiness(2, 1, m[2, 1])
-        three = bank(0, [P, N_TILES, P])
+        three = bank(5, [P, N_TILES, P])
         ys_third = [(three[:, n, :], n == 0, n == N_TILES - 1) for n in range(N_TILES)]
         damage_pass(ys_third, slice(HALF, HALF + QUARTER), 0)
         last = 3
-        ys = [bank(number, [P, P]) for number in (1, 2, 6)]
+        outer_pair(1, 1, 1, *pairs[1, 1][1], final)
+        ys = [bank(number, [P, P]) for number in (0, 3, 4)]
         ys_last = [(y[:], True, True) for y in ys]
         damage_pass(ys_last, slice(last * P, S), 0)
-        outer_pair(1, 1, 1, *pairs[1], final)
         quantise_h(1, 2, 3)
         add_hardiness(3, 1, m[3, 1])
         damage_pass(ys_third, slice(HALF, HALF + QUARTER), 1)

@@ -77,6 +77,7 @@ def tile_list_frost_risk_map_kernel(
         w1_bf = {(0, g): w1_bf0[:, g * PACK * KP : (g + 1) * PACK * KP] for g in range(PASSES)}
         for g in range(PASSES):
             w1_bf[1, g] = held(f"w1_bf1{g}", [P, PACK * KP], BF16)[:]
+        picked = [held(f"picked{n}", [P, 2, S], F32, tag=f"quad{n}1") for n in range(2)]
         lower = [held(f"lower{n}", [P, S], F32) for n in range(2)]
         x0 = held("x0", [P, PACK, S], F32)
         x1 = [held(f"x1_{h}", [P, PACK, HALF], F32) for h in range(2)]
@@ -292,9 +293,10 @@ def tile_list_frost_risk_map_kernel(
         nc.sync.dma_start(idx[:], offs)
         load_rows(0)
         nc.sync.dma_start(idx3[:], offs3)
-        load_rows(1)
         nc.sync.dma_start(idx2[:], offs2)
-        load_pair(2)
+        load_rows(1)
+        load_rows(2)
+        load_rows(3)
         nc.sync.dma_start(out=w1_pass0[:], in_=w1[0:KP, :].rearrange("(p i) c -> p i c", i=PACK))
         nc.vector.tensor_copy(out=v_rows[:], in_=tab_s[:].indirect(idx[:]))
         load_rows(4)
@@ -315,11 +317,11 @@ def tile_list_frost_risk_map_kernel(
         with nc.allow_non_contiguous_dma(reason="one bias value to a partition"):
             nc.sync.dma_start(out=b_sb[:], in_=b.rearrange("(n p) -> p n", p=P))
 
-        for e in range(2):
-            nc.vector.tensor_copy(out=lower[e][:], in_=rows[e][:].indirect(idx3[:]))
-        for e in range(2):
-            nc.vector.tensor_tensor(out=x0[:, e, :], in0=rows[e][:].indirect(idx2[:]), in1=lower[e][:], op=ALU.subtract)
-        pair_of_tiles(2, 0, S, [x0[:, 2 + e, :] for e in range(2)], [lower[1 - e][:] for e in range(2)])
+        for n in range(PACK):
+            both = picked[n % 2]
+            for e, offsets in enumerate((idx3, idx2)):
+                nc.vector.tensor_copy(out=both[:, e, :], in_=rows[n][:].indirect(offsets[:]))
+            nc.gpsimd.tensor_tensor(out=x0[:, n, :], in0=both[:, 1, :], in1=both[:, 0, :], op=ALU.subtract)
         for g in range(PASSES):
             round_w1(0, g, 0, P)
         all_columns(4)

@@ -68,28 +68,32 @@ def tile_list_frost_risk_map_kernel(
         for g in range(PASSES):
             w1_f32[1, g] = held(f"w1_f32_1{g}", [P, PACK, KP], F32)[:]
         w1_s0 = held("w1_s0", [P, H], U8)
-        codes0 = held("codes0", [P, KP + S], U32, tag="tab_w1")
-        w1_w = {(0, 0): held("w1_w00", [P, KP], U32)[:], (0, 1): codes0[:, 0:KP]}
+        codes0 = held("codes0", [P, H + S], U32, tag="tab_w1")
+        w1_w = {(0, g): codes0[:, g * KP : (g + 1) * KP] for g in range(PASSES)}
         w1_s = {(0, g): w1_s0[:, g * KP : (g + 1) * KP] for g in range(PASSES)}
         for g in range(PASSES):
             w1_s[1, g] = held(f"w1_s1{g}", [P, KP], U8)[:]
         w1_bf0 = held("w1_bf0", [P, PASSES * PACK * KP], BF16)
         w1_bf = {(0, g): w1_bf0[:, g * PACK * KP : (g + 1) * PACK * KP] for g in range(PASSES)}
-        for g in range(PASSES):
-            w1_bf[1, g] = held(f"w1_bf1{g}", [P, PACK * KP], BF16)[:]
+        w1_bf[1, 1] = held("w1_bf11", [P, PACK * KP], BF16)[:]
         picked = [held(f"picked{n}", [P, 2, S], F32, tag=f"quad{n}1") for n in range(2)]
-        lower = [held(f"lower{n}", [P, S], F32) for n in range(2)]
         x0 = held("x0", [P, PACK, S], F32)
-        x1 = [held(f"x1_{h}", [P, PACK, HALF], F32) for h in range(2)]
-        x0_w, x0_s = codes0[:, KP : KP + S], held("x0_s", [P, S], U8)
+        x1_first = held("x1_first", [P, PACK, HALF], F32)
+        x1_second = held("x1_second", [P, (PACK - 1) * HALF + PACK * KP // 2], F32)
+        x1 = [x1_first[:], x1_second[:, 0 : PACK * HALF].rearrange("p (i c) -> p i c", i=PACK)]
+        x0_w, x0_s = codes0[:, H : H + S], held("x0_s", [P, S], U8)
+        w1_bf[1, 0] = x1_second[:, (PACK - 1) * HALF :].bitcast(BF16)
         x1_w, x1_s = {}, {h: held(f"x1_s{h}", [P, HALF], U8) for h in range(2)}
-        m_half = {(h, g): held(f"m_t{h}{g}", [P, 2, PACK, P], F32) for h, g in ((0, 0), (0, 1), (1, 0))}
-        m_half[1, 1] = held("m_t11", [P, 2, PACK, P], F32, tag="w1_f32_10")
-        m_t = {(q, g): m_half[q // 2, g][:, q % 2, :, :] for q in range(4) for g in range(PASSES)}
+        m_t = {(q, g): held(f"m_t{q}{g}", [P, PACK, P], F32)[:] for q in range(4) for g in range(PASSES) if (q // 2, g) != (1, 1)}
+        m_t_last = held("m_t_last", [P, 2, PACK, P], F32, tag="w1_f32_10")
+        for q in (2, 3):
+            m_t[q, 1] = m_t_last[:, q - 2]
         quad = {(g, h): held(f"quad{g}{h}", [P, 2, HALF, 2], F32) for g in range(PASSES) for h in range(2)}
-        h_bf = {(g, q): held(f"h_bf{g}{q}", [P, n * KP], BF16) for g in range(PASSES) for q, n in ((0, 2), (2, 2))}
-        h_w = {(g, h): held(f"h_w{g}{h}", [P, HALF], U32) for g, h in ((0, 1), (1, 1))}
-        h_s = {(g, h): held(f"h_s{g}{h}", [P, HALF], U8) for g in range(PASSES) for h in range(2)}
+        h_tiles = [
+            (held(f"h_bf{h}", [P, 4 * KP], BF16, tag=f"h_bf{h}"), held(f"h_w{h}", [P, 4 * P], U32), held(f"h_s{h}", [P, 4 * P], U8))
+            for h in range(2)
+        ]
+        groups = (slice(0, HALF), slice(HALF, HALF + QUARTER), slice(HALF + QUARTER, S))
         y_half = held("y_half", [P, N_TILES, HALF], F32)
         y_sb = {q: held(f"y_sb{q}", [P, N_TILES, P], F32) for q in (2, 3)}
 
@@ -101,11 +105,6 @@ def tile_list_frost_risk_map_kernel(
         def load_rows(n, cols=slice(0, T2)):
             a, i = divmod(n, PACK)
             nc.sync.dma_start(out=rows[n][:, cols], in_=xT[a * KP : (a + 1) * KP, :].rearrange("(p i) t -> p i t", i=PACK)[:, i, cols])
-
-        def load_pair(n):
-            load_rows(n, slice(0, T2 - P))
-            load_rows(n + 1)
-            load_rows(n, slice(T2 - P, T2))
 
         def load_table(a):
             nc.sync.dma_start(out=tab_w[a][:], in_=tab_words[a].rearrange("p t i -> p (t i)").bitcast(I32))
@@ -124,47 +123,37 @@ def tile_list_frost_risk_map_kernel(
                 part = v_rows[16 * a + r : 16 * a + 16 : 4, :]
                 nc.sync.dma_start(out=v_s[a][r:P:32, :].bitcast(I32), in_=part.bitcast(I32))
 
-        def differences(n, first, width, outs, scratch):
-            cols = [slice((first + e * width) // STRIPE, (first + (e + 1) * width) // STRIPE) for e in range(2)]
+        def pick(n, cols, scratch, e):
+            entries = slice(cols.start // STRIPE, cols.stop // STRIPE)
+            nc.vector.tensor_copy(out=scratch[:, e, :], in_=rows[n][:].indirect((idx3, idx2)[e][:, entries]))
+
+        def differences(n, cols, scratch, x_out):
             for e in range(2):
-                nc.vector.tensor_copy(out=scratch[e], in_=rows[n][:].indirect(idx3[:, cols[e]]))
+                pick(n, cols, scratch, e)
+            nc.gpsimd.tensor_tensor(out=x_out, in0=scratch[:, 1, :], in1=scratch[:, 0, :], op=ALU.subtract)
+
+        def differences_by_halves(n, scratch):
             for e in range(2):
-                nc.vector.tensor_tensor(
-                    out=outs[e], in0=rows[n][:].indirect(idx2[:, cols[e]]), in1=scratch[e], op=ALU.subtract
-                )
+                pick(n, slice(0, S), scratch, e)
+            for h in range(2):
+                cols = slice(h * HALF, (h + 1) * HALF)
+                nc.gpsimd.tensor_tensor(out=x1[h][:, n - PACK, :], in0=scratch[:, 1, cols], in1=scratch[:, 0, cols], op=ALU.subtract)
 
-        def all_columns(n, scratch=None):
-            a, i = divmod(n, PACK)
-            outs = [x0[:, i, h * HALF : (h + 1) * HALF] if a == 0 else x1[h][:, i, :] for h in range(2)]
-            differences(n, 0, HALF, outs, scratch or [lower[e][:, 0:HALF] for e in range(2)])
+        def round_x_scalar(x_bf):
+            nc.scalar.activation(
+                out=x_bf.rearrange("p (c e i) -> p c i e", e=RUN, i=PACK),
+                in_=x0[:].rearrange("p i (c e) -> p c i e", e=RUN),
+                func=ACT.Copy,
+            )
 
-        def pair_of_tiles(n, first, width, outs, scratch):
-            cols = slice(first // STRIPE, (first + width) // STRIPE)
-            for e in (1, 0):
-                nc.vector.tensor_copy(out=scratch[e], in_=rows[n + e][:].indirect(idx3[:, cols]))
-            for e in (1, 0):
-                nc.vector.tensor_tensor(
-                    out=outs[e], in0=rows[n + e][:].indirect(idx2[:, cols]), in1=scratch[e], op=ALU.subtract
-                )
-
-        def round_x(x_f32, name, tag="", on_vector=False):
-            x_bf = held(name, [P, PACK * x_f32.shape[2]], BF16, tag=tag)
-            dst = x_bf[:].rearrange("p (c e i) -> p c i e", e=RUN, i=PACK)
-            src = x_f32[:].rearrange("p i (c e) -> p c i e", e=RUN)
-            if on_vector:
-                nc.vector.tensor_copy(out=x_bf[:].rearrange("p (c i) -> p c i", i=PACK), in_=x_f32[:].rearrange("p i c -> p c i"))
-            else:
-                nc.scalar.activation(out=dst, in_=src, func=ACT.Copy)
-            return x_bf
+        def round_x_vector(h, x_bf):
+            nc.vector.tensor_copy(
+                out=x_bf.rearrange("p (c i) -> p c i", i=PACK),
+                in_=x1[h].rearrange("p i c -> p c i"),
+            )
 
         def quantise(bf, words, scales):
             nc.vector.quantize_mx(out=words.bitcast(FP8X4), scales=scales, in_=bf)
-
-        def round_w1_vector(a, g, m0, m1):
-            nc.vector.tensor_copy(
-                out=w1_bf[a, g].rearrange("p (t m i) -> p m i t", t=PACK, i=PACK)[:, m0:m1, :, :],
-                in_=w1_f32[a, g].rearrange("p i (m t) -> p m i t", t=PACK)[:, m0:m1, :, :],
-            )
 
         def round_w1(a, g, m0, m1):
             part = w1_f32[a, g]
@@ -235,54 +224,40 @@ def tile_list_frost_risk_map_kernel(
                 op=ALU.mult,
             )
 
-        def quadratic_half(g, h, numbers):
-            for pair in range(2):
-                outer_pair(g, h, pair, *inner_pair(g, h, pair, numbers[pair]))
+        def sum_operands(q, g):
+            place = 2 * g + q % 2
+            h_part = h_tiles[q // 2][0][:, place * KP : (place + 1) * KP].rearrange("p (j r e) -> p j r e", r=2, e=2)
+            terms = quad[g, q // 2][:, :, (q % 2) * QUARTER : (q % 2 + 1) * QUARTER, :]
+            return h_part, terms.rearrange("p r j e -> p j r e")
 
         def add_hardiness_sbuf(q, g, m_sb):
-            terms = quad[g, q // 2][:, :, (q % 2) * QUARTER : (q % 2 + 1) * QUARTER, :]
-            nc.gpsimd.tensor_tensor(
-                out=h_bf[g, q - q % 2][:, (q % 2) * KP : (q % 2 + 1) * KP].rearrange("p (j r e) -> p j r e", r=2, e=2),
-                in0=m_sb[:].rearrange("p j (r e) -> p j r e", e=2),
-                in1=terms.rearrange("p r j e -> p j r e"),
-                op=ALU.add,
-            )
+            h_part, terms = sum_operands(q, g)
+            nc.gpsimd.tensor_tensor(out=h_part, in0=m_sb.rearrange("p j (r e) -> p j r e", e=2), in1=terms, op=ALU.add)
 
-        def hardiness_in_sbuf(q, g, m):
-            m_sb = held(f"m_sb{q}{g}", [P, P, PACK], F32)
-            nc.scalar.activation(out=m_sb[:], in_=m[:].rearrange("p t j -> p j t"), func=ACT.Copy)
-            return m_sb
+        def hardiness_to_sbuf(m_sb, m):
+            nc.scalar.activation(out=m_sb, in_=m[:].rearrange("p t j -> p j t"), func=ACT.Copy)
 
         def add_hardiness(q, g, m):
-            terms = quad[g, q // 2][:, :, (q % 2) * QUARTER : (q % 2 + 1) * QUARTER, :]
-            nc.vector.tensor_tensor(
-                out=h_bf[g, q - q % 2][:, (q % 2) * KP : (q % 2 + 1) * KP].rearrange("p (j r e) -> p j r e", r=2, e=2),
-                in0=m[:].rearrange("p (r e) j -> p j r e", e=2),
-                in1=terms.rearrange("p r j e -> p j r e"),
-                op=ALU.add,
-            )
+            h_part, terms = sum_operands(q, g)
+            nc.vector.tensor_tensor(out=h_part, in0=m[:].rearrange("p (r e) j -> p j r e", e=2), in1=terms, op=ALU.add)
 
-        def quantise_h(g, q0, q1):
-            h = q0 // 2
-            cols = slice(q0 * P - h * HALF, q1 * P - h * HALF)
-            quantise(h_bf[g, 2 * h][:, (q0 - 2 * h) * KP : (q1 - 2 * h) * KP], h_w[g, h][:, cols], h_s[g, h][:, cols])
-
-        def last_product(y, cols, n, g, start, stop):
-            h = cols.start // HALF
-            within = slice(cols.start - h * HALF, cols.stop - h * HALF)
-            nc.tensor.matmul_mx(
-                out=y,
-                lhsT=w3_w[:, g, n * P : (n + 1) * P].bitcast(FP8X4),
-                lhsT_scale=w3_s[:, g, n * P : (n + 1) * P],
-                rhs=h_w[g, h][:, within].bitcast(FP8X4),
-                rhs_scale=h_s[g, h][:, within],
-                start=start,
-                stop=stop,
-            )
+        def quantise_h(name, first, count):
+            bf, words, scales = h_tiles[name]
+            quantise(bf[:, first * KP : (first + count) * KP], words[:, first * P : (first + count) * P], scales[:, first * P : (first + count) * P])
 
         def damage_pass(ys, cols, g):
+            bf, words, scales = h_tiles[cols.start // HALF]
+            within = slice(g * HALF + cols.start % HALF, g * HALF + cols.start % HALF + cols.stop - cols.start)
             for n, (y, first, final) in enumerate(ys):
-                last_product(y, cols, n, g, start=(g == 0 and first), stop=(g == 1 and final))
+                nc.tensor.matmul_mx(
+                    out=y,
+                    lhsT=w3_w[:, g, n * P : (n + 1) * P].bitcast(FP8X4),
+                    lhsT_scale=w3_s[:, g, n * P : (n + 1) * P],
+                    rhs=words[:, within].bitcast(FP8X4),
+                    rhs_scale=scales[:, within],
+                    start=(g == 0 and first),
+                    stop=(g == 1 and final),
+                )
 
         def add_bias_and_store(ys, y_out, cols):
             for n, (y, first, final) in enumerate(ys):
@@ -306,9 +281,9 @@ def tile_list_frost_risk_map_kernel(
         nc.sync.dma_start(out=w2_w[:].bitcast(I32), in_=w2_words.rearrange("a p c -> p a c").bitcast(I32))
         load_scales(w2_s, w2_scales, nc.sync)
         load_rows(5)
-        load_rows(6)
-        load_w1(1, 0)
         load_rows(7)
+        load_w1(1, 0)
+        load_rows(6)
         load_w1(1, 1)
         nc.sync.dma_start(out=c1_sb[:], in_=c1.rearrange("(g p t) -> p g t", g=PASSES, t=PACK))
         nc.sync.dma_start(out=c2_sb[:], in_=c2.rearrange("(g p t) -> p g t", g=PASSES, t=PACK))
@@ -317,96 +292,97 @@ def tile_list_frost_risk_map_kernel(
         with nc.allow_non_contiguous_dma(reason="one bias value to a partition"):
             nc.sync.dma_start(out=b_sb[:], in_=b.rearrange("(n p) -> p n", p=P))
 
+        whole, halves = slice(0, S), (slice(0, HALF), slice(HALF, S))
         for n in range(PACK):
-            both = picked[n % 2]
-            for e, offsets in enumerate((idx3, idx2)):
-                nc.vector.tensor_copy(out=both[:, e, :], in_=rows[n][:].indirect(offsets[:]))
-            nc.gpsimd.tensor_tensor(out=x0[:, n, :], in0=both[:, 1, :], in1=both[:, 0, :], op=ALU.subtract)
+            differences(n, whole, picked[n % 2][:], x0[:, n, :])
         for g in range(PASSES):
             round_w1(0, g, 0, P)
-        all_columns(4)
-        quantise_w1(0, 0)
+        differences_by_halves(4, picked[0][:])
         for a in range(PASSES):
             gather_words(a)
-        quantise_w1(0, 1)
-        x0_bf = round_x(x0, "x0_bf", tag="w1_pass0")
+        quantise(w1_bf0[:], codes0[:, 0:H], w1_s0[:])
+        x0_bf = held("x0_bf", [P, PACK * S], BF16, tag="w1_pass0")
+        round_x_scalar(x0_bf[:])
         quantise(x0_bf[:], x0_w, x0_s[:])
-        all_columns(5)
         for h in range(2):
             for g in range(PASSES):
                 if (h, g) == (1, 1):
                     round_w1(1, 0, 0, P)
                 for q in (2 * h, 2 * h + 1):
                     hardiness_transposed(q, g)
+        round_w1(1, 1, 0, P)
         m = {(q, g): hardiness(q, g, 2 * g + q) for g in range(PASSES) for q in range(2)}
 
-        all_columns(6)
-        round_w1(1, 1, 0, P // 2)
-        lower7 = held("lower7", [P, HALF], F32, tag="w1_w10")
-        all_columns(7, [lower7[:], lower[1][:, 0:HALF]])
-        x1_bf0 = round_x(x1[0], "x1_bf0", on_vector=True)
+        differences_by_halves(5, picked[1][:])
+        slots = [picked[0][:, :, cols] for cols in halves] + [picked[1][:, :, halves[0]]]
+        differences(7, halves[0], slots[0], x1[0][:, 3, :])
+        differences(6, halves[0], slots[1], x1[0][:, 2, :])
+        differences(6, halves[1], slots[2], x1[1][:, 2, :])
+        x1_bf0 = held("x1_bf0", [P, PACK * HALF], BF16)
+        round_x_vector(0, x1_bf0[:])
+        pick(7, halves[1], slots[1], 0)
+        w1_w[1, 0] = held("w1_w10", [P, KP], U32, tag="x1_first")[:]
+        quantise_w1(1, 0)
         x1_w[0] = held("x1_w0", [P, HALF], U32)
         quantise(x1_bf0[:], x1_w[0][:], x1_s[0][:])
-        w1_w[1, 0] = held("w1_w10", [P, KP], U32)[:]
-        quantise_w1(1, 0)
-        x1_bf1 = round_x(x1[1], "x1_bf1", tag="w1_bf10", on_vector=True)
-        round_w1_vector(1, 1, P // 2, P)
-        x1_w[1] = held("x1_w1", [P, HALF], U32)
-        quantise(x1_bf1[:], x1_w[1][:], x1_s[1][:])
+        nc.vector.tensor_tensor(out=x1[1][:, 3, :], in0=rows[7][:].indirect(idx2[:, HALF // STRIPE :]), in1=slots[1][:, 0, :], op=ALU.subtract)
         w1_w[1, 1] = held("w1_w11", [P, KP], U32)[:]
         quantise_w1(1, 1)
-        m_sb = {(q, g): hardiness_in_sbuf(q, g, m[q, g]) for q, g in ((1, 0), (0, 1))}
+        x1_bf1 = held("x1_bf1", [P, PACK * HALF], BF16, tag="w1_f32_11")
+        round_x_vector(1, x1_bf1[:])
         pairs = {(0, 0): [inner_pair(0, 0, pair, 4 + pair) for pair in range(2)]}
-        m_sb[1, 1] = hardiness_in_sbuf(1, 1, m[1, 1])
+        m_sb = {(1, 0): held("m_sb10", [P, P, PACK], F32, tag="w1_bf11")}
+        hardiness_to_sbuf(m_sb[1, 0][:], m[1, 0])
         pairs[1, 0] = [inner_pair(1, 0, pair, 6 + pair) for pair in range(2)]
-        pairs[0, 1] = [inner_pair(0, 1, pair, 1 + pair) for pair in range(2)]
-        for pair in range(2):
-            outer_pair(0, 0, pair, *pairs[0, 0][pair])
-        add_hardiness_sbuf(1, 0, m_sb[1, 0])
+        outer_pair(0, 0, 0, *pairs[0, 0][0])
+        x1_w[1] = held("x1_w1", [P, HALF], U32)
+        quantise(x1_bf1[:], x1_w[1][:], x1_s[1][:])
+        outer_pair(0, 0, 1, *pairs[0, 0][1])
+        add_hardiness_sbuf(1, 0, m_sb[1, 0][:])
+        m_sb[0, 1] = held("m_sb01", [P, P, PACK], F32, tag="inner000")
+        hardiness_to_sbuf(m_sb[0, 1][:], m[0, 1])
+        pairs[0, 1] = [inner_pair(0, 1, pair, (1, 4)[pair]) for pair in range(2)]
+        outer_pair(1, 0, 0, *pairs[1, 0][0])
         add_hardiness(0, 0, m[0, 0])
-        pairs[1, 1] = [inner_pair(1, 1, pair, 3 + pair) for pair in range(2)]
-        m[2, 0] = hardiness(2, 0, 5)
-        m[3, 0] = hardiness(3, 0, 0)
-        for pair in range(2):
-            outer_pair(1, 0, pair, *pairs[1, 0][pair])
-            if pair == 0:
-                h_w[0, 0] = held("h_w00", [P, HALF], U32, tag="inner100")
-                quantise_h(0, 0, 2)
-        for q in (2, 3):
-            m[q, 1] = hardiness(q, 1, 4 + q)
+        outer_pair(1, 0, 1, *pairs[1, 0][1])
+        quantise_h(0, 0, 2)
+        m_sb[1, 1] = held("m_sb11", [P, P, PACK], F32, tag="inner101")
+        hardiness_to_sbuf(m_sb[1, 1][:], m[1, 1])
+        pairs[1, 1] = [inner_pair(1, 1, pair, (5, 2)[pair]) for pair in range(2)]
         for q in range(2):
-            add_hardiness_sbuf(q, 1, m_sb[q, 1])
+            add_hardiness_sbuf(q, 1, m_sb[q, 1][:])
+        for (q, g), number in (((2, 0), 0), ((3, 0), 6), ((2, 1), 7), ((3, 1), 3)):
+            m[q, g] = hardiness(q, g, number)
         for pair in range(2):
             outer_pair(0, 1, pair, *pairs[0, 1][pair])
-        two, one = bank(1, [P, 2, HALF]), bank(2, [P, HALF])
+        two, one = bank(1, [P, 2, HALF]), bank(4, [P, HALF])
         ys_half = [(two[:, 0, :], True, False), (two[:, 1, :], False, True), (one[:], True, True)]
-        damage_pass(ys_half, slice(0, HALF), 0)
-        add_hardiness(2, 0, m[2, 0])
-        add_hardiness(3, 0, m[3, 0])
+        damage_pass(ys_half, groups[0], 0)
         first, final = slice(0, QUARTER), slice(QUARTER, HALF)
         outer_pair(1, 1, 0, *pairs[1, 1][0], first)
-        h_w[1, 0] = held("h_w10", [P, HALF], U32)
-        quantise_h(1, 0, 2)
-        quantise_h(0, 2, 4)
+        add_hardiness(2, 0, m[2, 0])
+        add_hardiness(3, 0, m[3, 0])
         outer_pair(1, 1, 1, *pairs[1, 1][1], first)
-        damage_pass(ys_half, slice(0, HALF), 1)
-        add_bias_and_store(ys_half, y_half, slice(0, HALF))
+        quantise_h(0, 2, 2)
+        quantise_h(1, 0, 2)
+        damage_pass(ys_half, groups[0], 1)
+        add_bias_and_store(ys_half, y_half, groups[0])
         outer_pair(1, 1, 0, *pairs[1, 1][0], final)
         add_hardiness(2, 1, m[2, 1])
-        three = bank(5, [P, N_TILES, P])
-        ys_third = [(three[:, n, :], n == 0, n == N_TILES - 1) for n in range(N_TILES)]
-        damage_pass(ys_third, slice(HALF, HALF + QUARTER), 0)
-        last = 3
         outer_pair(1, 1, 1, *pairs[1, 1][1], final)
-        ys = [bank(number, [P, P]) for number in (0, 3, 4)]
+        quantise_h(1, 2, 1)
+        three = bank(0, [P, N_TILES, P])
+        ys_third = [(three[:, n, :], n == 0, n == N_TILES - 1) for n in range(N_TILES)]
+        for g in range(PASSES):
+            damage_pass(ys_third, groups[1], g)
+        last = 3
+        ys = [bank(number, [P, P]) for number in (6, 5, 2)]
         ys_last = [(y[:], True, True) for y in ys]
-        damage_pass(ys_last, slice(last * P, S), 0)
-        quantise_h(1, 2, 3)
+        damage_pass(ys_last, groups[2], 0)
         add_hardiness(3, 1, m[3, 1])
-        damage_pass(ys_third, slice(HALF, HALF + QUARTER), 1)
-        add_bias_and_store(ys_third, y_sb[2], slice(HALF, HALF + QUARTER))
-        quantise_h(1, last, last + 1)
-        damage_pass(ys_last, slice(last * P, S), 1)
+        add_bias_and_store(ys_third, y_sb[2], groups[1])
+        quantise_h(1, 3, 1)
+        damage_pass(ys_last, groups[2], 1)
         nc.vector.tensor_scalar_add(out=y_sb[last][:, 0, :], in0=ys[0][:], scalar1=b_sb[:, 0:1])
         nc.scalar.activation(out=y_sb[last][:, 1, :], in_=ys[1][:], func=ACT.Identity, bias=b_sb[:, 1:2])
         nc.vector.tensor_scalar_add(out=y_sb[last][:, 2, :], in0=ys[2][:], scalar1=b_sb[:, 2:3])

@@ -90,7 +90,7 @@ def tile_list_frost_risk_map_kernel(
             m_t[q, 1] = m_t_last[:, q - 2]
         quad = {(g, h): held(f"quad{g}{h}", [P, 2, HALF, 2], F32) for g in range(PASSES) for h in range(2)}
         h_tiles = [
-            (held(f"h_bf{h}", [P, 4 * KP], BF16, tag=f"h_bf{h}"), held(f"h_w{h}", [P, 4 * P], U32), held(f"h_s{h}", [P, 4 * P], U8))
+            (held(f"h_bf{h}", [P, 4 * KP], BF16, tag=f"h_bf{h}"), held(f"h_w{h}", [P, 4 * P], U32, tag=f"h_w{h}"), held(f"h_s{h}", [P, 4 * P], U8))
             for h in range(2)
         ]
         groups = (slice(0, HALF), slice(HALF, HALF + QUARTER), slice(HALF + QUARTER, S))
@@ -138,6 +138,14 @@ def tile_list_frost_risk_map_kernel(
             for h in range(2):
                 cols = slice(h * HALF, (h + 1) * HALF)
                 nc.gpsimd.tensor_tensor(out=x1[h][:, n - PACK, :], in0=scratch[:, 1, cols], in1=scratch[:, 0, cols], op=ALU.subtract)
+
+        def fused_difference(n, lower_values):
+            nc.vector.tensor_tensor(
+                out=x1[1][:, n - PACK, :],
+                in0=rows[n][:].indirect(idx2[:, HALF // STRIPE :]),
+                in1=lower_values,
+                op=ALU.subtract,
+            )
 
         def round_x_scalar(x_bf):
             nc.scalar.activation(
@@ -224,8 +232,11 @@ def tile_list_frost_risk_map_kernel(
                 op=ALU.mult,
             )
 
+        def bf_place(h, place):
+            return place % 2 if h == 0 else place
+
         def sum_operands(q, g):
-            place = 2 * g + q % 2
+            place = bf_place(q // 2, 2 * g + q % 2)
             h_part = h_tiles[q // 2][0][:, place * KP : (place + 1) * KP].rearrange("p (j r e) -> p j r e", r=2, e=2)
             terms = quad[g, q // 2][:, :, (q % 2) * QUARTER : (q % 2 + 1) * QUARTER, :]
             return h_part, terms.rearrange("p r j e -> p j r e")
@@ -243,7 +254,8 @@ def tile_list_frost_risk_map_kernel(
 
         def quantise_h(name, first, count):
             bf, words, scales = h_tiles[name]
-            quantise(bf[:, first * KP : (first + count) * KP], words[:, first * P : (first + count) * P], scales[:, first * P : (first + count) * P])
+            start = bf_place(name, first) * KP
+            quantise(bf[:, start : start + count * KP], words[:, first * P : (first + count) * P], scales[:, first * P : (first + count) * P])
 
         def damage_pass(ys, cols, g):
             bf, words, scales = h_tiles[cols.start // HALF]
@@ -314,25 +326,27 @@ def tile_list_frost_risk_map_kernel(
         m = {(q, g): hardiness(q, g, 2 * g + q) for g in range(PASSES) for q in range(2)}
 
         differences_by_halves(5, picked[1][:])
-        slots = [picked[0][:, :, cols] for cols in halves] + [picked[1][:, :, halves[0]]]
+        slots = [picked[0][:, :, cols] for cols in halves]
         differences(7, halves[0], slots[0], x1[0][:, 3, :])
+        lower = held("lower", [P, 2, HALF], F32)
+        pick(7, halves[1], lower[:, 1:2, :], 0)
         differences(6, halves[0], slots[1], x1[0][:, 2, :])
-        differences(6, halves[1], slots[2], x1[1][:, 2, :])
+        pick(6, halves[1], lower[:, 0:1, :], 0)
+        fused_difference(6, lower[:, 0, :])
         x1_bf0 = held("x1_bf0", [P, PACK * HALF], BF16)
         round_x_vector(0, x1_bf0[:])
-        pick(7, halves[1], slots[1], 0)
-        w1_w[1, 0] = held("w1_w10", [P, KP], U32, tag="x1_first")[:]
+        w1_w[1, 0] = held("w1_w10", [P, KP], U32)[:]
         quantise_w1(1, 0)
         x1_w[0] = held("x1_w0", [P, HALF], U32)
         quantise(x1_bf0[:], x1_w[0][:], x1_s[0][:])
-        nc.vector.tensor_tensor(out=x1[1][:, 3, :], in0=rows[7][:].indirect(idx2[:, HALF // STRIPE :]), in1=slots[1][:, 0, :], op=ALU.subtract)
+        fused_difference(7, lower[:, 1, :])
         w1_w[1, 1] = held("w1_w11", [P, KP], U32)[:]
         quantise_w1(1, 1)
         x1_bf1 = held("x1_bf1", [P, PACK * HALF], BF16, tag="w1_f32_11")
         round_x_vector(1, x1_bf1[:])
-        pairs = {(0, 0): [inner_pair(0, 0, pair, 4 + pair) for pair in range(2)]}
-        m_sb = {(1, 0): held("m_sb10", [P, P, PACK], F32, tag="w1_bf11")}
+        m_sb = {(1, 0): held("m_sb10", [P, P, PACK], F32)}
         hardiness_to_sbuf(m_sb[1, 0][:], m[1, 0])
+        pairs = {(0, 0): [inner_pair(0, 0, pair, 4 + pair) for pair in range(2)]}
         pairs[1, 0] = [inner_pair(1, 0, pair, 6 + pair) for pair in range(2)]
         outer_pair(0, 0, 0, *pairs[0, 0][0])
         x1_w[1] = held("x1_w1", [P, HALF], U32)
@@ -363,11 +377,11 @@ def tile_list_frost_risk_map_kernel(
         add_hardiness(2, 0, m[2, 0])
         add_hardiness(3, 0, m[3, 0])
         outer_pair(1, 1, 1, *pairs[1, 1][1], first)
+        outer_pair(1, 1, 0, *pairs[1, 1][0], final)
         quantise_h(0, 2, 2)
         quantise_h(1, 0, 2)
         damage_pass(ys_half, groups[0], 1)
         add_bias_and_store(ys_half, y_half, groups[0])
-        outer_pair(1, 1, 0, *pairs[1, 1][0], final)
         add_hardiness(2, 1, m[2, 1])
         outer_pair(1, 1, 1, *pairs[1, 1][1], final)
         quantise_h(1, 2, 1)

@@ -284,14 +284,15 @@ def tile_list_frost_risk_map_kernel(
         load_rows(1)
         load_rows(2)
         load_rows(3)
-        nc.sync.dma_start(out=w1_pass0[:], in_=w1[0:KP, :].rearrange("(p i) c -> p i c", i=PACK))
         nc.vector.tensor_copy(out=v_rows[:], in_=tab_s[:].indirect(idx[:]))
+        place_gathered_scales(0)
+        nc.sync.dma_start(out=w1_pass0[:], in_=w1[0:KP, :].rearrange("(p i) c -> p i c", i=PACK))
+        place_gathered_scales(1)
         load_rows(4)
-        for a in range(PASSES):
-            place_gathered_scales(a)
-            load_table(a)
-        nc.sync.dma_start(out=w2_w[:].bitcast(I32), in_=w2_words.rearrange("a p c -> p a c").bitcast(I32))
+        load_table(0)
         load_scales(w2_s, w2_scales, nc.sync)
+        load_table(1)
+        nc.sync.dma_start(out=w2_w[:].bitcast(I32), in_=w2_words.rearrange("a p c -> p a c").bitcast(I32))
         load_rows(5)
         load_rows(7)
         load_w1(1, 0)
@@ -344,9 +345,9 @@ def tile_list_frost_risk_map_kernel(
         quantise_w1(1, 1)
         x1_bf1 = held("x1_bf1", [P, PACK * HALF], BF16, tag="w1_f32_11")
         round_x_vector(1, x1_bf1[:])
-        m_sb = {(1, 0): held("m_sb10", [P, P, PACK], F32)}
-        hardiness_to_sbuf(m_sb[1, 0][:], m[1, 0])
         pairs = {(0, 0): [inner_pair(0, 0, pair, 4 + pair) for pair in range(2)]}
+        m_sb = {(1, 0): held("m_sb10", [P, P, PACK], F32, tag="w1_bf11")}
+        hardiness_to_sbuf(m_sb[1, 0][:], m[1, 0])
         pairs[1, 0] = [inner_pair(1, 0, pair, 6 + pair) for pair in range(2)]
         outer_pair(0, 0, 0, *pairs[0, 0][0])
         x1_w[1] = held("x1_w1", [P, HALF], U32)

@@ -85,9 +85,8 @@ def tile_list_frost_risk_map_kernel(
         w1_bf[1, 0] = x1_second[:, (PACK - 1) * HALF :].bitcast(BF16)
         x1_w, x1_s = {}, {h: held(f"x1_s{h}", [P, HALF], U8) for h in range(2)}
         m_t = {(q, g): held(f"m_t{q}{g}", [P, PACK, P], F32)[:] for q in range(4) for g in range(PASSES) if (q // 2, g) != (1, 1)}
-        m_t_last = held("m_t_last", [P, 2, PACK, P], F32, tag="w1_f32_10")
         for q in (2, 3):
-            m_t[q, 1] = m_t_last[:, q - 2]
+            m_t[q, 1] = held(f"m_t{q}1", [P, PACK, P], F32)[:]
         quad = {(g, h): held(f"quad{g}{h}", [P, 2, HALF, 2], F32) for g in range(PASSES) for h in range(2)}
         h_tiles = [
             (held(f"h_bf{h}", [P, 4 * KP], BF16, tag=f"h_bf{h}"), held(f"h_w{h}", [P, 4 * P], U32, tag=f"h_w{h}"), held(f"h_s{h}", [P, 4 * P], U8))
@@ -177,8 +176,8 @@ def tile_list_frost_risk_map_kernel(
         def gather_words(a):
             nc.vector.tensor_copy(out=v_w[a][:], in_=tab_w[a][:].bitcast(U32).indirect(idx[:]))
 
-        def hardiness_transposed(q, g):
-            sums = bank(4 * (q // 2) + 2 * g + q % 2, [P, KP])
+        def hardiness_transposed(q, g, number):
+            sums = bank(number, [P, KP])
             for a in (1, 0):
                 nc.tensor.matmul_mx(
                     out=sums[:],
@@ -317,14 +316,13 @@ def tile_list_frost_risk_map_kernel(
         x0_bf = held("x0_bf", [P, PACK * S], BF16, tag="w1_pass0")
         round_x_scalar(x0_bf[:])
         quantise(x0_bf[:], x0_w, x0_s[:])
-        for h in range(2):
-            for g in range(PASSES):
-                if (h, g) == (1, 1):
-                    round_w1(1, 0, 0, P)
-                for q in (2 * h, 2 * h + 1):
-                    hardiness_transposed(q, g)
-        round_w1(1, 1, 0, P)
+        for number, (q, g) in enumerate(((0, 0), (1, 0), (0, 1), (1, 1), (2, 0), (3, 0))):
+            hardiness_transposed(q, g, number)
+        round_w1(1, 0, 0, P)
         m = {(q, g): hardiness(q, g, 2 * g + q) for g in range(PASSES) for q in range(2)}
+        m_sb = {(1, 0): held("m_sb10", [P, P, PACK], F32, tag="w1_f32_10")}
+        hardiness_to_sbuf(m_sb[1, 0][:], m[1, 0])
+        round_w1(1, 1, 0, P)
 
         differences_by_halves(5, picked[1][:])
         slots = [picked[0][:, :, cols] for cols in halves]
@@ -346,8 +344,6 @@ def tile_list_frost_risk_map_kernel(
         x1_bf1 = held("x1_bf1", [P, PACK * HALF], BF16, tag="w1_f32_11")
         round_x_vector(1, x1_bf1[:])
         pairs = {(0, 0): [inner_pair(0, 0, pair, 4 + pair) for pair in range(2)]}
-        m_sb = {(1, 0): held("m_sb10", [P, P, PACK], F32, tag="w1_bf11")}
-        hardiness_to_sbuf(m_sb[1, 0][:], m[1, 0])
         pairs[1, 0] = [inner_pair(1, 0, pair, 6 + pair) for pair in range(2)]
         outer_pair(0, 0, 0, *pairs[0, 0][0])
         x1_w[1] = held("x1_w1", [P, HALF], U32)
@@ -366,8 +362,12 @@ def tile_list_frost_risk_map_kernel(
         pairs[1, 1] = [inner_pair(1, 1, pair, (5, 2)[pair]) for pair in range(2)]
         for q in range(2):
             add_hardiness_sbuf(q, 1, m_sb[q, 1][:])
-        for (q, g), number in (((2, 0), 0), ((3, 0), 6), ((2, 1), 7), ((3, 1), 3)):
-            m[q, g] = hardiness(q, g, number)
+        m[2, 0] = hardiness(2, 0, 0)
+        m[3, 0] = hardiness(3, 0, 6)
+        hardiness_transposed(2, 1, 7)
+        hardiness_transposed(3, 1, 3)
+        m[2, 1] = hardiness(2, 1, 7)
+        m[3, 1] = hardiness(3, 1, 3)
         for pair in range(2):
             outer_pair(0, 1, pair, *pairs[0, 1][pair])
         two, one = bank(1, [P, 2, HALF]), bank(4, [P, HALF])

@@ -24,9 +24,12 @@ PASSES = 2
 HALF = S // 2
 QUARTER = S // 4
 N_TILES = N // P
-QUADRANTS = 4
+QUADRANT = 32
+SCALE_ROWS = 4
+BLOCKS = 16
 STRIPE = 16
 RUN = 4
+PLACES = 4
 ALIGN = 256
 
 
@@ -65,8 +68,8 @@ def tile_list_frost_risk_map_kernel(
         ident = held("ident", [P, P], F32)
         w1_pass0 = held("w1_pass0", [P, PACK, H], F32)
         w1_f32 = {(0, g): w1_pass0[:, :, g * KP : (g + 1) * KP] for g in range(PASSES)}
-        for g in range(PASSES):
-            w1_f32[1, g] = held(f"w1_f32_1{g}", [P, PACK, KP], F32)[:]
+        w1_f32[1, 0] = held("w1_f32_10", [P, PACK, KP], F32)[:]
+        w1_last = [held(f"w1_last{n}", [P, PACK, HALF], F32) for n in range(2)]
         w1_s0 = held("w1_s0", [P, H], U8)
         codes0 = held("codes0", [P, H + S], U32, tag="tab_w1")
         w1_w = {(0, g): codes0[:, g * KP : (g + 1) * KP] for g in range(PASSES)}
@@ -83,60 +86,69 @@ def tile_list_frost_risk_map_kernel(
         x1 = [x1_first[:], x1_second[:, 0 : PACK * HALF].rearrange("p (i c) -> p i c", i=PACK)]
         x0_w, x0_s = codes0[:, H : H + S], held("x0_s", [P, S], U8)
         w1_bf[1, 0] = x1_second[:, (PACK - 1) * HALF :].bitcast(BF16)
-        x1_w, x1_s = {}, {h: held(f"x1_s{h}", [P, HALF], U8) for h in range(2)}
-        m_t = {(q, g): held(f"m_t{q}{g}", [P, PACK, P], F32)[:] for q in range(4) for g in range(PASSES) if (q // 2, g) != (1, 1)}
-        for q in (2, 3):
-            m_t[q, 1] = held(f"m_t{q}1", [P, PACK, P], F32)[:]
-        quad = {(g, h): held(f"quad{g}{h}", [P, 2, HALF, 2], F32) for g in range(PASSES) for h in range(2)}
+        x1_w, x1_s = {}, {half: held(f"x1_s{half}", [P, HALF], U8) for half in range(2)}
+        late_m = ((2, 1), (3, 1))
+        early_m = [(q, g) for q in range(4) for g in range(PASSES) if (q, g) not in late_m]
+        m_t = {(q, g): held(f"m_t{q}{g}", [P, PACK, P], F32)[:] for q, g in early_m + list(late_m)}
+        quad = {(g, half): held(f"quad{g}{half}", [P, 2, HALF, 2], F32) for g in range(PASSES) for half in range(2)}
         h_tiles = [
-            (held(f"h_bf{h}", [P, 4 * KP], BF16, tag=f"h_bf{h}"), held(f"h_w{h}", [P, 4 * P], U32, tag=f"h_w{h}"), held(f"h_s{h}", [P, 4 * P], U8))
-            for h in range(2)
+            (
+                held(f"h_bf{half}", [P, PLACES * KP], BF16),
+                held(f"h_w{half}", [P, PLACES * P], U32),
+                held(f"h_s{half}", [P, PLACES * P], U8),
+            )
+            for half in range(2)
         ]
         groups = (slice(0, HALF), slice(HALF, HALF + QUARTER), slice(HALF + QUARTER, S))
         y_half = held("y_half", [P, N_TILES, HALF], F32)
         y_sb = {q: held(f"y_sb{q}", [P, N_TILES, P], F32) for q in (2, 3)}
 
-        nc.vector.memset(tab_s[64:P, :].bitcast(I32), 0)
-        for part in (tab_s[32:64, :], v_s[0][:], v_s[1][:], w2_s[:], w3_s[:]):
+        nc.vector.memset(tab_s[2 * QUADRANT : P, :].bitcast(I32), 0)
+        for part in (tab_s[QUADRANT : 2 * QUADRANT, :], v_s[0][:], v_s[1][:], w2_s[:], w3_s[:]):
             nc.gpsimd.memset(part.bitcast(I32), 0)
         make_identity(nc, ident[:])
 
-        def load_rows(n, cols=slice(0, T2)):
+        def load_rows(n):
             a, i = divmod(n, PACK)
-            nc.sync.dma_start(out=rows[n][:, cols], in_=xT[a * KP : (a + 1) * KP, :].rearrange("(p i) t -> p i t", i=PACK)[:, i, cols])
+            part = xT[a * KP : (a + 1) * KP, :].rearrange("(p i) t -> p i t", i=PACK)
+            nc.sync.dma_start(out=rows[n][:], in_=part[:, i, :])
 
         def load_table(a):
             nc.sync.dma_start(out=tab_w[a][:], in_=tab_words[a].rearrange("p t i -> p (t i)").bitcast(I32))
 
-        def load_w1(a, g):
-            part = w1[a * KP : (a + 1) * KP, g * KP : (g + 1) * KP]
-            nc.sync.dma_start(out=w1_f32[a, g], in_=part.rearrange("(p i) c -> p i c", i=PACK))
+        def load_w1(tile, a, channels):
+            part = w1[a * KP : (a + 1) * KP, channels]
+            nc.sync.dma_start(out=tile, in_=part.rearrange("(p i) c -> p i c", i=PACK))
 
-        def load_scales(tile, scales, queue):
-            for r in range(4):
-                part = scales[:, r:16:4, :].rearrange("a n c -> n a c")
-                queue.dma_start(out=tile[r:P:32, :, :].bitcast(I32), in_=part.bitcast(I32))
+        def load_scales(tile, scales):
+            for row in range(SCALE_ROWS):
+                part = scales[:, row:BLOCKS:SCALE_ROWS, :].rearrange("a n c -> n a c")
+                nc.sync.dma_start(out=tile[row:P:QUADRANT, :, :].bitcast(I32), in_=part.bitcast(I32))
 
         def place_gathered_scales(a):
-            for r in range(4):
-                part = v_rows[16 * a + r : 16 * a + 16 : 4, :]
-                nc.sync.dma_start(out=v_s[a][r:P:32, :].bitcast(I32), in_=part.bitcast(I32))
+            for row in range(SCALE_ROWS):
+                part = v_rows[BLOCKS * a + row : BLOCKS * (a + 1) : SCALE_ROWS, :]
+                nc.sync.dma_start(out=v_s[a][row:P:QUADRANT, :].bitcast(I32), in_=part.bitcast(I32))
 
-        def pick(n, cols, scratch, e):
+        def pick(n, offsets, cols, values):
             entries = slice(cols.start // STRIPE, cols.stop // STRIPE)
-            nc.vector.tensor_copy(out=scratch[:, e, :], in_=rows[n][:].indirect((idx3, idx2)[e][:, entries]))
+            nc.vector.tensor_copy(out=values, in_=rows[n][:].indirect(offsets[:, entries]))
 
-        def differences(n, cols, scratch, x_out):
-            for e in range(2):
-                pick(n, cols, scratch, e)
-            nc.gpsimd.tensor_tensor(out=x_out, in0=scratch[:, 1, :], in1=scratch[:, 0, :], op=ALU.subtract)
+        def pick_both(n, cols, both):
+            for e, offsets in enumerate((idx3, idx2)):
+                pick(n, offsets, cols, both[:, e, :])
 
-        def differences_by_halves(n, scratch):
-            for e in range(2):
-                pick(n, slice(0, S), scratch, e)
-            for h in range(2):
-                cols = slice(h * HALF, (h + 1) * HALF)
-                nc.gpsimd.tensor_tensor(out=x1[h][:, n - PACK, :], in0=scratch[:, 1, cols], in1=scratch[:, 0, cols], op=ALU.subtract)
+        def subtract(both, x_out):
+            nc.gpsimd.tensor_tensor(out=x_out, in0=both[:, 1, :], in1=both[:, 0, :], op=ALU.subtract)
+
+        def differences(n, cols, both, x_out):
+            pick_both(n, cols, both)
+            subtract(both, x_out)
+
+        def differences_by_halves(n, both):
+            pick_both(n, whole, both)
+            for half in range(2):
+                subtract(both[:, :, halves[half]], x1[half][:, n - PACK, :])
 
         def fused_difference(n, lower_values):
             nc.vector.tensor_tensor(
@@ -146,27 +158,26 @@ def tile_list_frost_risk_map_kernel(
                 op=ALU.subtract,
             )
 
-        def round_x_scalar(x_bf):
+        def round_x0(x_bf):
             nc.scalar.activation(
                 out=x_bf.rearrange("p (c e i) -> p c i e", e=RUN, i=PACK),
                 in_=x0[:].rearrange("p i (c e) -> p c i e", e=RUN),
                 func=ACT.Copy,
             )
 
-        def round_x_vector(h, x_bf):
+        def round_x1(half, x_bf):
             nc.vector.tensor_copy(
                 out=x_bf.rearrange("p (c i) -> p c i", i=PACK),
-                in_=x1[h].rearrange("p i c -> p c i"),
+                in_=x1[half].rearrange("p i c -> p c i"),
             )
 
         def quantise(bf, words, scales):
             nc.vector.quantize_mx(out=words.bitcast(FP8X4), scales=scales, in_=bf)
 
-        def round_w1(a, g, m0, m1):
-            part = w1_f32[a, g]
+        def round_w1(a, g, part, words=slice(0, P)):
             nc.scalar.activation(
-                out=w1_bf[a, g].rearrange("p (t m i) -> p m i t", t=PACK, i=PACK)[:, m0:m1, :, :],
-                in_=part.rearrange("p i (m t) -> p m i t", t=PACK)[:, m0:m1, :, :],
+                out=w1_bf[a, g].rearrange("p (t u i) -> p u i t", t=PACK, i=PACK)[:, words, :, :],
+                in_=part.rearrange("p i (u t) -> p u i t", t=PACK),
                 func=ACT.Copy,
             )
 
@@ -188,16 +199,16 @@ def tile_list_frost_risk_map_kernel(
                     start=(a == 1),
                     stop=(a == 0),
                 )
-            nc.scalar.activation(out=m_t[q, g], in_=sums[:].rearrange("p (m t) -> p t m", t=PACK), func=ACT.Copy)
+            nc.scalar.activation(out=m_t[q, g], in_=sums[:].rearrange("j (p t) -> j t p", t=PACK), func=ACT.Copy)
 
         def hardiness(q, g, number):
-            m = bank(number, [P, PACK, P])
+            turned = bank(number, [P, PACK, P])
             for t in range(PACK):
-                nc.tensor.transpose(m[:, t, :], m_t[q, g][:, t, :], ident[:])
-            return m
+                nc.tensor.transpose(turned[:, t, :], m_t[q, g][:, t, :], ident[:])
+            return turned
 
-        def response(d, a, g, t, cols, start, stop):
-            x_w, x_s = (x0_w[:, cols], x0_s[:, cols]) if a == 0 else (x1_w[cols.start // HALF][:], x1_s[cols.start // HALF][:])
+        def response(d, a, g, t, half, start, stop):
+            x_w, x_s = (x0_w[:, halves[half]], x0_s[:, halves[half]]) if a == 0 else (x1_w[half][:], x1_s[half][:])
             nc.tensor.matmul_mx(
                 out=d,
                 lhsT=w1_w[a, g][:, t * P : (t + 1) * P].bitcast(FP8X4),
@@ -213,127 +224,144 @@ def tile_list_frost_risk_map_kernel(
                 out=inner, in_=d, func=ACT.Identity, scale=c2_sb[:, g, t : t + 1], bias=c1_sb[:, g, t : t + 1]
             )
 
-        def inner_pair(g, h, pair, number):
+        def inner_pair(g, half, pair, number):
             d = bank(number, [P, 2, HALF])
-            inner = held(f"inner{g}{h}{pair}", [P, 2, HALF], F32)
+            inner = held(f"inner{g}{half}{pair}", [P, 2, HALF], F32)
             for a in range(PASSES):
                 for e in range(2):
-                    response(d[:, e, :], a, g, 2 * pair + e, slice(h * HALF, (h + 1) * HALF), a + e == 0, a + e == 2)
+                    response(d[:, e, :], a, g, 2 * pair + e, half, (a, e) == (0, 0), (a, e) == (1, 1))
             for e in range(2):
                 inner_step(inner[:, e, :], d[:, e, :], g, 2 * pair + e)
             return d, inner
 
-        def outer_pair(g, h, pair, d, inner, cols=slice(0, HALF)):
+        def outer_pair(g, half, pair, cols=slice(0, HALF)):
+            d, inner = pairs[g, half][pair]
             nc.vector.tensor_tensor(
-                out=quad[g, h][:, pair, cols, :],
+                out=quad[g, half][:, pair, cols, :],
                 in0=d[:, :, cols].rearrange("p e j -> p j e"),
                 in1=inner[:, :, cols].rearrange("p e j -> p j e"),
                 op=ALU.mult,
             )
 
-        def bf_place(h, place):
-            return place % 2 if h == 0 else place
+        def rounded_place(half, place):
+            return place % 2 if half == 0 else place
 
         def sum_operands(q, g):
-            place = bf_place(q // 2, 2 * g + q % 2)
-            h_part = h_tiles[q // 2][0][:, place * KP : (place + 1) * KP].rearrange("p (j r e) -> p j r e", r=2, e=2)
+            place = rounded_place(q // 2, 2 * g + q % 2)
+            h_part = h_tiles[q // 2][0][:, place * KP : (place + 1) * KP]
             terms = quad[g, q // 2][:, :, (q % 2) * QUARTER : (q % 2 + 1) * QUARTER, :]
-            return h_part, terms.rearrange("p r j e -> p j r e")
+            h_part = h_part.rearrange("p (j pair e) -> p j pair e", pair=2, e=2)
+            return h_part, terms.rearrange("p pair j e -> p j pair e")
 
-        def add_hardiness_sbuf(q, g, m_sb):
+        def hardiness_to_sbuf(q, g, tag):
+            m_sb[q, g] = held(f"m_sb{q}{g}", [P, P, PACK], F32, tag=tag)
+            nc.scalar.activation(out=m_sb[q, g][:], in_=m[q, g][:].rearrange("p t j -> p j t"), func=ACT.Copy)
+
+        def add_hardiness_gpsimd(q, g):
             h_part, terms = sum_operands(q, g)
-            nc.gpsimd.tensor_tensor(out=h_part, in0=m_sb.rearrange("p j (r e) -> p j r e", e=2), in1=terms, op=ALU.add)
+            m_part = m_sb[q, g][:].rearrange("p j (pair e) -> p j pair e", e=2)
+            nc.gpsimd.tensor_tensor(out=h_part, in0=m_part, in1=terms, op=ALU.add)
 
-        def hardiness_to_sbuf(m_sb, m):
-            nc.scalar.activation(out=m_sb, in_=m[:].rearrange("p t j -> p j t"), func=ACT.Copy)
-
-        def add_hardiness(q, g, m):
+        def add_hardiness(q, g):
             h_part, terms = sum_operands(q, g)
-            nc.vector.tensor_tensor(out=h_part, in0=m[:].rearrange("p (r e) j -> p j r e", e=2), in1=terms, op=ALU.add)
+            m_part = m[q, g][:].rearrange("p (pair e) j -> p j pair e", e=2)
+            nc.vector.tensor_tensor(out=h_part, in0=m_part, in1=terms, op=ALU.add)
 
-        def quantise_h(name, first, count):
-            bf, words, scales = h_tiles[name]
-            start = bf_place(name, first) * KP
-            quantise(bf[:, start : start + count * KP], words[:, first * P : (first + count) * P], scales[:, first * P : (first + count) * P])
+        def quantise_h(half, place, count):
+            rounded, words, scales = h_tiles[half]
+            start = rounded_place(half, place) * KP
+            cols = slice(place * P, (place + count) * P)
+            quantise(rounded[:, start : start + count * KP], words[:, cols], scales[:, cols])
 
         def damage_pass(ys, cols, g):
-            bf, words, scales = h_tiles[cols.start // HALF]
-            within = slice(g * HALF + cols.start % HALF, g * HALF + cols.start % HALF + cols.stop - cols.start)
-            for n, (y, first, final) in enumerate(ys):
+            words, scales = h_tiles[cols.start // HALF][1:]
+            begin = g * HALF + cols.start % HALF
+            within = slice(begin, begin + cols.stop - cols.start)
+            for n, (y, opens, closes) in enumerate(ys):
                 nc.tensor.matmul_mx(
                     out=y,
                     lhsT=w3_w[:, g, n * P : (n + 1) * P].bitcast(FP8X4),
                     lhsT_scale=w3_s[:, g, n * P : (n + 1) * P],
                     rhs=words[:, within].bitcast(FP8X4),
                     rhs_scale=scales[:, within],
-                    start=(g == 0 and first),
-                    stop=(g == 1 and final),
+                    start=(g == 0 and opens),
+                    stop=(g == 1 and closes),
                 )
 
         def add_bias_and_store(ys, y_out, cols):
-            for n, (y, first, final) in enumerate(ys):
-                nc.scalar.activation(out=y_out[:, n, :], in_=y, func=ACT.Identity, bias=b_sb[:, n : n + 1])
+            for n in range(N_TILES):
+                nc.scalar.activation(out=y_out[:, n, :], in_=ys[n][0], func=ACT.Identity, bias=b_sb[:, n : n + 1])
                 nc.sync.dma_start(out=out[n * P : (n + 1) * P, cols], in_=y_out[:, n, :])
 
-        nc.sync.dma_start(out=tab_s[0:32, :].bitcast(I32), in_=tab_scales.rearrange("a n t -> (a n) t").bitcast(I32))
+        whole, halves = slice(0, S), (slice(0, HALF), slice(HALF, S))
+        pairs, m, m_sb = {}, {}, {}
+
+        nc.sync.dma_start(
+            out=tab_s[0 : PASSES * BLOCKS, :].bitcast(I32), in_=tab_scales.rearrange("a n t -> (a n) t").bitcast(I32)
+        )
         nc.sync.dma_start(idx[:], offs)
         load_rows(0)
         nc.sync.dma_start(idx3[:], offs3)
         nc.sync.dma_start(idx2[:], offs2)
-        load_rows(1)
-        load_rows(2)
-        load_rows(3)
+        for n in range(1, PACK):
+            load_rows(n)
         nc.vector.tensor_copy(out=v_rows[:], in_=tab_s[:].indirect(idx[:]))
         place_gathered_scales(0)
-        nc.sync.dma_start(out=w1_pass0[:], in_=w1[0:KP, :].rearrange("(p i) c -> p i c", i=PACK))
+        load_w1(w1_pass0[:], 0, slice(0, H))
         place_gathered_scales(1)
         load_rows(4)
         load_table(0)
-        load_scales(w2_s, w2_scales, nc.sync)
+        load_scales(w2_s, w2_scales)
         load_table(1)
         nc.sync.dma_start(out=w2_w[:].bitcast(I32), in_=w2_words.rearrange("a p c -> p a c").bitcast(I32))
         load_rows(5)
         load_rows(7)
-        load_w1(1, 0)
+        load_w1(w1_f32[1, 0], 1, slice(0, KP))
         load_rows(6)
-        load_w1(1, 1)
+        for n in range(2):
+            load_w1(w1_last[n][:], 1, slice(KP + n * HALF, KP + (n + 1) * HALF))
         nc.sync.dma_start(out=c1_sb[:], in_=c1.rearrange("(g p t) -> p g t", g=PASSES, t=PACK))
         nc.sync.dma_start(out=c2_sb[:], in_=c2.rearrange("(g p t) -> p g t", g=PASSES, t=PACK))
         nc.sync.dma_start(out=w3_w[:], in_=w3_words.rearrange("a p c i -> p a (c i)").bitcast(I32))
-        load_scales(w3_s, w3_scales, nc.sync)
+        load_scales(w3_s, w3_scales)
         with nc.allow_non_contiguous_dma(reason="one bias value to a partition"):
             nc.sync.dma_start(out=b_sb[:], in_=b.rearrange("(n p) -> p n", p=P))
 
-        whole, halves = slice(0, S), (slice(0, HALF), slice(HALF, S))
         for n in range(PACK):
             differences(n, whole, picked[n % 2][:], x0[:, n, :])
         for g in range(PASSES):
-            round_w1(0, g, 0, P)
+            round_w1(0, g, w1_f32[0, g])
         differences_by_halves(4, picked[0][:])
         for a in range(PASSES):
             gather_words(a)
         quantise(w1_bf0[:], codes0[:, 0:H], w1_s0[:])
         x0_bf = held("x0_bf", [P, PACK * S], BF16, tag="w1_pass0")
-        round_x_scalar(x0_bf[:])
+        round_x0(x0_bf[:])
         quantise(x0_bf[:], x0_w, x0_s[:])
-        for number, (q, g) in enumerate(((0, 0), (1, 0), (0, 1), (1, 1), (2, 0), (3, 0))):
-            hardiness_transposed(q, g, number)
-        round_w1(1, 0, 0, P)
-        m = {(q, g): hardiness(q, g, 2 * g + q) for g in range(PASSES) for q in range(2)}
-        m_sb = {(1, 0): held("m_sb10", [P, P, PACK], F32, tag="w1_f32_10")}
-        hardiness_to_sbuf(m_sb[1, 0][:], m[1, 0])
-        round_w1(1, 1, 0, P)
+
+        for half in range(2):
+            for g in range(PASSES):
+                for q in (2 * half, 2 * half + 1):
+                    if (q, g) in early_m:
+                        hardiness_transposed(q, g, PLACES * half + 2 * g + q % 2)
+        round_w1(1, 0, w1_f32[1, 0])
+        for g in range(PASSES):
+            for q in range(2):
+                m[q, g] = hardiness(q, g, 2 * g + q)
+        for n in range(2):
+            round_w1(1, 1, w1_last[n][:], slice(n * P // 2, (n + 1) * P // 2))
+        hardiness_to_sbuf(1, 0, "w1_last0")
+        hardiness_to_sbuf(0, 1, "w1_f32_10")
 
         differences_by_halves(5, picked[1][:])
-        slots = [picked[0][:, :, cols] for cols in halves]
-        differences(7, halves[0], slots[0], x1[0][:, 3, :])
+        differences(7, halves[0], picked[0][:, :, halves[0]], x1[0][:, 3, :])
         lower = held("lower", [P, 2, HALF], F32)
-        pick(7, halves[1], lower[:, 1:2, :], 0)
-        differences(6, halves[0], slots[1], x1[0][:, 2, :])
-        pick(6, halves[1], lower[:, 0:1, :], 0)
+        pick(7, idx3, halves[1], lower[:, 1, :])
+        differences(6, halves[0], picked[0][:, :, halves[1]], x1[0][:, 2, :])
+        pick(6, idx3, halves[1], lower[:, 0, :])
         fused_difference(6, lower[:, 0, :])
         x1_bf0 = held("x1_bf0", [P, PACK * HALF], BF16)
-        round_x_vector(0, x1_bf0[:])
+        round_x1(0, x1_bf0[:])
         w1_w[1, 0] = held("w1_w10", [P, KP], U32)[:]
         quantise_w1(1, 0)
         x1_w[0] = held("x1_w0", [P, HALF], U32)
@@ -341,65 +369,66 @@ def tile_list_frost_risk_map_kernel(
         fused_difference(7, lower[:, 1, :])
         w1_w[1, 1] = held("w1_w11", [P, KP], U32)[:]
         quantise_w1(1, 1)
-        x1_bf1 = held("x1_bf1", [P, PACK * HALF], BF16, tag="w1_f32_11")
-        round_x_vector(1, x1_bf1[:])
-        pairs = {(0, 0): [inner_pair(0, 0, pair, 4 + pair) for pair in range(2)]}
-        pairs[1, 0] = [inner_pair(1, 0, pair, 6 + pair) for pair in range(2)]
-        outer_pair(0, 0, 0, *pairs[0, 0][0])
+        x1_bf1 = held("x1_bf1", [P, PACK * HALF], BF16, tag="w1_last1")
+        round_x1(1, x1_bf1[:])
+
+        for g in range(PASSES):
+            pairs[g, 0] = [inner_pair(g, 0, pair, 4 + 2 * g + pair) for pair in range(2)]
+        outer_pair(0, 0, 0)
         x1_w[1] = held("x1_w1", [P, HALF], U32)
         quantise(x1_bf1[:], x1_w[1][:], x1_s[1][:])
-        outer_pair(0, 0, 1, *pairs[0, 0][1])
-        add_hardiness_sbuf(1, 0, m_sb[1, 0][:])
-        m_sb[0, 1] = held("m_sb01", [P, P, PACK], F32, tag="inner000")
-        hardiness_to_sbuf(m_sb[0, 1][:], m[0, 1])
-        pairs[0, 1] = [inner_pair(0, 1, pair, (1, 4)[pair]) for pair in range(2)]
-        outer_pair(1, 0, 0, *pairs[1, 0][0])
-        add_hardiness(0, 0, m[0, 0])
-        outer_pair(1, 0, 1, *pairs[1, 0][1])
+        outer_pair(0, 0, 1)
+        add_hardiness_gpsimd(1, 0)
+        pairs[0, 1] = [inner_pair(0, 1, pair, 1 + pair) for pair in range(2)]
+        outer_pair(1, 0, 0)
+        add_hardiness(0, 0)
+        outer_pair(1, 0, 1)
         quantise_h(0, 0, 2)
-        m_sb[1, 1] = held("m_sb11", [P, P, PACK], F32, tag="inner101")
-        hardiness_to_sbuf(m_sb[1, 1][:], m[1, 1])
-        pairs[1, 1] = [inner_pair(1, 1, pair, (5, 2)[pair]) for pair in range(2)]
+        hardiness_to_sbuf(1, 1, "inner101")
+        pairs[1, 1] = [inner_pair(1, 1, pair, 4 + pair) for pair in range(2)]
         for q in range(2):
-            add_hardiness_sbuf(q, 1, m_sb[q, 1][:])
+            add_hardiness_gpsimd(q, 1)
+
         m[2, 0] = hardiness(2, 0, 0)
         m[3, 0] = hardiness(3, 0, 6)
-        hardiness_transposed(2, 1, 7)
-        hardiness_transposed(3, 1, 3)
-        m[2, 1] = hardiness(2, 1, 7)
-        m[3, 1] = hardiness(3, 1, 3)
+        late_banks = (7, 3)
+        for (q, g), number in zip(late_m, late_banks):
+            hardiness_transposed(q, g, number)
+        for (q, g), number in zip(late_m, late_banks):
+            m[q, g] = hardiness(q, g, number)
+
         for pair in range(2):
-            outer_pair(0, 1, pair, *pairs[0, 1][pair])
-        two, one = bank(1, [P, 2, HALF]), bank(4, [P, HALF])
+            outer_pair(0, 1, pair)
+        two, one = bank(1, [P, 2, HALF]), bank(2, [P, HALF])
         ys_half = [(two[:, 0, :], True, False), (two[:, 1, :], False, True), (one[:], True, True)]
         damage_pass(ys_half, groups[0], 0)
-        first, final = slice(0, QUARTER), slice(QUARTER, HALF)
-        outer_pair(1, 1, 0, *pairs[1, 1][0], first)
-        add_hardiness(2, 0, m[2, 0])
-        add_hardiness(3, 0, m[3, 0])
-        outer_pair(1, 1, 1, *pairs[1, 1][1], first)
-        outer_pair(1, 1, 0, *pairs[1, 1][0], final)
+        third, fourth = slice(0, QUARTER), slice(QUARTER, HALF)
+        outer_pair(1, 1, 0, third)
+        add_hardiness(2, 0)
+        add_hardiness(3, 0)
+        outer_pair(1, 1, 1, third)
+        outer_pair(1, 1, 0, fourth)
         quantise_h(0, 2, 2)
         quantise_h(1, 0, 2)
         damage_pass(ys_half, groups[0], 1)
         add_bias_and_store(ys_half, y_half, groups[0])
-        add_hardiness(2, 1, m[2, 1])
-        outer_pair(1, 1, 1, *pairs[1, 1][1], final)
+        add_hardiness(2, 1)
+        outer_pair(1, 1, 1, fourth)
         quantise_h(1, 2, 1)
         three = bank(0, [P, N_TILES, P])
         ys_third = [(three[:, n, :], n == 0, n == N_TILES - 1) for n in range(N_TILES)]
         for g in range(PASSES):
             damage_pass(ys_third, groups[1], g)
-        last = 3
-        ys = [bank(number, [P, P]) for number in (6, 5, 2)]
+        ys = [bank(number, [P, P]) for number in (6, 4, 5)]
         ys_last = [(y[:], True, True) for y in ys]
         damage_pass(ys_last, groups[2], 0)
-        add_hardiness(3, 1, m[3, 1])
+        add_hardiness(3, 1)
         add_bias_and_store(ys_third, y_sb[2], groups[1])
         quantise_h(1, 3, 1)
         damage_pass(ys_last, groups[2], 1)
-        nc.vector.tensor_scalar_add(out=y_sb[last][:, 0, :], in0=ys[0][:], scalar1=b_sb[:, 0:1])
-        nc.scalar.activation(out=y_sb[last][:, 1, :], in_=ys[1][:], func=ACT.Identity, bias=b_sb[:, 1:2])
-        nc.vector.tensor_scalar_add(out=y_sb[last][:, 2, :], in0=ys[2][:], scalar1=b_sb[:, 2:3])
+        y_last = y_sb[3]
+        nc.vector.tensor_scalar_add(out=y_last[:, 0, :], in0=ys[0][:], scalar1=b_sb[:, 0:1])
+        nc.scalar.activation(out=y_last[:, 1, :], in_=ys[1][:], func=ACT.Identity, bias=b_sb[:, 1:2])
+        nc.vector.tensor_scalar_add(out=y_last[:, 2, :], in0=ys[2][:], scalar1=b_sb[:, 2:3])
         for n, queue in enumerate((nc.sync, nc.scalar, nc.sync)):
-            queue.dma_start(out=out[n * P : (n + 1) * P, last * P : (last + 1) * P], in_=y_sb[last][:, n, :])
+            queue.dma_start(out=out[n * P : (n + 1) * P, groups[2]], in_=y_last[:, n, :])

@@ -1,7 +1,7 @@
+import math
 from contextlib import ExitStack
 
 import concourse.mybir as mybir
-from concourse.masks import make_identity
 
 K, T, T2, S, H, N = 1024, 2048, 1024, 512, 1024, 384
 FLOPS = 2 * S * (K * H + K * H + H * N)
@@ -29,7 +29,7 @@ SCALE_ROWS = 4
 BLOCKS = 16
 STRIPE = 16
 RUN = 4
-PLACES = 4
+KB = 1024
 ALIGN = 256
 
 
@@ -41,9 +41,19 @@ def tile_list_frost_risk_map_kernel(
         lists = ctx.enter_context(tc.tile_pool(name="lists", bufs=1))
         keep = ctx.enter_context(tc.tile_pool(name="keep", bufs=1))
         psum = ctx.enter_context(tc.psum_pool(name="psum", bufs=1))
+        starts, ends = {}, [0]
 
-        def held(name, shape, dtype, tag=""):
-            return keep.tile(shape, dtype, name=name, tag=tag, align_bytes=ALIGN)
+        def reserve(name, size):
+            starts[name] = ends[-1]
+            ends.append(ends[-1] + -(-size // ALIGN) * ALIGN)
+
+        def held(name, shape, dtype, on=None, skip=0):
+            if on is None:
+                width = 4 if dtype in (F32, I32, U32) else 2 if dtype in (BF16, U16) else 1
+                reserve(name, math.prod(shape[1:]) * width)
+            else:
+                starts[name] = starts[on] + skip
+            return keep.tile(shape, dtype, name=name, align_bytes=ALIGN, offset=starts[name])
 
         def bank(number, shape):
             return psum.tile(shape, F32, name=f"bank{number}")
@@ -52,73 +62,49 @@ def tile_list_frost_risk_map_kernel(
         idx2 = lists.tile([P, S // STRIPE], U16, name="idx2")
         idx3 = lists.tile([P, S // STRIPE], U16, name="idx3")
 
-        rows = [held(f"rows{n}", [P, T2], F32) for n in range(PASSES * PACK)]
+        rows = {n: held(f"rows{n}", [P, T2], F32)[:] for n in (0, 1, 2, 4, 5, 6)}
+        rows_7_3 = held("rows_7_3", [P, 2 * T2], F32)
+        rows[7], rows[3] = rows_7_3[:, 0:T2], rows_7_3[:, T2:]
         tab_w = [held(f"tab_w{a}", [P, T], I32) for a in range(PASSES)]
         tab_s = held("tab_s", [P, T], U8)
         v_rows = held("v_rows", [P, S], U8)
-        v_w = [held(f"v_w{a}", [P, S], U32) for a in range(PASSES)]
         v_s = [held(f"v_s{a}", [P, S], U8) for a in range(PASSES)]
-        w2_w = held("w2_w", [P, PASSES, 2 * H], U8)
-        w2_s = held("w2_s", [P, PASSES, H], U8)
+        w2_w_raw = held("w2_w_raw", [P, PASSES, 2 * H], U8)
+        w2_s_raw = held("w2_s_raw", [P, PASSES, H], U8)
+        w2_w = held("w2_w", [P, PASSES * H], U16)
+        w2_s = [held(f"w2_s{a}", [P, H], U8) for a in range(PASSES)]
         w3_w = held("w3_w", [P, PASSES, N], I32)
         w3_s = held("w3_s", [P, PASSES, N], U8)
         c1_sb = held("c1_sb", [P, PASSES, PACK], F32)
         c2_sb = held("c2_sb", [P, PASSES, PACK], F32)
         b_sb = held("b_sb", [P, N_TILES], F32)
-        ident = held("ident", [P, P], F32)
-        w1_pass0 = held("w1_pass0", [P, PACK, H], F32)
-        w1_f32 = {(0, g): w1_pass0[:, :, g * KP : (g + 1) * KP] for g in range(PASSES)}
-        w1_f32[1, 0] = held("w1_f32_10", [P, PACK, KP], F32)[:]
-        w1_last = [held(f"w1_last{n}", [P, PACK, HALF], F32) for n in range(2)]
-        w1_s0 = held("w1_s0", [P, H], U8)
-        codes0 = held("codes0", [P, H + S], U32, tag="tab_w1")
-        w1_w = {(0, g): codes0[:, g * KP : (g + 1) * KP] for g in range(PASSES)}
-        w1_s = {(0, g): w1_s0[:, g * KP : (g + 1) * KP] for g in range(PASSES)}
-        for g in range(PASSES):
-            w1_s[1, g] = held(f"w1_s1{g}", [P, KP], U8)[:]
-        w1_bf0 = held("w1_bf0", [P, PASSES * PACK * KP], BF16)
-        w1_bf = {(0, g): w1_bf0[:, g * PACK * KP : (g + 1) * PACK * KP] for g in range(PASSES)}
-        w1_bf[1, 1] = held("w1_bf11", [P, PACK * KP], BF16)[:]
-        picked = [held(f"picked{n}", [P, 2, S], F32, tag=f"quad{n}1") for n in range(2)]
-        x0 = held("x0", [P, PACK, S], F32)
-        x1_first = held("x1_first", [P, PACK, HALF], F32)
-        x1_second = held("x1_second", [P, (PACK - 1) * HALF + PACK * KP // 2], F32)
-        x1 = [x1_first[:], x1_second[:, 0 : PACK * HALF].rearrange("p (i c) -> p i c", i=PACK)]
-        x0_w, x0_s = codes0[:, H : H + S], held("x0_s", [P, S], U8)
-        w1_bf[1, 0] = x1_second[:, (PACK - 1) * HALF :].bitcast(BF16)
-        x1_w, x1_s = {}, {half: held(f"x1_s{half}", [P, HALF], U8) for half in range(2)}
-        late_m = ((2, 1), (3, 1))
-        early_m = [(q, g) for q in range(4) for g in range(PASSES) if (q, g) not in late_m]
-        m_t = {(q, g): held(f"m_t{q}{g}", [P, PACK, P], F32)[:] for q, g in early_m + list(late_m)}
-        quad = {(g, half): held(f"quad{g}{half}", [P, 2, HALF, 2], F32) for g in range(PASSES) for half in range(2)}
-        h_tiles = [
-            (
-                held(f"h_bf{half}", [P, PLACES * KP], BF16),
-                held(f"h_w{half}", [P, PLACES * P], U32),
-                held(f"h_s{half}", [P, PLACES * P], U8),
-            )
-            for half in range(2)
-        ]
-        groups = (slice(0, HALF), slice(HALF, HALF + QUARTER), slice(HALF + QUARTER, S))
-        y_half = held("y_half", [P, N_TILES, HALF], F32)
-        y_sb = {q: held(f"y_sb{q}", [P, N_TILES, P], F32) for q in (2, 3)}
+        w1_f32 = {(a, g): held(f"w1_f32_{a}{g}", [P, PACK, KP], F32) for a, g in ((0, 0), (1, 0), (0, 1))}
+        reserve("last_w1", 14 * KB)
+        w1_f32[1, 1] = held("w1_f32_11", [P, PACK, KP], F32, on="last_w1", skip=2 * KB)
+        w1_bf = {(a, 0): held(f"w1_bf{a}0", [P, PACK * KP], BF16)[:] for a in range(PASSES)}
+        w1_w = {(0, 0): held("w1_w00", [P, KP], U32)[:]}
+        w1_s = {(a, 0): held(f"w1_s{a}0", [P, KP], U8)[:] for a in range(PASSES)}
+        w1_bf1 = held("w1_bf1", [P, PASSES * PACK * KP], BF16)
+        w1_s1 = held("w1_s1", [P, PASSES * KP], U8)
+        for a in range(PASSES):
+            w1_bf[a, 1] = w1_bf1[:, a * PACK * KP : (a + 1) * PACK * KP]
+            w1_s[a, 1] = w1_s1[:, a * KP : (a + 1) * KP]
 
         nc.vector.memset(tab_s[2 * QUADRANT : P, :].bitcast(I32), 0)
-        for part in (tab_s[QUADRANT : 2 * QUADRANT, :], v_s[0][:], v_s[1][:], w2_s[:], w3_s[:]):
+        for part in (tab_s[QUADRANT : 2 * QUADRANT, :], w2_s_raw[:], v_s[0][:], v_s[1][:], w3_s[:]):
             nc.gpsimd.memset(part.bitcast(I32), 0)
-        make_identity(nc, ident[:])
 
         def load_rows(n):
             a, i = divmod(n, PACK)
             part = xT[a * KP : (a + 1) * KP, :].rearrange("(p i) t -> p i t", i=PACK)
-            nc.sync.dma_start(out=rows[n][:], in_=part[:, i, :])
+            nc.sync.dma_start(out=rows[n], in_=part[:, i, :])
 
         def load_table(a):
             nc.sync.dma_start(out=tab_w[a][:], in_=tab_words[a].rearrange("p t i -> p (t i)").bitcast(I32))
 
-        def load_w1(tile, a, channels):
-            part = w1[a * KP : (a + 1) * KP, channels]
-            nc.sync.dma_start(out=tile, in_=part.rearrange("(p i) c -> p i c", i=PACK))
+        def load_w1(a, g):
+            part = w1[a * KP : (a + 1) * KP, g * KP : (g + 1) * KP]
+            nc.sync.dma_start(out=w1_f32[a, g][:], in_=part.rearrange("(p i) c -> p i c", i=PACK))
 
         def load_scales(tile, scales):
             for row in range(SCALE_ROWS):
@@ -130,112 +116,103 @@ def tile_list_frost_risk_map_kernel(
                 part = v_rows[BLOCKS * a + row : BLOCKS * (a + 1) : SCALE_ROWS, :]
                 nc.sync.dma_start(out=v_s[a][row:P:QUADRANT, :].bitcast(I32), in_=part.bitcast(I32))
 
-        def pick(n, offsets, cols, values):
+        def pick(n, cols, picked, wide=None):
             entries = slice(cols.start // STRIPE, cols.stop // STRIPE)
-            nc.vector.tensor_copy(out=values, in_=rows[n][:].indirect(offsets[:, entries]))
+            for l, offsets in enumerate((idx3, idx2)):
+                window = wide if wide is not None and l == 0 else rows[n]
+                nc.vector.tensor_copy(out=picked[:, l, n % 2, :], in_=window.indirect(offsets[:, entries]))
 
-        def pick_both(n, cols, both):
-            for e, offsets in enumerate((idx3, idx2)):
-                pick(n, offsets, cols, both[:, e, :])
-
-        def subtract(both, x_out):
-            nc.gpsimd.tensor_tensor(out=x_out, in0=both[:, 1, :], in1=both[:, 0, :], op=ALU.subtract)
-
-        def differences(n, cols, both, x_out):
-            pick_both(n, cols, both)
-            subtract(both, x_out)
-
-        def differences_by_halves(n, both):
-            pick_both(n, whole, both)
-            for half in range(2):
-                subtract(both[:, :, halves[half]], x1[half][:, n - PACK, :])
-
-        def fused_difference(n, lower_values):
-            nc.vector.tensor_tensor(
-                out=x1[1][:, n - PACK, :],
-                in0=rows[n][:].indirect(idx2[:, HALF // STRIPE :]),
-                in1=lower_values,
+        def subtract_pair(picked, x_pair):
+            nc.gpsimd.tensor_tensor(
+                out=x_pair.rearrange("p (c r e) -> p c e r", r=RUN, e=2),
+                in0=picked[:, 1, :, :].rearrange("p e (c r) -> p c e r", r=RUN),
+                in1=picked[:, 0, :, :].rearrange("p e (c r) -> p c e r", r=RUN),
                 op=ALU.subtract,
             )
 
-        def round_x0(x_bf):
-            nc.scalar.activation(
-                out=x_bf.rearrange("p (c e i) -> p c i e", e=RUN, i=PACK),
-                in_=x0[:].rearrange("p i (c e) -> p c i e", e=RUN),
-                func=ACT.Copy,
-            )
-
-        def round_x1(half, x_bf):
-            nc.vector.tensor_copy(
-                out=x_bf.rearrange("p (c i) -> p c i", i=PACK),
-                in_=x1[half].rearrange("p i c -> p c i"),
+        def weave(x_pairs, x_bf):
+            nc.scalar.copy(
+                out=x_bf[:].bitcast(U32).rearrange("p (c u) -> p c u", u=2),
+                in_=x_pairs[:].bitcast(U32).rearrange("p u c -> p c u"),
             )
 
         def quantise(bf, words, scales):
             nc.vector.quantize_mx(out=words.bitcast(FP8X4), scales=scales, in_=bf)
 
-        def round_w1(a, g, part, words=slice(0, P)):
+        def round_w1(a, g):
             nc.scalar.activation(
-                out=w1_bf[a, g].rearrange("p (t u i) -> p u i t", t=PACK, i=PACK)[:, words, :, :],
-                in_=part.rearrange("p i (u t) -> p u i t", t=PACK),
+                out=w1_bf[a, g].rearrange("p (t u i) -> p u i t", t=PACK, i=PACK),
+                in_=w1_f32[a, g][:].rearrange("p i (u t) -> p u i t", t=PACK),
                 func=ACT.Copy,
             )
-
-        def quantise_w1(a, g):
-            quantise(w1_bf[a, g], w1_w[a, g], w1_s[a, g])
 
         def gather_words(a):
             nc.vector.tensor_copy(out=v_w[a][:], in_=tab_w[a][:].bitcast(U32).indirect(idx[:]))
 
-        def hardiness_transposed(q, g, number):
-            sums = bank(number, [P, KP])
-            for a in (1, 0):
-                nc.tensor.matmul_mx(
-                    out=sums[:],
-                    lhsT=v_w[a][:, q * P : (q + 1) * P].bitcast(FP8X4),
-                    lhsT_scale=v_s[a][:, q * P : (q + 1) * P],
-                    rhs=w2_w[:, a, 2 * g * KP : 2 * (g + 1) * KP].bitcast(FP4X4),
-                    rhs_scale=w2_s[:, a, g * KP : (g + 1) * KP],
-                    start=(a == 1),
-                    stop=(a == 0),
-                )
-            nc.scalar.activation(out=m_t[q, g], in_=sums[:].rearrange("j (p t) -> j t p", t=PACK), func=ACT.Copy)
-
-        def hardiness(q, g, number):
-            turned = bank(number, [P, PACK, P])
-            for t in range(PACK):
-                nc.tensor.transpose(turned[:, t, :], m_t[q, g][:, t, :], ident[:])
-            return turned
-
-        def response(d, a, g, t, half, start, stop):
-            x_w, x_s = (x0_w[:, halves[half]], x0_s[:, halves[half]]) if a == 0 else (x1_w[half][:], x1_s[half][:])
+        def hardiness_pass(y, a, g, t, cols, start, stop):
+            first = a * H + g * KP + t * P
             nc.tensor.matmul_mx(
-                out=d,
-                lhsT=w1_w[a, g][:, t * P : (t + 1) * P].bitcast(FP8X4),
-                lhsT_scale=w1_s[a, g][:, t * P : (t + 1) * P],
-                rhs=x_w.bitcast(FP8X4),
-                rhs_scale=x_s,
+                out=y,
+                lhsT=w2_w[:, first : first + P].bitcast(FP4X4),
+                lhsT_scale=w2_s[a][:, g * KP + t * P : g * KP + (t + 1) * P],
+                rhs=v_w[a][:, cols].bitcast(FP8X4),
+                rhs_scale=v_s[a][:, cols],
                 start=start,
                 stop=stop,
             )
 
-        def inner_step(inner, d, g, t):
-            nc.scalar.activation(
-                out=inner, in_=d, func=ACT.Identity, scale=c2_sb[:, g, t : t + 1], bias=c1_sb[:, g, t : t + 1]
+        def hardiness_quarter(g, q, number):
+            m[g, q] = bank(number, [P, PACK, QUARTER])
+            for a in range(PASSES):
+                for t in range(PACK):
+                    cols = slice(q * QUARTER, (q + 1) * QUARTER)
+                    hardiness_pass(m[g, q][:, t, :], a, g, t, cols, (a, t) == (0, 0), (a, t) == (1, PACK - 1))
+
+        def hardiness_to_sbuf(q):
+            m_sb[q] = held(f"m_sb{q}", [P, QUARTER, PACK], F32)
+            nc.scalar.activation(out=m_sb[q][:], in_=m[0, q][:].rearrange("p t j -> p j t"), func=ACT.Copy)
+
+        def response_to_sbuf(pair):
+            d_sb[pair] = held(f"d_sb{pair}", [P, HALF, 2], F32, on="last_w1", skip=ALIGN + (4 * pair + 2) * KB)
+            nc.scalar.activation(out=d_sb[pair][:], in_=pairs[0, 0, pair][0][:].rearrange("p e j -> p j e"), func=ACT.Copy)
+
+        def outer_pair_gpsimd(pair):
+            nc.gpsimd.tensor_tensor(
+                out=quad[0, 0][:, pair, :, :],
+                in0=d_sb[pair][:],
+                in1=pairs[0, 0, pair][1][:].rearrange("p e j -> p j e"),
+                op=ALU.mult,
             )
 
-        def inner_pair(g, half, pair, number):
+        def inner_pair(g, half, pair, number, **place):
             d = bank(number, [P, 2, HALF])
-            inner = held(f"inner{g}{half}{pair}", [P, 2, HALF], F32)
+            inner = held(f"inner{g}{half}{pair}", [P, 2, HALF], F32, **place)
             for a in range(PASSES):
+                x_w, x_s = (x0_w[:, halves[half]], x0_s[:, halves[half]]) if a == 0 else (x1_w[half][:], x1_s[half][:])
                 for e in range(2):
-                    response(d[:, e, :], a, g, 2 * pair + e, half, (a, e) == (0, 0), (a, e) == (1, 1))
+                    t = 2 * pair + e
+                    nc.tensor.matmul_mx(
+                        out=d[:, e, :],
+                        lhsT=w1_w[a, g][:, t * P : (t + 1) * P].bitcast(FP8X4),
+                        lhsT_scale=w1_s[a, g][:, t * P : (t + 1) * P],
+                        rhs=x_w.bitcast(FP8X4),
+                        rhs_scale=x_s,
+                        start=(a, e) == (0, 0),
+                        stop=(a, e) == (1, 1),
+                    )
             for e in range(2):
-                inner_step(inner[:, e, :], d[:, e, :], g, 2 * pair + e)
-            return d, inner
+                t = 2 * pair + e
+                nc.scalar.activation(
+                    out=inner[:, e, :],
+                    in_=d[:, e, :],
+                    func=ACT.Identity,
+                    scale=c2_sb[:, g, t : t + 1],
+                    bias=c1_sb[:, g, t : t + 1],
+                )
+            pairs[g, half, pair] = d, inner
 
         def outer_pair(g, half, pair, cols=slice(0, HALF)):
-            d, inner = pairs[g, half][pair]
+            d, inner = pairs[g, half, pair]
             nc.vector.tensor_tensor(
                 out=quad[g, half][:, pair, cols, :],
                 in0=d[:, :, cols].rearrange("p e j -> p j e"),
@@ -243,50 +220,32 @@ def tile_list_frost_risk_map_kernel(
                 op=ALU.mult,
             )
 
-        def rounded_place(half, place):
-            return place % 2 if half == 0 else place
-
-        def sum_operands(q, g):
-            place = rounded_place(q // 2, 2 * g + q % 2)
-            h_part = h_tiles[q // 2][0][:, place * KP : (place + 1) * KP]
+        def sum_operands(g, q, h_part):
             terms = quad[g, q // 2][:, :, (q % 2) * QUARTER : (q % 2 + 1) * QUARTER, :]
-            h_part = h_part.rearrange("p (j pair e) -> p j pair e", pair=2, e=2)
-            return h_part, terms.rearrange("p pair j e -> p j pair e")
+            return h_part.rearrange("p (j pair e) -> p j pair e", pair=2, e=2), terms.rearrange("p pair j e -> p j pair e")
 
-        def hardiness_to_sbuf(q, g, tag):
-            m_sb[q, g] = held(f"m_sb{q}{g}", [P, P, PACK], F32, tag=tag)
-            nc.scalar.activation(out=m_sb[q, g][:], in_=m[q, g][:].rearrange("p t j -> p j t"), func=ACT.Copy)
-
-        def add_hardiness_gpsimd(q, g):
-            h_part, terms = sum_operands(q, g)
-            m_part = m_sb[q, g][:].rearrange("p j (pair e) -> p j pair e", e=2)
+        def add_hardiness_gpsimd(q, h_part):
+            h_part, terms = sum_operands(0, q, h_part)
+            m_part = m_sb[q][:].rearrange("p j (pair e) -> p j pair e", e=2)
             nc.gpsimd.tensor_tensor(out=h_part, in0=m_part, in1=terms, op=ALU.add)
 
-        def add_hardiness(q, g):
-            h_part, terms = sum_operands(q, g)
-            m_part = m[q, g][:].rearrange("p (pair e) j -> p j pair e", e=2)
+        def add_hardiness(g, q, h_part):
+            h_part, terms = sum_operands(g, q, h_part)
+            m_part = m[g, q][:].rearrange("p (pair e) j -> p j pair e", e=2)
             nc.vector.tensor_tensor(out=h_part, in0=m_part, in1=terms, op=ALU.add)
 
-        def quantise_h(half, place, count):
-            rounded, words, scales = h_tiles[half]
-            start = rounded_place(half, place) * KP
-            cols = slice(place * P, (place + count) * P)
-            quantise(rounded[:, start : start + count * KP], words[:, cols], scales[:, cols])
-
-        def damage_pass(ys, cols, g):
-            words, scales = h_tiles[cols.start // HALF][1:]
-            begin = g * HALF + cols.start % HALF
-            within = slice(begin, begin + cols.stop - cols.start)
-            for n, (y, opens, closes) in enumerate(ys):
-                nc.tensor.matmul_mx(
-                    out=y,
-                    lhsT=w3_w[:, g, n * P : (n + 1) * P].bitcast(FP8X4),
-                    lhsT_scale=w3_s[:, g, n * P : (n + 1) * P],
-                    rhs=words[:, within].bitcast(FP8X4),
-                    rhs_scale=scales[:, within],
-                    start=(g == 0 and opens),
-                    stop=(g == 1 and closes),
-                )
+        def damage(ys, words, scales, width, passes=range(PASSES)):
+            for g in passes:
+                for n, (y, opens, closes) in enumerate(ys):
+                    nc.tensor.matmul_mx(
+                        out=y,
+                        lhsT=w3_w[:, g, n * P : (n + 1) * P].bitcast(FP8X4),
+                        lhsT_scale=w3_s[:, g, n * P : (n + 1) * P],
+                        rhs=words[:, g * width : (g + 1) * width].bitcast(FP8X4),
+                        rhs_scale=scales[:, g * width : (g + 1) * width],
+                        start=(g == 0 and opens),
+                        stop=(g == 1 and closes),
+                    )
 
         def add_bias_and_store(ys, y_out, cols):
             for n in range(N_TILES):
@@ -294,7 +253,8 @@ def tile_list_frost_risk_map_kernel(
                 nc.sync.dma_start(out=out[n * P : (n + 1) * P, cols], in_=y_out[:, n, :])
 
         whole, halves = slice(0, S), (slice(0, HALF), slice(HALF, S))
-        pairs, m, m_sb = {}, {}, {}
+        pairs, m, x1_w, x1_s, v_w = {}, {}, {}, {}, {}
+        quad, m_sb, d_sb = {}, {}, {}
 
         nc.sync.dma_start(
             out=tab_s[0 : PASSES * BLOCKS, :].bitcast(I32), in_=tab_scales.rearrange("a n t -> (a n) t").bitcast(I32)
@@ -303,132 +263,157 @@ def tile_list_frost_risk_map_kernel(
         load_rows(0)
         nc.sync.dma_start(idx3[:], offs3)
         nc.sync.dma_start(idx2[:], offs2)
-        for n in range(1, PACK):
-            load_rows(n)
+        load_rows(1)
+        load_scales(w2_s_raw, w2_scales)
+        nc.sync.dma_start(out=w2_w_raw[:].bitcast(I32), in_=w2_words.rearrange("a p c -> p a c").bitcast(I32))
+        load_rows(2)
         nc.vector.tensor_copy(out=v_rows[:], in_=tab_s[:].indirect(idx[:]))
         place_gathered_scales(0)
-        load_w1(w1_pass0[:], 0, slice(0, H))
+        load_w1(0, 0)
+        load_rows(3)
         place_gathered_scales(1)
         load_rows(4)
-        load_table(0)
-        load_scales(w2_s, w2_scales)
-        load_table(1)
-        nc.sync.dma_start(out=w2_w[:].bitcast(I32), in_=w2_words.rearrange("a p c -> p a c").bitcast(I32))
         load_rows(5)
-        load_rows(7)
-        load_w1(w1_f32[1, 0], 1, slice(0, KP))
-        load_rows(6)
-        for n in range(2):
-            load_w1(w1_last[n][:], 1, slice(KP + n * HALF, KP + (n + 1) * HALF))
         nc.sync.dma_start(out=c1_sb[:], in_=c1.rearrange("(g p t) -> p g t", g=PASSES, t=PACK))
         nc.sync.dma_start(out=c2_sb[:], in_=c2.rearrange("(g p t) -> p g t", g=PASSES, t=PACK))
-        nc.sync.dma_start(out=w3_w[:], in_=w3_words.rearrange("a p c i -> p a (c i)").bitcast(I32))
+        load_rows(6)
+        load_rows(7)
+        load_w1(1, 0)
+        load_w1(0, 1)
         load_scales(w3_s, w3_scales)
+        load_w1(1, 1)
+        load_table(0)
         with nc.allow_non_contiguous_dma(reason="one bias value to a partition"):
             nc.sync.dma_start(out=b_sb[:], in_=b.rearrange("(n p) -> p n", p=P))
+        load_table(1)
+        nc.sync.dma_start(out=w3_w[:], in_=w3_words.rearrange("a p c i -> p a (c i)").bitcast(I32))
 
-        for n in range(PACK):
-            differences(n, whole, picked[n % 2][:], x0[:, n, :])
-        for g in range(PASSES):
-            round_w1(0, g, w1_f32[0, g])
-        differences_by_halves(4, picked[0][:])
+        nc.scalar.copy(
+            out=w2_w[:].rearrange("p (s t u) -> p s t u", t=PACK, u=P),
+            in_=w2_w_raw[:].rearrange("p a c -> p (a c)").bitcast(U16).rearrange("p (s u t) -> p s t u", t=PACK, u=P),
+        )
         for a in range(PASSES):
-            gather_words(a)
-        quantise(w1_bf0[:], codes0[:, 0:H], w1_s0[:])
-        x0_bf = held("x0_bf", [P, PACK * S], BF16, tag="w1_pass0")
-        round_x0(x0_bf[:])
-        quantise(x0_bf[:], x0_w, x0_s[:])
+            nc.gpsimd.tensor_copy(
+                out=w2_s[a][:].rearrange("p (g t u) -> p g t u", t=PACK, u=P),
+                in_=w2_s_raw[:, a, :].rearrange("p (g u t) -> p g t u", t=PACK, u=P),
+            )
 
-        for half in range(2):
-            for g in range(PASSES):
-                for q in (2 * half, 2 * half + 1):
-                    if (q, g) in early_m:
-                        hardiness_transposed(q, g, PLACES * half + 2 * g + q % 2)
-        round_w1(1, 0, w1_f32[1, 0])
-        for g in range(PASSES):
-            for q in range(2):
-                m[q, g] = hardiness(q, g, 2 * g + q)
-        for n in range(2):
-            round_w1(1, 1, w1_last[n][:], slice(n * P // 2, (n + 1) * P // 2))
-        hardiness_to_sbuf(1, 0, "w1_last0")
-        hardiness_to_sbuf(0, 1, "w1_f32_10")
+        x0_pairs = held("x0_pairs", [P, 2, 2 * S], BF16)
+        for u in range(2):
+            picked = held(f"picked0{u}", [P, 2, 2, S], F32)
+            for e in range(2):
+                pick(2 * u + e, whole, picked)
+            if u == 1:
+                round_w1(0, 0)
+                quantise(w1_bf[0, 0], w1_w[0, 0], w1_s[0, 0])
+            subtract_pair(picked, x0_pairs[:, u, :])
+        x0_bf = held("x0_bf", [P, PACK * S], BF16)
+        weave(x0_pairs, x0_bf)
 
-        differences_by_halves(5, picked[1][:])
-        differences(7, halves[0], picked[0][:, :, halves[0]], x1[0][:, 3, :])
-        lower = held("lower", [P, 2, HALF], F32)
-        pick(7, idx3, halves[1], lower[:, 1, :])
-        differences(6, halves[0], picked[0][:, :, halves[1]], x1[0][:, 2, :])
-        pick(6, idx3, halves[1], lower[:, 0, :])
-        fused_difference(6, lower[:, 0, :])
-        x1_bf0 = held("x1_bf0", [P, PACK * HALF], BF16)
-        round_x1(0, x1_bf0[:])
-        w1_w[1, 0] = held("w1_w10", [P, KP], U32)[:]
-        quantise_w1(1, 0)
-        x1_w[0] = held("x1_w0", [P, HALF], U32)
+        x1_pairs0 = held("x1_pairs0", [P, 2, 2 * HALF], BF16)
+        for u in range(2):
+            picked = held(f"picked10{u}", [P, 2, 2, HALF], F32)
+            pick(PACK + 2 * u, halves[0], picked)
+            pick(PACK + 2 * u + 1, halves[0], picked, rows_7_3[:] if u == 1 else None)
+            subtract_pair(picked, x1_pairs0[:, u, :])
+        round_w1(1, 0)
+        x1_bf0 = held("x1_bf0", [P, PACK * HALF], BF16, on="w1_f32_10", skip=KB)
+        weave(x1_pairs0, x1_bf0)
+
+        picked_a = rows[3].rearrange("p (l e c) -> p l e c", l=2, e=2)
+        for e in range(2):
+            pick(PACK + e, halves[1], picked_a)
+        x0_w, x0_s = held("x0_w", [P, S], U32, on="rows4"), held("x0_s", [P, S], U8)
+        quantise(x0_bf[:], x0_w[:], x0_s[:])
+        w1_w[1, 0] = held("w1_w10", [P, KP], U32, on="rows4", skip=2 * KB)[:]
+        quantise(w1_bf[1, 0], w1_w[1, 0], w1_s[1, 0])
+        x1_w[0], x1_s[0] = held("x1_w0", [P, HALF], U32), held("x1_s0", [P, HALF], U8)
         quantise(x1_bf0[:], x1_w[0][:], x1_s[0][:])
-        fused_difference(7, lower[:, 1, :])
-        w1_w[1, 1] = held("w1_w11", [P, KP], U32)[:]
-        quantise_w1(1, 1)
-        x1_bf1 = held("x1_bf1", [P, PACK * HALF], BF16, tag="w1_last1")
-        round_x1(1, x1_bf1[:])
-
-        for g in range(PASSES):
-            pairs[g, 0] = [inner_pair(g, 0, pair, 4 + 2 * g + pair) for pair in range(2)]
-        outer_pair(0, 0, 0)
-        x1_w[1] = held("x1_w1", [P, HALF], U32)
+        x1_pairs1 = held("x1_pairs1", [P, 2, 2 * HALF], BF16, on="w1_f32_10")
+        subtract_pair(picked_a, x1_pairs1[:, 0, :])
+        picked_b = held("picked111", [P, 2, 2, HALF], F32, on="w1_f32_10", skip=2 * KB)
+        for e in range(2):
+            pick(PACK + 2 + e, halves[1], picked_b)
+        for a in range(PASSES):
+            round_w1(a, 1)
+        v_w[0] = held("v_w0", [P, S], U32, on="rows6")
+        gather_words(0)
+        subtract_pair(picked_b, x1_pairs1[:, 1, :])
+        x1_bf1 = held("x1_bf1", [P, PACK * HALF], BF16, on="last_w1", skip=ALIGN + 8 * KB)
+        inner_pair(0, 0, 0, 0, on="last_w1", skip=ALIGN)
+        response_to_sbuf(0)
+        weave(x1_pairs1, x1_bf1)
+        inner_pair(0, 0, 1, 1, on="last_w1", skip=ALIGN + 4 * KB)
+        response_to_sbuf(1)
+        w1_w1 = held("w1_w1", [P, PASSES * KP], U32, on="tab_w0")
+        for a in range(PASSES):
+            w1_w[a, 1] = w1_w1[:, a * KP : (a + 1) * KP]
+        quantise(w1_bf1[:], w1_w1[:], w1_s1[:])
+        x1_w[1], x1_s[1] = held("x1_w1", [P, HALF], U32, on="tab_w0", skip=4 * KB), held("x1_s1", [P, HALF], U8)
         quantise(x1_bf1[:], x1_w[1][:], x1_s[1][:])
-        outer_pair(0, 0, 1)
-        add_hardiness_gpsimd(1, 0)
-        pairs[0, 1] = [inner_pair(0, 1, pair, 1 + pair) for pair in range(2)]
-        outer_pair(1, 0, 0)
-        add_hardiness(0, 0)
-        outer_pair(1, 0, 1)
-        quantise_h(0, 0, 2)
-        hardiness_to_sbuf(1, 1, "inner101")
-        pairs[1, 1] = [inner_pair(1, 1, pair, 4 + pair) for pair in range(2)]
-        for q in range(2):
-            add_hardiness_gpsimd(q, 1)
+        v_w[1] = held("v_w1", [P, S], U32)
+        gather_words(1)
 
-        m[2, 0] = hardiness(2, 0, 0)
-        m[3, 0] = hardiness(3, 0, 6)
-        late_banks = (7, 3)
-        for (q, g), number in zip(late_m, late_banks):
-            hardiness_transposed(q, g, number)
-        for (q, g), number in zip(late_m, late_banks):
-            m[q, g] = hardiness(q, g, number)
+        quad[0, 0] = held("quad00", [P, 2, HALF, 2], F32, on="x1_bf1", skip=KB)
+        quad[1, 0] = held("quad10", [P, 2, HALF, 2], F32, on="tab_w1")
+        for g in range(PASSES):
+            quad[g, 1] = held(f"quad{g}1", [P, 2, HALF, 2], F32, on="picked00", skip=g * 4 * KB)
 
         for pair in range(2):
-            outer_pair(0, 1, pair)
-        two, one = bank(1, [P, 2, HALF]), bank(2, [P, HALF])
-        ys_half = [(two[:, 0, :], True, False), (two[:, 1, :], False, True), (one[:], True, True)]
-        damage_pass(ys_half, groups[0], 0)
-        third, fourth = slice(0, QUARTER), slice(QUARTER, HALF)
-        outer_pair(1, 1, 0, third)
-        add_hardiness(2, 0)
-        add_hardiness(3, 0)
-        outer_pair(1, 1, 1, third)
-        outer_pair(1, 1, 0, fourth)
-        quantise_h(0, 2, 2)
-        quantise_h(1, 0, 2)
-        damage_pass(ys_half, groups[0], 1)
-        add_bias_and_store(ys_half, y_half, groups[0])
-        add_hardiness(2, 1)
-        outer_pair(1, 1, 1, fourth)
-        quantise_h(1, 2, 1)
-        three = bank(0, [P, N_TILES, P])
-        ys_third = [(three[:, n, :], n == 0, n == N_TILES - 1) for n in range(N_TILES)]
+            outer_pair_gpsimd(pair)
+            inner_pair(1, 0, pair, 2 + pair)
+        for q in range(2):
+            hardiness_quarter(0, q, 6 + q)
+            hardiness_to_sbuf(q)
+        for q in range(2):
+            hardiness_quarter(1, q, q)
+        for pair in range(2):
+            inner_pair(0, 1, pair, 4 + pair)
+        for pair in range(2):
+            outer_pair(1, 0, pair)
+        h_bf = held("h_bf", [P, 4 * KP], BF16)
+        h_w, h_s = held("h_w", [P, 4 * P], U32), held("h_s", [P, 4 * P], U8)
+        for q in range(2):
+            add_hardiness_gpsimd(q, h_bf[:, q * KP : (q + 1) * KP])
+        for pair in range(2):
+            inner_pair(1, 1, pair, 6 + pair)
         for g in range(PASSES):
-            damage_pass(ys_third, groups[1], g)
-        ys = [bank(number, [P, P]) for number in (6, 4, 5)]
-        ys_last = [(y[:], True, True) for y in ys]
-        damage_pass(ys_last, groups[2], 0)
-        add_hardiness(3, 1)
-        add_bias_and_store(ys_third, y_sb[2], groups[1])
-        quantise_h(1, 3, 1)
-        damage_pass(ys_last, groups[2], 1)
-        y_last = y_sb[3]
-        nc.vector.tensor_scalar_add(out=y_last[:, 0, :], in0=ys[0][:], scalar1=b_sb[:, 0:1])
-        nc.scalar.activation(out=y_last[:, 1, :], in_=ys[1][:], func=ACT.Identity, bias=b_sb[:, 1:2])
-        nc.vector.tensor_scalar_add(out=y_last[:, 2, :], in0=ys[2][:], scalar1=b_sb[:, 2:3])
-        for n, queue in enumerate((nc.sync, nc.scalar, nc.sync)):
-            queue.dma_start(out=out[n * P : (n + 1) * P, groups[2]], in_=y_last[:, n, :])
+            hardiness_quarter(g, 2, 2 + g)
+        hardiness_to_sbuf(2)
+        for q in range(2):
+            add_hardiness(1, q, h_bf[:, (2 + q) * KP : (3 + q) * KP])
+        for g in range(PASSES):
+            hardiness_quarter(g, 3, g)
+        for pair in range(2):
+            outer_pair(0, 1, pair)
+        quantise(h_bf[:], h_w[:], h_s[:])
+        two, one = bank(4, [P, 2, HALF]), bank(5, [P, HALF])
+        ys_half = [(two[:, 0, :], True, False), (two[:, 1, :], False, True), (one[:], True, True)]
+        damage(ys_half, h_w, h_s, HALF)
+        y_half = held("y_half", [P, N_TILES, HALF], F32)
+        add_bias_and_store(ys_half, y_half, halves[0])
+
+        h2_bf = held("h2_bf", [P, 2 * KP], BF16, on="h_bf")
+        h3_bf = held("h3_bf", [P, 2 * KP], BF16, on="h_bf", skip=2 * KB)
+        add_hardiness_gpsimd(2, h2_bf[:, 0:KP])
+        for pair in range(2):
+            outer_pair(1, 1, pair)
+        add_hardiness(0, 3, h3_bf[:, 0:KP])
+        add_hardiness(1, 2, h2_bf[:, KP : 2 * KP])
+        add_hardiness(1, 3, h3_bf[:, KP : 2 * KP])
+        h2_w, h2_s = held("h2_w", [P, 2 * P], U32), held("h2_s", [P, 2 * P], U8)
+        h3_w, h3_s = held("h3_w", [P, 2 * P], U32), held("h3_s", [P, 2 * P], U8)
+        quantise(h2_bf[:], h2_w[:], h2_s[:])
+        quantise(h3_bf[:], h3_w[:], h3_s[:])
+        three = bank(2, [P, N_TILES, P])
+        ys_third = [(three[:, n, :], n == 0, n == N_TILES - 1) for n in range(N_TILES)]
+        damage(ys_third, h2_w, h2_s, QUARTER)
+        y_third = held("y_third", [P, N_TILES, P], F32)
+        ys = [bank(number, [P, P]) for number in (3, 6, 7)]
+        damage([(y[:], True, True) for y in ys], h3_w, h3_s, QUARTER)
+        add_bias_and_store(ys_third, y_third, slice(HALF, HALF + QUARTER))
+        y_last = held("y_last", [P, N_TILES, P], F32)
+        for n in range(N_TILES):
+            nc.vector.tensor_scalar_add(out=y_last[:, n, :], in0=ys[n][:], scalar1=b_sb[:, n : n + 1])
+        for n, queue in enumerate((nc.scalar, nc.sync, nc.scalar)):
+            queue.dma_start(out=out[n * P : (n + 1) * P, HALF + QUARTER : S], in_=y_last[:, n, :])

@@ -30,6 +30,8 @@ BLOCKS = 16
 STRIPE = 16
 RUN = 4
 KB = 1024
+SHARED = 64
+GPSIMD_WORDS = 48
 ALIGN = 256
 
 
@@ -81,9 +83,10 @@ def tile_list_frost_risk_map_kernel(
         w1_f32 = {(a, g): held(f"w1_f32_{a}{g}", [P, PACK, KP], F32) for a, g in ((0, 0), (1, 0), (0, 1))}
         reserve("last_w1", 14 * KB)
         w1_f32[1, 1] = held("w1_f32_11", [P, PACK, KP], F32, on="last_w1", skip=2 * KB)
-        w1_bf = {(a, 0): held(f"w1_bf{a}0", [P, PACK * KP], BF16)[:] for a in range(PASSES)}
+        mid_bf, mid_s = held("mid_bf", [P, 2 * PACK * KP], BF16), held("mid_s", [P, 2 * KP], U8)
+        w1_bf = {(0, 0): held("w1_bf00", [P, PACK * KP], BF16)[:], (1, 0): mid_bf[:, PACK * S :]}
         w1_w = {(0, 0): held("w1_w00", [P, KP], U32)[:]}
-        w1_s = {(a, 0): held(f"w1_s{a}0", [P, KP], U8)[:] for a in range(PASSES)}
+        w1_s = {(0, 0): held("w1_s00", [P, KP], U8)[:], (1, 0): mid_s[:, S:]}
         w1_bf1 = held("w1_bf1", [P, PASSES * PACK * KP], BF16)
         w1_s1 = held("w1_s1", [P, PASSES * KP], U8)
         for a in range(PASSES):
@@ -132,19 +135,22 @@ def tile_list_frost_risk_map_kernel(
 
         def weave(x_pairs, x_bf):
             nc.scalar.copy(
-                out=x_bf[:].bitcast(U32).rearrange("p (c u) -> p c u", u=2),
+                out=x_bf.bitcast(U32).rearrange("p (c u) -> p c u", u=2),
                 in_=x_pairs[:].bitcast(U32).rearrange("p u c -> p c u"),
             )
 
         def quantise(bf, words, scales):
             nc.vector.quantize_mx(out=words.bitcast(FP8X4), scales=scales, in_=bf)
 
-        def round_w1(a, g):
-            nc.scalar.activation(
-                out=w1_bf[a, g].rearrange("p (t u i) -> p u i t", t=PACK, i=PACK),
-                in_=w1_f32[a, g][:].rearrange("p i (u t) -> p u i t", t=PACK),
-                func=ACT.Copy,
+        def w1_views(a, g, words):
+            return (
+                w1_bf[a, g].rearrange("p (t u i) -> p u i t", t=PACK, i=PACK)[:, words, :, :],
+                w1_f32[a, g][:].rearrange("p i (u t) -> p u i t", t=PACK)[:, words, :, :],
             )
+
+        def round_w1(a, g, words=slice(0, P)):
+            rounded, values = w1_views(a, g, words)
+            nc.scalar.activation(out=rounded, in_=values, func=ACT.Copy)
 
         def gather_words(a):
             nc.vector.tensor_copy(out=v_w[a][:], in_=tab_w[a][:].bitcast(U32).indirect(idx[:]))
@@ -168,9 +174,9 @@ def tile_list_frost_risk_map_kernel(
                     cols = slice(q * QUARTER, (q + 1) * QUARTER)
                     hardiness_pass(m[g, q][:, t, :], a, g, t, cols, (a, t) == (0, 0), (a, t) == (1, PACK - 1))
 
-        def hardiness_to_sbuf(q):
-            m_sb[q] = held(f"m_sb{q}", [P, QUARTER, PACK], F32)
-            nc.scalar.activation(out=m_sb[q][:], in_=m[0, q][:].rearrange("p t j -> p j t"), func=ACT.Copy)
+        def hardiness_to_sbuf(q, count=QUARTER):
+            m_sb[q] = held(f"m_sb{q}", [P, count, PACK], F32)
+            nc.scalar.activation(out=m_sb[q][:], in_=m[0, q][:, :, 0:count].rearrange("p t j -> p j t"), func=ACT.Copy)
 
         def response_to_sbuf(pair):
             d_sb[pair] = held(f"d_sb{pair}", [P, HALF, 2], F32, on="last_w1", skip=ALIGN + (4 * pair + 2) * KB)
@@ -220,32 +226,32 @@ def tile_list_frost_risk_map_kernel(
                 op=ALU.mult,
             )
 
-        def sum_operands(g, q, h_part):
+        def sum_operands(g, q, h_part, cols):
             terms = quad[g, q // 2][:, :, (q % 2) * QUARTER : (q % 2 + 1) * QUARTER, :]
-            return h_part.rearrange("p (j pair e) -> p j pair e", pair=2, e=2), terms.rearrange("p pair j e -> p j pair e")
+            h_part = h_part.rearrange("p (j pair e) -> p j pair e", pair=2, e=2)
+            return h_part[:, cols, :, :], terms.rearrange("p pair j e -> p j pair e")[:, cols, :, :]
 
-        def add_hardiness_gpsimd(q, h_part):
-            h_part, terms = sum_operands(0, q, h_part)
+        def add_hardiness_gpsimd(q, h_part, cols=slice(0, QUARTER)):
+            h_part, terms = sum_operands(0, q, h_part, cols)
             m_part = m_sb[q][:].rearrange("p j (pair e) -> p j pair e", e=2)
             nc.gpsimd.tensor_tensor(out=h_part, in0=m_part, in1=terms, op=ALU.add)
 
-        def add_hardiness(g, q, h_part):
-            h_part, terms = sum_operands(g, q, h_part)
-            m_part = m[g, q][:].rearrange("p (pair e) j -> p j pair e", e=2)
+        def add_hardiness(g, q, h_part, cols=slice(0, QUARTER)):
+            h_part, terms = sum_operands(g, q, h_part, cols)
+            m_part = m[g, q][:, :, cols].rearrange("p (pair e) j -> p j pair e", e=2)
             nc.vector.tensor_tensor(out=h_part, in0=m_part, in1=terms, op=ALU.add)
 
-        def damage(ys, words, scales, width, passes=range(PASSES)):
-            for g in passes:
-                for n, (y, opens, closes) in enumerate(ys):
-                    nc.tensor.matmul_mx(
-                        out=y,
-                        lhsT=w3_w[:, g, n * P : (n + 1) * P].bitcast(FP8X4),
-                        lhsT_scale=w3_s[:, g, n * P : (n + 1) * P],
-                        rhs=words[:, g * width : (g + 1) * width].bitcast(FP8X4),
-                        rhs_scale=scales[:, g * width : (g + 1) * width],
-                        start=(g == 0 and opens),
-                        stop=(g == 1 and closes),
-                    )
+        def damage(ys, words, scales, g):
+            for n, (y, opens, closes) in enumerate(ys):
+                nc.tensor.matmul_mx(
+                    out=y,
+                    lhsT=w3_w[:, g, n * P : (n + 1) * P].bitcast(FP8X4),
+                    lhsT_scale=w3_s[:, g, n * P : (n + 1) * P],
+                    rhs=words.bitcast(FP8X4),
+                    rhs_scale=scales,
+                    start=(g == 0 and opens),
+                    stop=(g == 1 and closes),
+                )
 
         def add_bias_and_store(ys, y_out, cols):
             for n in range(N_TILES):
@@ -280,13 +286,13 @@ def tile_list_frost_risk_map_kernel(
         load_rows(7)
         load_w1(1, 0)
         load_w1(0, 1)
-        load_scales(w3_s, w3_scales)
         load_w1(1, 1)
         load_table(0)
-        with nc.allow_non_contiguous_dma(reason="one bias value to a partition"):
-            nc.sync.dma_start(out=b_sb[:], in_=b.rearrange("(n p) -> p n", p=P))
         load_table(1)
         nc.sync.dma_start(out=w3_w[:], in_=w3_words.rearrange("a p c i -> p a (c i)").bitcast(I32))
+        load_scales(w3_s, w3_scales)
+        with nc.allow_non_contiguous_dma(reason="one bias value to a partition"):
+            nc.sync.dma_start(out=b_sb[:], in_=b.rearrange("(n p) -> p n", p=P))
 
         nc.scalar.copy(
             out=w2_w[:].rearrange("p (s t u) -> p s t u", t=PACK, u=P),
@@ -307,8 +313,7 @@ def tile_list_frost_risk_map_kernel(
                 round_w1(0, 0)
                 quantise(w1_bf[0, 0], w1_w[0, 0], w1_s[0, 0])
             subtract_pair(picked, x0_pairs[:, u, :])
-        x0_bf = held("x0_bf", [P, PACK * S], BF16)
-        weave(x0_pairs, x0_bf)
+        weave(x0_pairs, mid_bf[:, 0 : PACK * S])
 
         x1_pairs0 = held("x1_pairs0", [P, 2, 2 * HALF], BF16)
         for u in range(2):
@@ -318,15 +323,19 @@ def tile_list_frost_risk_map_kernel(
             subtract_pair(picked, x1_pairs0[:, u, :])
         round_w1(1, 0)
         x1_bf0 = held("x1_bf0", [P, PACK * HALF], BF16, on="w1_f32_10", skip=KB)
-        weave(x1_pairs0, x1_bf0)
+        weave(x1_pairs0, x1_bf0[:])
+
+        rounded, values = w1_views(0, 1, slice(0, GPSIMD_WORDS))
+        nc.gpsimd.tensor_copy(out=rounded.rearrange("p u i t -> p u t i"), in_=values.rearrange("p u i t -> p u t i"))
+        round_w1(0, 1, slice(GPSIMD_WORDS, P))
+        round_w1(1, 1)
 
         picked_a = rows[3].rearrange("p (l e c) -> p l e c", l=2, e=2)
         for e in range(2):
             pick(PACK + e, halves[1], picked_a)
-        x0_w, x0_s = held("x0_w", [P, S], U32, on="rows4"), held("x0_s", [P, S], U8)
-        quantise(x0_bf[:], x0_w[:], x0_s[:])
-        w1_w[1, 0] = held("w1_w10", [P, KP], U32, on="rows4", skip=2 * KB)[:]
-        quantise(w1_bf[1, 0], w1_w[1, 0], w1_s[1, 0])
+        mid_w = held("mid_w", [P, S + KP], U32, on="rows4")
+        quantise(mid_bf[:], mid_w[:], mid_s[:])
+        x0_w, x0_s, w1_w[1, 0] = mid_w[:, 0:S], mid_s[:, 0:S], mid_w[:, S:]
         x1_w[0], x1_s[0] = held("x1_w0", [P, HALF], U32), held("x1_s0", [P, HALF], U8)
         quantise(x1_bf0[:], x1_w[0][:], x1_s[0][:])
         x1_pairs1 = held("x1_pairs1", [P, 2, 2 * HALF], BF16, on="w1_f32_10")
@@ -334,84 +343,91 @@ def tile_list_frost_risk_map_kernel(
         picked_b = held("picked111", [P, 2, 2, HALF], F32, on="w1_f32_10", skip=2 * KB)
         for e in range(2):
             pick(PACK + 2 + e, halves[1], picked_b)
-        for a in range(PASSES):
-            round_w1(a, 1)
         v_w[0] = held("v_w0", [P, S], U32, on="rows6")
         gather_words(0)
         subtract_pair(picked_b, x1_pairs1[:, 1, :])
         x1_bf1 = held("x1_bf1", [P, PACK * HALF], BF16, on="last_w1", skip=ALIGN + 8 * KB)
-        inner_pair(0, 0, 0, 0, on="last_w1", skip=ALIGN)
-        response_to_sbuf(0)
-        weave(x1_pairs1, x1_bf1)
-        inner_pair(0, 0, 1, 1, on="last_w1", skip=ALIGN + 4 * KB)
-        response_to_sbuf(1)
+        for pair in range(2):
+            inner_pair(0, 0, pair, pair, on="last_w1", skip=ALIGN + 4 * pair * KB)
+            response_to_sbuf(pair)
+        weave(x1_pairs1, x1_bf1[:])
         w1_w1 = held("w1_w1", [P, PASSES * KP], U32, on="tab_w0")
         for a in range(PASSES):
             w1_w[a, 1] = w1_w1[:, a * KP : (a + 1) * KP]
         quantise(w1_bf1[:], w1_w1[:], w1_s1[:])
-        x1_w[1], x1_s[1] = held("x1_w1", [P, HALF], U32, on="tab_w0", skip=4 * KB), held("x1_s1", [P, HALF], U8)
-        quantise(x1_bf1[:], x1_w[1][:], x1_s[1][:])
         v_w[1] = held("v_w1", [P, S], U32)
         gather_words(1)
+        x1_w[1], x1_s[1] = held("x1_w1", [P, HALF], U32, on="tab_w1"), held("x1_s1", [P, HALF], U8)
+        quantise(x1_bf1[:], x1_w[1][:], x1_s[1][:])
 
-        quad[0, 0] = held("quad00", [P, 2, HALF, 2], F32, on="x1_bf1", skip=KB)
-        quad[1, 0] = held("quad10", [P, 2, HALF, 2], F32, on="tab_w1")
+        quad[0, 0] = held("quad00", [P, 2, HALF, 2], F32, on="w1_bf1")
+        quad[1, 0] = held("quad10", [P, 2, HALF, 2], F32, on="tab_w1", skip=4 * KB)
         for g in range(PASSES):
             quad[g, 1] = held(f"quad{g}1", [P, 2, HALF, 2], F32, on="picked00", skip=g * 4 * KB)
 
         for pair in range(2):
             outer_pair_gpsimd(pair)
             inner_pair(1, 0, pair, 2 + pair)
-        for q in range(2):
-            hardiness_quarter(0, q, 6 + q)
-            hardiness_to_sbuf(q)
-        for q in range(2):
-            hardiness_quarter(1, q, q)
-        for pair in range(2):
-            inner_pair(0, 1, pair, 4 + pair)
+        hardiness_quarter(0, 0, 6)
+        hardiness_to_sbuf(0)
+        hardiness_quarter(1, 0, 0)
+        inner_pair(0, 1, 0, 4)
+        hardiness_quarter(0, 1, 7)
+        hardiness_to_sbuf(1)
+        hardiness_quarter(1, 1, 1)
+        inner_pair(0, 1, 1, 5)
         for pair in range(2):
             outer_pair(1, 0, pair)
         h_bf = held("h_bf", [P, 4 * KP], BF16)
         h_w, h_s = held("h_w", [P, 4 * P], U32), held("h_s", [P, 4 * P], U8)
         for q in range(2):
             add_hardiness_gpsimd(q, h_bf[:, q * KP : (q + 1) * KP])
+        hardiness_quarter(0, 2, 2)
+        hardiness_to_sbuf(2)
         for pair in range(2):
             inner_pair(1, 1, pair, 6 + pair)
-        for g in range(PASSES):
-            hardiness_quarter(g, 2, 2 + g)
-        hardiness_to_sbuf(2)
+        hardiness_quarter(1, 2, 3)
+        outer_pair(0, 1, 0)
         for q in range(2):
             add_hardiness(1, q, h_bf[:, (2 + q) * KP : (3 + q) * KP])
-        for g in range(PASSES):
-            hardiness_quarter(g, 3, g)
-        for pair in range(2):
-            outer_pair(0, 1, pair)
+        hardiness_quarter(0, 3, 0)
+        hardiness_to_sbuf(3, SHARED)
+        outer_pair(0, 1, 1)
         quantise(h_bf[:], h_w[:], h_s[:])
+
         two, one = bank(4, [P, 2, HALF]), bank(5, [P, HALF])
         ys_half = [(two[:, 0, :], True, False), (two[:, 1, :], False, True), (one[:], True, True)]
-        damage(ys_half, h_w, h_s, HALF)
+        for g in range(PASSES):
+            damage(ys_half, h_w[:, halves[g]], h_s[:, halves[g]], g)
         y_half = held("y_half", [P, N_TILES, HALF], F32)
         add_bias_and_store(ys_half, y_half, halves[0])
 
-        h2_bf = held("h2_bf", [P, 2 * KP], BF16, on="h_bf")
-        h3_bf = held("h3_bf", [P, 2 * KP], BF16, on="h_bf", skip=2 * KB)
-        add_hardiness_gpsimd(2, h2_bf[:, 0:KP])
+        h0_bf, h1_bf = held("h0_bf", [P, 2 * KP], BF16, on="h_bf"), held("h1_bf", [P, 2 * KP], BF16, on="h_bf", skip=2 * KB)
+        late_w, late_s = held("late_w", [P, 4 * P], U32), held("late_s", [P, 4 * P], U8)
+        add_hardiness_gpsimd(2, h0_bf[:, 0:KP])
+        add_hardiness_gpsimd(3, h0_bf[:, KP : 2 * KP], slice(0, SHARED))
         for pair in range(2):
             outer_pair(1, 1, pair)
-        add_hardiness(0, 3, h3_bf[:, 0:KP])
-        add_hardiness(1, 2, h2_bf[:, KP : 2 * KP])
-        add_hardiness(1, 3, h3_bf[:, KP : 2 * KP])
-        h2_w, h2_s = held("h2_w", [P, 2 * P], U32), held("h2_s", [P, 2 * P], U8)
-        h3_w, h3_s = held("h3_w", [P, 2 * P], U32), held("h3_s", [P, 2 * P], U8)
-        quantise(h2_bf[:], h2_w[:], h2_s[:])
-        quantise(h3_bf[:], h3_w[:], h3_s[:])
+        hardiness_quarter(1, 3, 7)
+        add_hardiness(0, 3, h0_bf[:, KP : 2 * KP], slice(SHARED, QUARTER))
+        for q in (2, 3):
+            add_hardiness(1, q, h1_bf[:, (q - 2) * KP : (q - 1) * KP])
         three = bank(2, [P, N_TILES, P])
         ys_third = [(three[:, n, :], n == 0, n == N_TILES - 1) for n in range(N_TILES)]
-        damage(ys_third, h2_w, h2_s, QUARTER)
+        ys = [bank(number, [P, P]) for number in (0, 6, 1)]
+        ys_last = [(y[:], True, True) for y in ys]
+        quantise(h0_bf[:], late_w[:, 0:HALF], late_s[:, 0:HALF])
+        damage(ys_third, late_w[:, 0:P], late_s[:, 0:P], 0)
+        damage(ys_last, late_w[:, P:HALF], late_s[:, P:HALF], 0)
+        for n, group in enumerate((ys_third, ys_last)):
+            cols = slice(HALF + n * P, HALF + (n + 1) * P)
+            quantise(h1_bf[:, n * KP : (n + 1) * KP], late_w[:, cols], late_s[:, cols])
+            damage(group, late_w[:, cols], late_s[:, cols], 1)
         y_third = held("y_third", [P, N_TILES, P], F32)
-        ys = [bank(number, [P, P]) for number in (3, 6, 7)]
-        damage([(y[:], True, True) for y in ys], h3_w, h3_s, QUARTER)
-        add_bias_and_store(ys_third, y_third, slice(HALF, HALF + QUARTER))
+        for n in range(N_TILES):
+            nc.scalar.activation(out=y_third[:, n, :], in_=three[:, n, :], func=ACT.Identity, bias=b_sb[:, n : n + 1])
+        by_tile = out.rearrange("(n p) j -> p n j", p=P)
+        nc.sync.dma_start(out=by_tile[:, :, HALF : HALF + QUARTER], in_=y_third[:])
         y_last = held("y_last", [P, N_TILES, P], F32)
         for n in range(N_TILES):
             nc.vector.tensor_scalar_add(out=y_last[:, n, :], in0=ys[n][:], scalar1=b_sb[:, n : n + 1])

@@ -31,7 +31,6 @@ STRIPE = 16
 RUN = 4
 KB = 1024
 SHARED = 64
-GPSIMD_WORDS = 48
 ALIGN = 256
 
 
@@ -142,15 +141,12 @@ def tile_list_frost_risk_map_kernel(
         def quantise(bf, words, scales):
             nc.vector.quantize_mx(out=words.bitcast(FP8X4), scales=scales, in_=bf)
 
-        def w1_views(a, g, words):
-            return (
-                w1_bf[a, g].rearrange("p (t u i) -> p u i t", t=PACK, i=PACK)[:, words, :, :],
-                w1_f32[a, g][:].rearrange("p i (u t) -> p u i t", t=PACK)[:, words, :, :],
+        def round_w1(a, g):
+            nc.scalar.activation(
+                out=w1_bf[a, g].rearrange("p (t u i) -> p u i t", t=PACK, i=PACK),
+                in_=w1_f32[a, g][:].rearrange("p i (u t) -> p u i t", t=PACK),
+                func=ACT.Copy,
             )
-
-        def round_w1(a, g, words=slice(0, P)):
-            rounded, values = w1_views(a, g, words)
-            nc.scalar.activation(out=rounded, in_=values, func=ACT.Copy)
 
         def gather_words(a):
             nc.vector.tensor_copy(out=v_w[a][:], in_=tab_w[a][:].bitcast(U32).indirect(idx[:]))
@@ -325,9 +321,7 @@ def tile_list_frost_risk_map_kernel(
         x1_bf0 = held("x1_bf0", [P, PACK * HALF], BF16, on="w1_f32_10", skip=KB)
         weave(x1_pairs0, x1_bf0[:])
 
-        rounded, values = w1_views(0, 1, slice(0, GPSIMD_WORDS))
-        nc.gpsimd.tensor_copy(out=rounded.rearrange("p u i t -> p u t i"), in_=values.rearrange("p u i t -> p u t i"))
-        round_w1(0, 1, slice(GPSIMD_WORDS, P))
+        round_w1(0, 1)
         round_w1(1, 1)
 
         picked_a = rows[3].rearrange("p (l e c) -> p l e c", l=2, e=2)

@@ -30,7 +30,6 @@ BLOCKS = 16
 STRIPE = 16
 RUN = 4
 KB = 1024
-SHARED = 64
 ALIGN = 256
 
 
@@ -384,9 +383,10 @@ def tile_list_frost_risk_map_kernel(
         outer_pair(0, 1, 0)
         for q in range(2):
             add_hardiness(1, q, h_bf[:, (2 + q) * KP : (3 + q) * KP])
-        hardiness_quarter(0, 3, 0)
-        hardiness_to_sbuf(3, SHARED)
+        for g in range(PASSES):
+            hardiness_quarter(g, 3, g)
         outer_pair(0, 1, 1)
+        outer_pair(1, 1, 0)
         quantise(h_bf[:], h_w[:], h_s[:])
 
         two, one = bank(4, [P, 2, HALF]), bank(5, [P, HALF])
@@ -399,31 +399,27 @@ def tile_list_frost_risk_map_kernel(
         h0_bf, h1_bf = held("h0_bf", [P, 2 * KP], BF16, on="h_bf"), held("h1_bf", [P, 2 * KP], BF16, on="h_bf", skip=2 * KB)
         late_w, late_s = held("late_w", [P, 4 * P], U32), held("late_s", [P, 4 * P], U8)
         add_hardiness_gpsimd(2, h0_bf[:, 0:KP])
-        add_hardiness_gpsimd(3, h0_bf[:, KP : 2 * KP], slice(0, SHARED))
-        for pair in range(2):
-            outer_pair(1, 1, pair)
-        hardiness_quarter(1, 3, 7)
-        add_hardiness(0, 3, h0_bf[:, KP : 2 * KP], slice(SHARED, QUARTER))
-        for q in (2, 3):
-            add_hardiness(1, q, h1_bf[:, (q - 2) * KP : (q - 1) * KP])
+        outer_pair(1, 1, 1)
+        add_hardiness(0, 3, h0_bf[:, KP : 2 * KP])
+        add_hardiness(1, 2, h1_bf[:, 0:KP])
         three = bank(2, [P, N_TILES, P])
         ys_third = [(three[:, n, :], n == 0, n == N_TILES - 1) for n in range(N_TILES)]
-        ys = [bank(number, [P, P]) for number in (0, 6, 1)]
+        ys = [bank(number, [P, P]) for number in (0, 6, 7)]
         ys_last = [(y[:], True, True) for y in ys]
         quantise(h0_bf[:], late_w[:, 0:HALF], late_s[:, 0:HALF])
         damage(ys_third, late_w[:, 0:P], late_s[:, 0:P], 0)
         damage(ys_last, late_w[:, P:HALF], late_s[:, P:HALF], 0)
         for n, group in enumerate((ys_third, ys_last)):
             cols = slice(HALF + n * P, HALF + (n + 1) * P)
+            if n == 1:
+                add_hardiness(1, 3, h1_bf[:, KP : 2 * KP])
             quantise(h1_bf[:, n * KP : (n + 1) * KP], late_w[:, cols], late_s[:, cols])
             damage(group, late_w[:, cols], late_s[:, cols], 1)
         y_third = held("y_third", [P, N_TILES, P], F32)
-        for n in range(N_TILES):
-            nc.scalar.activation(out=y_third[:, n, :], in_=three[:, n, :], func=ACT.Identity, bias=b_sb[:, n : n + 1])
-        by_tile = out.rearrange("(n p) j -> p n j", p=P)
-        nc.sync.dma_start(out=by_tile[:, :, HALF : HALF + QUARTER], in_=y_third[:])
+        add_bias_and_store(ys_third, y_third, slice(HALF, HALF + QUARTER))
         y_last = held("y_last", [P, N_TILES, P], F32)
-        for n in range(N_TILES):
-            nc.vector.tensor_scalar_add(out=y_last[:, n, :], in0=ys[n][:], scalar1=b_sb[:, n : n + 1])
-        for n, queue in enumerate((nc.scalar, nc.sync, nc.scalar)):
+        nc.vector.tensor_scalar_add(out=y_last[:, 0, :], in0=ys[0][:], scalar1=b_sb[:, 0:1])
+        nc.scalar.activation(out=y_last[:, 1, :], in_=ys[1][:], func=ACT.Identity, bias=b_sb[:, 1:2])
+        nc.vector.tensor_scalar_add(out=y_last[:, 2, :], in0=ys[2][:], scalar1=b_sb[:, 2:3])
+        for n, queue in enumerate((nc.sync, nc.scalar, nc.sync)):
             queue.dma_start(out=out[n * P : (n + 1) * P, HALF + QUARTER : S], in_=y_last[:, n, :])

@@ -85,11 +85,9 @@ def tile_list_frost_risk_map_kernel(
         w1_bf = {(0, 0): held("w1_bf00", [P, PACK * KP], BF16)[:], (1, 0): mid_bf[:, PACK * S :]}
         w1_w = {(0, 0): held("w1_w00", [P, KP], U32)[:]}
         w1_s = {(0, 0): held("w1_s00", [P, KP], U8)[:], (1, 0): mid_s[:, S:]}
-        w1_bf1 = held("w1_bf1", [P, PASSES * PACK * KP], BF16)
-        w1_s1 = held("w1_s1", [P, PASSES * KP], U8)
         for a in range(PASSES):
-            w1_bf[a, 1] = w1_bf1[:, a * PACK * KP : (a + 1) * PACK * KP]
-            w1_s[a, 1] = w1_s1[:, a * KP : (a + 1) * KP]
+            w1_bf[a, 1] = held(f"w1_bf{a}1", [P, PACK * KP], BF16)[:]
+            w1_s[a, 1] = held(f"w1_s{a}1", [P, KP], U8)[:]
 
         nc.vector.memset(tab_s[2 * QUADRANT : P, :].bitcast(I32), 0)
         for part in (tab_s[QUADRANT : 2 * QUADRANT, :], w2_s_raw[:], v_s[0][:], v_s[1][:], w3_s[:]):
@@ -336,24 +334,25 @@ def tile_list_frost_risk_map_kernel(
         picked_b = held("picked111", [P, 2, 2, HALF], F32, on="w1_f32_10", skip=2 * KB)
         for e in range(2):
             pick(PACK + 2 + e, halves[1], picked_b)
+        w1_w[0, 1] = held("w1_w01", [P, KP], U32, on="rows6", skip=2 * KB)[:]
+        quantise(w1_bf[0, 1], w1_w[0, 1], w1_s[0, 1])
         v_w[0] = held("v_w0", [P, S], U32, on="rows6")
         gather_words(0)
         subtract_pair(picked_b, x1_pairs1[:, 1, :])
         x1_bf1 = held("x1_bf1", [P, PACK * HALF], BF16, on="last_w1", skip=ALIGN + 8 * KB)
-        for pair in range(2):
-            inner_pair(0, 0, pair, pair, on="last_w1", skip=ALIGN + 4 * pair * KB)
-            response_to_sbuf(pair)
+        inner_pair(0, 0, 0, 0, on="last_w1", skip=ALIGN)
+        response_to_sbuf(0)
         weave(x1_pairs1, x1_bf1[:])
-        w1_w1 = held("w1_w1", [P, PASSES * KP], U32, on="tab_w0")
-        for a in range(PASSES):
-            w1_w[a, 1] = w1_w1[:, a * KP : (a + 1) * KP]
-        quantise(w1_bf1[:], w1_w1[:], w1_s1[:])
+        inner_pair(0, 0, 1, 1, on="last_w1", skip=ALIGN + 4 * KB)
+        response_to_sbuf(1)
+        w1_w[1, 1] = held("w1_w11", [P, KP], U32, on="tab_w0")[:]
+        quantise(w1_bf[1, 1], w1_w[1, 1], w1_s[1, 1])
         v_w[1] = held("v_w1", [P, S], U32)
         gather_words(1)
         x1_w[1], x1_s[1] = held("x1_w1", [P, HALF], U32, on="tab_w1"), held("x1_s1", [P, HALF], U8)
         quantise(x1_bf1[:], x1_w[1][:], x1_s[1][:])
 
-        quad[0, 0] = held("quad00", [P, 2, HALF, 2], F32, on="w1_bf1")
+        quad[0, 0] = held("quad00", [P, 2, HALF, 2], F32, on="w1_bf11")
         quad[1, 0] = held("quad10", [P, 2, HALF, 2], F32, on="tab_w1", skip=4 * KB)
         for g in range(PASSES):
             quad[g, 1] = held(f"quad{g}1", [P, 2, HALF, 2], F32, on="picked00", skip=g * 4 * KB)
@@ -375,10 +374,10 @@ def tile_list_frost_risk_map_kernel(
         h_w, h_s = held("h_w", [P, 4 * P], U32), held("h_s", [P, 4 * P], U8)
         for q in range(2):
             add_hardiness_gpsimd(q, h_bf[:, q * KP : (q + 1) * KP])
+        inner_pair(1, 1, 0, 6)
         hardiness_quarter(0, 2, 2)
         hardiness_to_sbuf(2)
-        for pair in range(2):
-            inner_pair(1, 1, pair, 6 + pair)
+        inner_pair(1, 1, 1, 7)
         hardiness_quarter(1, 2, 3)
         outer_pair(0, 1, 0)
         for q in range(2):

@@ -325,7 +325,8 @@ def tile_list_frost_risk_map_kernel(
         for e in range(2):
             pick(PACK + e, halves[1], picked_a)
         mid_w = held("mid_w", [P, S + KP], U32, on="rows4")
-        quantise(mid_bf[:], mid_w[:], mid_s[:])
+        for n in range(2):
+            quantise(mid_bf[:, n * PACK * S : (n + 1) * PACK * S], mid_w[:, n * S : (n + 1) * S], mid_s[:, n * S : (n + 1) * S])
         x0_w, x0_s, w1_w[1, 0] = mid_w[:, 0:S], mid_s[:, 0:S], mid_w[:, S:]
         x1_w[0], x1_s[0] = held("x1_w0", [P, HALF], U32), held("x1_s0", [P, HALF], U8)
         quantise(x1_bf0[:], x1_w[0][:], x1_s[0][:])

@@ -332,7 +332,7 @@ def tile_list_frost_risk_map_kernel(
         quantise(x1_bf0[:], x1_w[0][:], x1_s[0][:])
         x1_pairs1 = held("x1_pairs1", [P, 2, 2 * HALF], BF16, on="w1_f32_10")
         subtract_pair(picked_a, x1_pairs1[:, 0, :])
-        picked_b = held("picked111", [P, 2, 2, HALF], F32, on="w1_f32_10", skip=2 * KB)
+        picked_b = held("picked111", [P, 2, 2, HALF], F32, on="mid_bf", skip=4 * KB)
         for e in range(2):
             pick(PACK + 2 + e, halves[1], picked_b)
         w1_w[0, 1] = held("w1_w01", [P, KP], U32, on="rows6", skip=2 * KB)[:]

@@ -255,7 +255,7 @@ def tile_list_frost_risk_map_kernel(
         pairs, m, x1_w, x1_s, v_w = {}, {}, {}, {}, {}
         quad, m_sb, d_sb = {}, {}, {}
 
-        nc.sync.dma_start(
+        nc.scalar.dma_start(
             out=tab_s[0 : PASSES * BLOCKS, :].bitcast(I32), in_=tab_scales.rearrange("a n t -> (a n) t").bitcast(I32)
         )
         nc.sync.dma_start(idx[:], offs)
@@ -264,12 +264,12 @@ def tile_list_frost_risk_map_kernel(
         nc.sync.dma_start(idx2[:], offs2)
         load_rows(1)
         load_scales(w2_s_raw, w2_scales)
-        nc.sync.dma_start(out=w2_w_raw[:].bitcast(I32), in_=w2_words.rearrange("a p c -> p a c").bitcast(I32))
         load_rows(2)
         nc.vector.tensor_copy(out=v_rows[:], in_=tab_s[:].indirect(idx[:]))
         place_gathered_scales(0)
         load_w1(0, 0)
         load_rows(3)
+        nc.sync.dma_start(out=w2_w_raw[:].bitcast(I32), in_=w2_words.rearrange("a p c -> p a c").bitcast(I32))
         place_gathered_scales(1)
         load_rows(4)
         load_rows(5)

@@ -139,10 +139,9 @@ def tile_list_frost_risk_map_kernel(
             nc.vector.quantize_mx(out=words.bitcast(FP8X4), scales=scales, in_=bf)
 
         def round_w1(a, g):
-            nc.scalar.activation(
-                out=w1_bf[a, g].rearrange("p (t u i) -> p u i t", t=PACK, i=PACK),
-                in_=w1_f32[a, g][:].rearrange("p i (u t) -> p u i t", t=PACK),
-                func=ACT.Copy,
+            nc.scalar.copy(
+                out=w1_bf[a, g].rearrange("p (s e u i) -> p s u i e", s=2, e=2, i=PACK),
+                in_=w1_f32[a, g][:].rearrange("p i (u s e) -> p s u i e", s=2, e=2),
             )
 
         def gather_words(a):

import math
from contextlib import ExitStack

import concourse.mybir as mybir

K, T, T2, S, H, N = 1024, 2048, 1024, 512, 1024, 384
FLOPS = 2 * S * (K * H + K * H + H * N)

F32 = mybir.dt.float32
BF16 = mybir.dt.bfloat16
I32 = mybir.dt.int32
U32 = mybir.dt.uint32
U16 = mybir.dt.uint16
U8 = mybir.dt.uint8
FP8X4 = mybir.dt.float8_e4m3fn_x4
FP4X4 = mybir.dt.float4_e2m1fn_x4
ALU = mybir.AluOpType
ACT = mybir.ActivationFunctionType

P = 128
PACK = 4
KP = P * PACK
PASSES = 2
HALF = S // 2
QUARTER = S // 4
N_TILES = N // P
QUADRANT = 32
SCALE_ROWS = 4
BLOCKS = 16
STRIPE = 16
RUN = 4
KB = 1024
ALIGN = 256


def tile_list_frost_risk_map_kernel(
    tc, tab_words, tab_scales, offs, xT, offs2, offs3, w1, w2_words, w2_scales, c1, c2, w3_words, w3_scales, b, out
):
    nc = tc.nc
    with ExitStack() as ctx:
        lists = ctx.enter_context(tc.tile_pool(name="lists", bufs=1))
        keep = ctx.enter_context(tc.tile_pool(name="keep", bufs=1))
        psum = ctx.enter_context(tc.psum_pool(name="psum", bufs=1))
        starts, ends = {}, [0]

        def reserve(name, size):
            starts[name] = ends[-1]
            ends.append(ends[-1] + -(-size // ALIGN) * ALIGN)

        def held(name, shape, dtype, on=None, skip=0):
            if on is None:
                width = 4 if dtype in (F32, I32, U32) else 2 if dtype in (BF16, U16) else 1
                reserve(name, math.prod(shape[1:]) * width)
            else:
                starts[name] = starts[on] + skip
            return keep.tile(shape, dtype, name=name, align_bytes=ALIGN, offset=starts[name])

        def bank(number, shape):
            return psum.tile(shape, F32, name=f"bank{number}")

        idx = lists.tile([P, S // STRIPE], U16, name="idx")
        idx2 = lists.tile([P, S // STRIPE], U16, name="idx2")
        idx3 = lists.tile([P, S // STRIPE], U16, name="idx3")

        rows = {n: held(f"rows{n}", [P, T2], F32)[:] for n in (0, 1, 2, 4, 5, 6)}
        rows_7_3 = held("rows_7_3", [P, 2 * T2], F32)
        rows[7], rows[3] = rows_7_3[:, 0:T2], rows_7_3[:, T2:]
        tab_w = [held(f"tab_w{a}", [P, T], I32) for a in range(PASSES)]
        tab_s = held("tab_s", [P, T], U8)
        v_rows = held("v_rows", [P, S], U8)
        v_s = [held(f"v_s{a}", [P, S], U8) for a in range(PASSES)]
        w2_w_raw = held("w2_w_raw", [P, PASSES, 2 * H], U8)
        w2_s_raw = held("w2_s_raw", [P, PASSES, H], U8)
        w2_w = held("w2_w", [P, PASSES * H], U16)
        w2_s = [held(f"w2_s{a}", [P, H], U8) for a in range(PASSES)]
        w3_w = held("w3_w", [P, PASSES, N], I32)
        w3_s = held("w3_s", [P, PASSES, N], U8)
        c1_sb = held("c1_sb", [P, PASSES, PACK], F32)
        c2_sb = held("c2_sb", [P, PASSES, PACK], F32)
        b_sb = held("b_sb", [P, N_TILES], F32)
        w1_f32 = {(a, g): held(f"w1_f32_{a}{g}", [P, PACK, KP], F32) for a, g in ((0, 0), (1, 0), (0, 1))}
        reserve("last_w1", 14 * KB)
        w1_f32[1, 1] = held("w1_f32_11", [P, PACK, KP], F32, on="last_w1", skip=2 * KB)
        mid_bf, mid_s = held("mid_bf", [P, 2 * PACK * KP], BF16), held("mid_s", [P, 2 * KP], U8)
        w1_bf = {(0, 0): held("w1_bf00", [P, PACK * KP], BF16)[:], (1, 0): mid_bf[:, PACK * S :]}
        w1_w = {(0, 0): held("w1_w00", [P, KP], U32)[:]}
        w1_s = {(0, 0): held("w1_s00", [P, KP], U8)[:], (1, 0): mid_s[:, S:]}
        for a in range(PASSES):
            w1_bf[a, 1] = held(f"w1_bf{a}1", [P, PACK * KP], BF16)[:]
            w1_s[a, 1] = held(f"w1_s{a}1", [P, KP], U8)[:]

        nc.vector.memset(tab_s[2 * QUADRANT : P, :].bitcast(I32), 0)
        for part in (tab_s[QUADRANT : 2 * QUADRANT, :], w2_s_raw[:], v_s[0][:], v_s[1][:], w3_s[:]):
            nc.gpsimd.memset(part.bitcast(I32), 0)

        def load_rows(n):
            a, i = divmod(n, PACK)
            part = xT[a * KP : (a + 1) * KP, :].rearrange("(p i) t -> p i t", i=PACK)
            nc.sync.dma_start(out=rows[n], in_=part[:, i, :])

        def load_table(a):
            nc.sync.dma_start(out=tab_w[a][:], in_=tab_words[a].rearrange("p t i -> p (t i)").bitcast(I32))

        def load_w1(a, g):
            part = w1[a * KP : (a + 1) * KP, g * KP : (g + 1) * KP]
            nc.sync.dma_start(out=w1_f32[a, g][:], in_=part.rearrange("(p i) c -> p i c", i=PACK))

        def load_scales(tile, scales):
            for row in range(SCALE_ROWS):
                part = scales[:, row:BLOCKS:SCALE_ROWS, :].rearrange("a n c -> n a c")
                nc.sync.dma_start(out=tile[row:P:QUADRANT, :, :].bitcast(I32), in_=part.bitcast(I32))

        def place_gathered_scales(a):
            for row in range(SCALE_ROWS):
                part = v_rows[BLOCKS * a + row : BLOCKS * (a + 1) : SCALE_ROWS, :]
                nc.sync.dma_start(out=v_s[a][row:P:QUADRANT, :].bitcast(I32), in_=part.bitcast(I32))

        def pick(n, cols, picked, wide=None):
            entries = slice(cols.start // STRIPE, cols.stop // STRIPE)
            for l, offsets in enumerate((idx3, idx2)):
                window = wide if wide is not None and l == 0 else rows[n]
                nc.vector.tensor_copy(out=picked[:, l, n % 2, :], in_=window.indirect(offsets[:, entries]))

        def subtract_pair(picked, x_pair):
            nc.gpsimd.tensor_tensor(
                out=x_pair.rearrange("p (c r e) -> p c e r", r=RUN, e=2),
                in0=picked[:, 1, :, :].rearrange("p e (c r) -> p c e r", r=RUN),
                in1=picked[:, 0, :, :].rearrange("p e (c r) -> p c e r", r=RUN),
                op=ALU.subtract,
            )

        def weave(x_pairs, x_bf):
            nc.scalar.copy(
                out=x_bf.bitcast(U32).rearrange("p (c u) -> p c u", u=2),
                in_=x_pairs[:].bitcast(U32).rearrange("p u c -> p c u"),
            )

        def quantise(bf, words, scales):
            nc.vector.quantize_mx(out=words.bitcast(FP8X4), scales=scales, in_=bf)

        def round_w1(a, g):
            nc.scalar.copy(
                out=w1_bf[a, g].rearrange("p (s e u i) -> p s u i e", s=2, e=2, i=PACK),
                in_=w1_f32[a, g][:].rearrange("p i (u s e) -> p s u i e", s=2, e=2),
            )

        def gather_words(a):
            nc.vector.tensor_copy(out=v_w[a][:], in_=tab_w[a][:].bitcast(U32).indirect(idx[:]))

        def hardiness_pass(y, a, g, t, cols, start, stop):
            first = a * H + g * KP + t * P
            nc.tensor.matmul_mx(
                out=y,
                lhsT=w2_w[:, first : first + P].bitcast(FP4X4),
                lhsT_scale=w2_s[a][:, g * KP + t * P : g * KP + (t + 1) * P],
                rhs=v_w[a][:, cols].bitcast(FP8X4),
                rhs_scale=v_s[a][:, cols],
                start=start,
                stop=stop,
            )

        def hardiness_quarter(g, q, number):
            m[g, q] = bank(number, [P, PACK, QUARTER])
            for a in range(PASSES):
                for t in range(PACK):
                    cols = slice(q * QUARTER, (q + 1) * QUARTER)
                    hardiness_pass(m[g, q][:, t, :], a, g, t, cols, (a, t) == (0, 0), (a, t) == (1, PACK - 1))

        def hardiness_to_sbuf(q, count=QUARTER):
            m_sb[q] = held(f"m_sb{q}", [P, count, PACK], F32)
            nc.scalar.activation(out=m_sb[q][:], in_=m[0, q][:, :, 0:count].rearrange("p t j -> p j t"), func=ACT.Copy)

        def response_to_sbuf(pair):
            d_sb[pair] = held(f"d_sb{pair}", [P, HALF, 2], F32, on="last_w1", skip=ALIGN + (4 * pair + 2) * KB)
            nc.scalar.activation(out=d_sb[pair][:], in_=pairs[0, 0, pair][0][:].rearrange("p e j -> p j e"), func=ACT.Copy)

        def outer_pair_gpsimd(pair):
            nc.gpsimd.tensor_tensor(
                out=quad[0, 0][:, pair, :, :],
                in0=d_sb[pair][:],
                in1=pairs[0, 0, pair][1][:].rearrange("p e j -> p j e"),
                op=ALU.mult,
            )

        def inner_pair(g, half, pair, number, **place):
            d = bank(number, [P, 2, HALF])
            inner = held(f"inner{g}{half}{pair}", [P, 2, HALF], F32, **place)
            for a in range(PASSES):
                x_w, x_s = (x0_w[:, halves[half]], x0_s[:, halves[half]]) if a == 0 else (x1_w[half][:], x1_s[half][:])
                for e in range(2):
                    t = 2 * pair + e
                    nc.tensor.matmul_mx(
                        out=d[:, e, :],
                        lhsT=w1_w[a, g][:, t * P : (t + 1) * P].bitcast(FP8X4),
                        lhsT_scale=w1_s[a, g][:, t * P : (t + 1) * P],
                        rhs=x_w.bitcast(FP8X4),
                        rhs_scale=x_s,
                        start=(a, e) == (0, 0),
                        stop=(a, e) == (1, 1),
                    )
            for e in range(2):
                t = 2 * pair + e
                nc.scalar.activation(
                    out=inner[:, e, :],
                    in_=d[:, e, :],
                    func=ACT.Identity,
                    scale=c2_sb[:, g, t : t + 1],
                    bias=c1_sb[:, g, t : t + 1],
                )
            pairs[g, half, pair] = d, inner

        def outer_pair(g, half, pair, cols=slice(0, HALF)):
            d, inner = pairs[g, half, pair]
            nc.vector.tensor_tensor(
                out=quad[g, half][:, pair, cols, :],
                in0=d[:, :, cols].rearrange("p e j -> p j e"),
                in1=inner[:, :, cols].rearrange("p e j -> p j e"),
                op=ALU.mult,
            )

        def sum_operands(g, q, h_part, cols):
            terms = quad[g, q // 2][:, :, (q % 2) * QUARTER : (q % 2 + 1) * QUARTER, :]
            h_part = h_part.rearrange("p (j pair e) -> p j pair e", pair=2, e=2)
            return h_part[:, cols, :, :], terms.rearrange("p pair j e -> p j pair e")[:, cols, :, :]

        def add_hardiness_gpsimd(q, h_part, cols=slice(0, QUARTER)):
            h_part, terms = sum_operands(0, q, h_part, cols)
            m_part = m_sb[q][:].rearrange("p j (pair e) -> p j pair e", e=2)
            nc.gpsimd.tensor_tensor(out=h_part, in0=m_part, in1=terms, op=ALU.add)

        def add_hardiness(g, q, h_part, cols=slice(0, QUARTER)):
            h_part, terms = sum_operands(g, q, h_part, cols)
            m_part = m[g, q][:, :, cols].rearrange("p (pair e) j -> p j pair e", e=2)
            nc.vector.tensor_tensor(out=h_part, in0=m_part, in1=terms, op=ALU.add)

        def damage(ys, words, scales, g):
            for n, (y, opens, closes) in enumerate(ys):
                nc.tensor.matmul_mx(
                    out=y,
                    lhsT=w3_w[:, g, n * P : (n + 1) * P].bitcast(FP8X4),
                    lhsT_scale=w3_s[:, g, n * P : (n + 1) * P],
                    rhs=words.bitcast(FP8X4),
                    rhs_scale=scales,
                    start=(g == 0 and opens),
                    stop=(g == 1 and closes),
                )

        def add_bias_and_store(ys, y_out, cols):
            for n in range(N_TILES):
                nc.scalar.activation(out=y_out[:, n, :], in_=ys[n][0], func=ACT.Identity, bias=b_sb[:, n : n + 1])
                nc.sync.dma_start(out=out[n * P : (n + 1) * P, cols], in_=y_out[:, n, :])

        whole, halves = slice(0, S), (slice(0, HALF), slice(HALF, S))
        pairs, m, x1_w, x1_s, v_w = {}, {}, {}, {}, {}
        quad, m_sb, d_sb = {}, {}, {}

        nc.scalar.dma_start(
            out=tab_s[0 : PASSES * BLOCKS, :].bitcast(I32), in_=tab_scales.rearrange("a n t -> (a n) t").bitcast(I32)
        )
        nc.sync.dma_start(idx[:], offs)
        load_rows(0)
        nc.sync.dma_start(idx3[:], offs3)
        nc.sync.dma_start(idx2[:], offs2)
        load_rows(1)
        load_scales(w2_s_raw, w2_scales)
        load_rows(2)
        nc.vector.tensor_copy(out=v_rows[:], in_=tab_s[:].indirect(idx[:]))
        place_gathered_scales(0)
        load_w1(0, 0)
        load_rows(3)
        nc.sync.dma_start(out=w2_w_raw[:].bitcast(I32), in_=w2_words.rearrange("a p c -> p a c").bitcast(I32))
        place_gathered_scales(1)
        load_rows(4)
        load_rows(5)
        nc.sync.dma_start(out=c1_sb[:], in_=c1.rearrange("(g p t) -> p g t", g=PASSES, t=PACK))
        nc.sync.dma_start(out=c2_sb[:], in_=c2.rearrange("(g p t) -> p g t", g=PASSES, t=PACK))
        load_rows(6)
        load_rows(7)
        load_w1(1, 0)
        load_w1(0, 1)
        load_w1(1, 1)
        load_table(0)
        load_table(1)
        nc.sync.dma_start(out=w3_w[:], in_=w3_words.rearrange("a p c i -> p a (c i)").bitcast(I32))
        load_scales(w3_s, w3_scales)
        with nc.allow_non_contiguous_dma(reason="one bias value to a partition"):
            nc.sync.dma_start(out=b_sb[:], in_=b.rearrange("(n p) -> p n", p=P))

        nc.scalar.copy(
            out=w2_w[:].rearrange("p (s t u) -> p s t u", t=PACK, u=P),
            in_=w2_w_raw[:].rearrange("p a c -> p (a c)").bitcast(U16).rearrange("p (s u t) -> p s t u", t=PACK, u=P),
        )
        for a in range(PASSES):
            nc.gpsimd.tensor_copy(
                out=w2_s[a][:].rearrange("p (g t u) -> p g t u", t=PACK, u=P),
                in_=w2_s_raw[:, a, :].rearrange("p (g u t) -> p g t u", t=PACK, u=P),
            )

        x0_pairs = held("x0_pairs", [P, 2, 2 * S], BF16)
        for u in range(2):
            picked = held(f"picked0{u}", [P, 2, 2, S], F32)
            for e in range(2):
                pick(2 * u + e, whole, picked)
            if u == 1:
                round_w1(0, 0)
                quantise(w1_bf[0, 0], w1_w[0, 0], w1_s[0, 0])
            subtract_pair(picked, x0_pairs[:, u, :])
        weave(x0_pairs, mid_bf[:, 0 : PACK * S])

        x1_pairs0 = held("x1_pairs0", [P, 2, 2 * HALF], BF16)
        for u in range(2):
            picked = held(f"picked10{u}", [P, 2, 2, HALF], F32)
            pick(PACK + 2 * u, halves[0], picked)
            pick(PACK + 2 * u + 1, halves[0], picked, rows_7_3[:] if u == 1 else None)
            subtract_pair(picked, x1_pairs0[:, u, :])
        round_w1(1, 0)
        x1_bf0 = held("x1_bf0", [P, PACK * HALF], BF16, on="w1_f32_10", skip=KB)
        weave(x1_pairs0, x1_bf0[:])

        round_w1(0, 1)
        round_w1(1, 1)

        picked_a = rows[3].rearrange("p (l e c) -> p l e c", l=2, e=2)
        for e in range(2):
            pick(PACK + e, halves[1], picked_a)
        mid_w = held("mid_w", [P, S + KP], U32, on="rows4")
        for n in range(2):
            quantise(mid_bf[:, n * PACK * S : (n + 1) * PACK * S], mid_w[:, n * S : (n + 1) * S], mid_s[:, n * S : (n + 1) * S])
        x0_w, x0_s, w1_w[1, 0] = mid_w[:, 0:S], mid_s[:, 0:S], mid_w[:, S:]
        x1_w[0], x1_s[0] = held("x1_w0", [P, HALF], U32), held("x1_s0", [P, HALF], U8)
        quantise(x1_bf0[:], x1_w[0][:], x1_s[0][:])
        x1_pairs1 = held("x1_pairs1", [P, 2, 2 * HALF], BF16, on="w1_f32_10")
        subtract_pair(picked_a, x1_pairs1[:, 0, :])
        picked_b = held("picked111", [P, 2, 2, HALF], F32, on="mid_bf", skip=4 * KB)
        for e in range(2):
            pick(PACK + 2 + e, halves[1], picked_b)
        w1_w[0, 1] = held("w1_w01", [P, KP], U32, on="rows6", skip=2 * KB)[:]
        quantise(w1_bf[0, 1], w1_w[0, 1], w1_s[0, 1])
        v_w[0] = held("v_w0", [P, S], U32, on="rows6")
        gather_words(0)
        subtract_pair(picked_b, x1_pairs1[:, 1, :])
        x1_bf1 = held("x1_bf1", [P, PACK * HALF], BF16, on="last_w1", skip=ALIGN + 8 * KB)
        inner_pair(0, 0, 0, 0, on="last_w1", skip=ALIGN)
        response_to_sbuf(0)
        weave(x1_pairs1, x1_bf1[:])
        inner_pair(0, 0, 1, 1, on="last_w1", skip=ALIGN + 4 * KB)
        response_to_sbuf(1)
        w1_w[1, 1] = held("w1_w11", [P, KP], U32, on="tab_w0")[:]
        quantise(w1_bf[1, 1], w1_w[1, 1], w1_s[1, 1])
        v_w[1] = held("v_w1", [P, S], U32)
        gather_words(1)
        x1_w[1], x1_s[1] = held("x1_w1", [P, HALF], U32, on="tab_w1"), held("x1_s1", [P, HALF], U8)
        quantise(x1_bf1[:], x1_w[1][:], x1_s[1][:])

        quad[0, 0] = held("quad00", [P, 2, HALF, 2], F32, on="w1_bf11")
        quad[1, 0] = held("quad10", [P, 2, HALF, 2], F32, on="tab_w1", skip=4 * KB)
        for g in range(PASSES):
            quad[g, 1] = held(f"quad{g}1", [P, 2, HALF, 2], F32, on="picked00", skip=g * 4 * KB)

        for pair in range(2):
            outer_pair_gpsimd(pair)
            inner_pair(1, 0, pair, 2 + pair)
        hardiness_quarter(0, 0, 6)
        hardiness_to_sbuf(0)
        hardiness_quarter(1, 0, 0)
        inner_pair(0, 1, 0, 4)
        hardiness_quarter(0, 1, 7)
        hardiness_to_sbuf(1)
        hardiness_quarter(1, 1, 1)
        inner_pair(0, 1, 1, 5)
        for pair in range(2):
            outer_pair(1, 0, pair)
        h_bf = held("h_bf", [P, 4 * KP], BF16)
        h_w, h_s = held("h_w", [P, 4 * P], U32), held("h_s", [P, 4 * P], U8)
        for q in range(2):
            add_hardiness_gpsimd(q, h_bf[:, q * KP : (q + 1) * KP])
        inner_pair(1, 1, 0, 6)
        hardiness_quarter(0, 2, 2)
        hardiness_to_sbuf(2)
        inner_pair(1, 1, 1, 7)
        hardiness_quarter(1, 2, 3)
        outer_pair(0, 1, 0)
        for q in range(2):
            add_hardiness(1, q, h_bf[:, (2 + q) * KP : (3 + q) * KP])
        for g in range(PASSES):
            hardiness_quarter(g, 3, g)
        outer_pair(0, 1, 1)
        outer_pair(1, 1, 0)
        quantise(h_bf[:], h_w[:], h_s[:])

        two, one = bank(4, [P, 2, HALF]), bank(5, [P, HALF])
        ys_half = [(two[:, 0, :], True, False), (two[:, 1, :], False, True), (one[:], True, True)]
        for g in range(PASSES):
            damage(ys_half, h_w[:, halves[g]], h_s[:, halves[g]], g)
        y_half = held("y_half", [P, N_TILES, HALF], F32)
        add_bias_and_store(ys_half, y_half, halves[0])

        h0_bf, h1_bf = held("h0_bf", [P, 2 * KP], BF16, on="h_bf"), held("h1_bf", [P, 2 * KP], BF16, on="h_bf", skip=2 * KB)
        late_w, late_s = held("late_w", [P, 4 * P], U32), held("late_s", [P, 4 * P], U8)
        add_hardiness_gpsimd(2, h0_bf[:, 0:KP])
        outer_pair(1, 1, 1)
        add_hardiness(0, 3, h0_bf[:, KP : 2 * KP])
        add_hardiness(1, 2, h1_bf[:, 0:KP])
        three = bank(2, [P, N_TILES, P])
        ys_third = [(three[:, n, :], n == 0, n == N_TILES - 1) for n in range(N_TILES)]
        ys = [bank(number, [P, P]) for number in (0, 6, 7)]
        ys_last = [(y[:], True, True) for y in ys]
        quantise(h0_bf[:], late_w[:, 0:HALF], late_s[:, 0:HALF])
        damage(ys_third, late_w[:, 0:P], late_s[:, 0:P], 0)
        damage(ys_last, late_w[:, P:HALF], late_s[:, P:HALF], 0)
        for n, group in enumerate((ys_third, ys_last)):
            cols = slice(HALF + n * P, HALF + (n + 1) * P)
            if n == 1:
                add_hardiness(1, 3, h1_bf[:, KP : 2 * KP])
            quantise(h1_bf[:, n * KP : (n + 1) * KP], late_w[:, cols], late_s[:, cols])
            damage(group, late_w[:, cols], late_s[:, cols], 1)
        y_third = held("y_third", [P, N_TILES, P], F32)
        add_bias_and_store(ys_third, y_third, slice(HALF, HALF + QUARTER))
        y_last = held("y_last", [P, N_TILES, P], F32)
        nc.vector.tensor_scalar_add(out=y_last[:, 0, :], in0=ys[0][:], scalar1=b_sb[:, 0:1])
        nc.scalar.activation(out=y_last[:, 1, :], in_=ys[1][:], func=ACT.Identity, bias=b_sb[:, 1:2])
        nc.vector.tensor_scalar_add(out=y_last[:, 2, :], in0=ys[2][:], scalar1=b_sb[:, 2:3])
        for n, queue in enumerate((nc.sync, nc.scalar, nc.sync)):
            queue.dma_start(out=out[n * P : (n + 1) * P, HALF + QUARTER : S], in_=y_last[:, n, :])
